import numpy as np, ml_dtypes
CORES = [16,18,20,22]
N = 4
BF = ml_dtypes.bfloat16
C, L, S0, K, T, R, Q = 4096, 256, 256, 16, 4, 11, 9
M, S = C // L, S0 + L * T
def perms(rng):
    return np.ascontiguousarray(np.argsort(rng.random((N, 8, S0)), axis=-1))
def parts(rng):
    x = np.floor(rng.random((N, 8, 16, C)) * rng.integers(160, 257, (N, 8, 1, C))).astype(np.int64)
    v = np.floor(rng.random((N, 8, 16, S0)) * rng.integers(96, 257, (N, 8, 1, S0))).astype(np.int64)
    w = rng.integers(0, S0, (N, 8, C)); few = rng.integers(0, S0, (N, 8, 16))
    w = np.where(rng.random((N, 8, C)) < 0.25, np.take_along_axis(few, rng.integers(0, 16, (N, 8, C)), 2), w)
    th = rng.integers(48, 208, (N, 8, 1, T)) + rng.integers(-16, 17, (N, 8, 16, T))
    return x, v, perms(rng), perms(rng), w, th
def pack(x, v, e, h, w, th):
    big = lambda a: np.ascontiguousarray(a.reshape(N, 128, -1)).astype(np.float32).astype(BF)
    return {"x0": big(x), "v0": big(v), "e0": e.astype(np.int32), "h0": h.astype(np.int32), "w0": w.astype(np.int32), "th": big(th)}
def put(p, s, at):
    j = int(np.argmax(p == at)); p[j] = p[s]; p[s] = at
def setup_inputs(rng):
    return pack(*parts(rng))
def setup_inputs_spread(rng):
    x, v, e, h, w, th = parts(rng)
    x = np.floor(np.exp2(8 * rng.random((N, 8, 1, C))) * rng.random((N, 8, 16, C)) * (rng.random((N, 8, 1, C)) > 0.0625)).astype(np.int64)
    v = np.floor(np.exp2(8 * rng.random((N, 8, 1, S0)) * rng.random((N, 8, 1, S0))) * rng.random((N, 8, 16, S0)) * (rng.random((N, 8, 1, S0)) > 0.0625)).astype(np.int64)
    w = np.minimum(np.floor(S0 * rng.random((N, 8, C)) ** 3).astype(np.int64), S0 - 1)
    th = np.floor(np.exp2(8 * rng.random((N, 8, 1, T))) * rng.random((N, 8, 16, T))).astype(np.int64)
    return pack(x, v, e, h, w, th)
def setup_inputs_ends(rng):
    bx = rng.choice(np.array([0.0, 0.1, 0.5, 0.9, 1.0, 1.0]), (N, 8, 1, C)); bv = rng.choice(np.array([0.0, 0.1, 0.5, 0.9, 1.0]), (N, 8, 1, S0))
    bx[:, 7] = rng.choice(np.array([0.0, 0.0, 0.1, 0.1, 1.0]), (N, 1, C)); bx[:, 7, :, ::64] = 0.0
    x = 255 * (rng.random((N, 8, 16, C)) < bx).astype(np.int64); v = 255 * (rng.random((N, 8, 16, S0)) < bv).astype(np.int64)
    w = np.where(rng.random((N, 8, C)) < 0.75, (S0 - 1) * rng.integers(0, 2, (N, 8, C)), rng.integers(0, S0, (N, 8, C)))
    e, h = perms(rng), perms(rng)
    th = 255 * (rng.random((N, 8, 16, T)) < rng.choice(np.array([0.0, 0.25, 0.5, 0.75, 1.0]), (N, 8, 1, T))).astype(np.int64); th[:, 0, :, 0] = 0; th[:, 5, :, T - 1] = 255
    v[..., 0] = 255 * rng.integers(0, 2, (N, 8, 1)); v[..., S0 - 1] = 255 * rng.integers(0, 2, (N, 8, 1))
    v[:, 7, :, 0] = 255; v[:, 7, :, S0 - 1] = 255; w[:, 7] = np.where(((np.arange(C) >> 9) & 1) == 1, 0, S0 - 1)
    v[:, 0, :, 1] = 0; v[:, 0, 15, 1] = 132; v[:, 0, 1, 1] = 1
    v[:, 7, :, L - 2] = 255; v[:, 7, 15, L - 2] = 132; v[:, 7, 13, L - 2] = 254; v[:, 7, 0, L - 2] = 254
    for r in range(N):
        for g in range(8):
            opp = g == 7 or (g & 1) == 0
            put(e[r, g], 0, 0); put(e[r, g], S0 - 1, S0 - 1)
            put(h[r, g], 0, S0 - 1 if opp else 0); put(h[r, g], S0 - 1, 0 if opp else S0 - 1)
        if r & 1: x[r, 6] = 255; v[r, 6] = 0; th[r, 6] = 0
    return pack(x, v, e, h, w, th)
def setup_inputs_corners(rng):
    x, v, e, h, w, th = parts(rng); shift = int(rng.integers(0, 8))
    for r in range(N):
        for g in range(8):
            m = (r + g + shift) & 7; two = rng.permutation(L)[:2]; s1, s2 = int(two[0]), int(two[1])
            if m == 0:
                x[r, g] = 0; v[r, g][:, two] = 255; v[r, g][8, two] = 254; w[r, g] = np.where(((np.arange(C) >> 9) & 1) == 1, s1, s2)
                put(e[r, g], s1, 0); put(e[r, g], s2, 1); put(h[r, g], s1, S0 - 1); put(h[r, g], s2, S0 - 2)
            elif m == 1:
                x[r, g] = rng.integers(0, 100, (16, C)); v[r, g][:, s1] = rng.integers(100, 256, 16); w[r, g] = s1
                put(e[r, g], s1, 0); put(h[r, g], s1, S0 - 1)
            elif m == 2: x[r, g] = 255; v[r, g] = 0; th[r, g] = 0
            elif m == 3: x[r, g] = 255; v[r, g] = 0; v[r, g][:, s1] = 255; th[r, g] = 1
            elif m == 4: w[r, g] = rng.choice(np.array([0, S0 - 1, s1, s2]), C)
            elif m == 5: h[r, g] = e[r, g]
            elif m == 6: h[r, g] = S0 - 1 - e[r, g]
            else: th[r, g] = 255; x[r, g] = np.minimum(x[r, g], 254)
    return pack(x, v, e, h, w, th)
def setup_inputs_crowd(rng):
    x, v, e, h, w, th = parts(rng); o = int(rng.integers(0, N)); other = (o + 1 + int(rng.integers(0, N - 1))) & (N - 1); B = 16 * N
    c = rng.integers(96, 256, (N, 8, 16, 1)); c[:, :, 0] = 255
    d = np.zeros((N, 8, L), np.int64) + ((o - np.arange(N)) & (N - 1))[:, None, None]
    for g, i in ((1, int(rng.integers(0, L))), (5, L - 1)): d[other, g, i] = (d[other, g, i] + 1) & (N - 1)
    z = np.floor(rng.random((N, 8, 16, S0)) * (c + 1)).astype(np.int64)
    z0 = 16 * d + rng.integers(0, 16, (N, 8, L)) - np.sum(z[:, :, 1:, :L] * (2 * np.arange(1, 16) + 1)[:, None], axis=2)
    z[:, :, 0, :L] = (z0 & (B - 1)) + B * rng.integers(0, 256 // B, (N, 8, L))
    return pack(np.zeros_like(x) + c, c - z, e, h, w, th)
def setup_inputs_ties(rng):
    e, h, w = perms(rng), perms(rng), rng.integers(0, S0, (N, 8, C)); one = rng.random((N, 8, 1, 1)) < 0.5; one[:, 0] = True; one[:, 7] = False
    st = np.where(one, 1, 32); v = np.where(one, rng.integers(1, 255, (N, 8, 16, S0)), 32 * rng.integers(1, 7, (N, 8, 16, S0)))
    n = rng.choice(np.array([R - 1] * 12 + [R, 0, 16, R - 1]), (N, 8, 1, C)); less = np.argsort(rng.random((N, 8, 16, C)), axis=2) < n
    x = np.take_along_axis(v, w[:, :, None, :], 3) + st * np.where(less, -1, np.where(rng.random((N, 8, 16, C)) < 0.25, 1, 0))
    th = np.where(one, rng.integers(32, 200, (N, 8, 16, T)), 32 * rng.integers(1, 7, (N, 8, 16, T)))
    return pack(x, v, e, h, w, th)
def check_inputs(d):
    bad = []
    for k, lo, hi in (("x0", 0, 255), ("v0", 0, 255), ("e0", 0, S0 - 1), ("h0", 0, S0 - 1), ("w0", 0, S0 - 1), ("th", 0, 255)):
        a = np.asarray(d[k]).astype(np.float64)
        if not np.all((a >= lo) & (a <= hi) & (a == np.floor(a))): bad.append("range of " + k)
    for k in ("e0", "h0"):
        if not np.all(np.sort(np.asarray(d[k]), axis=-1) == np.arange(S0)): bad.append("permutation " + k)
    return bad
def mark(z):
    return np.sum(z.astype(np.int64) * (2 * np.arange(16) + 1)[:, None], axis=2) & 4095
def reference(x0, v0, e0, h0, w0, th):
    take = np.take_along_axis
    X = x0.astype(np.float32).astype(np.int32).reshape(N, 8, 16, C); W = w0.astype(np.int64)
    V = np.zeros((N, 8, 16, S), np.int32); V[..., :S0] = v0.astype(np.float32).astype(np.int32).reshape(N, 8, 16, S0)
    E = np.full((N, 8, S), -1, np.int64); E[..., :S0] = e0; H = np.full((N, 8, S), -1, np.int64); H[..., :S0] = h0
    thr = th.astype(np.float32).astype(np.int32).reshape(N, 8, 16, T)
    lane = np.arange(L); k = np.arange(K); kap = k * k + k + 1; lower = lane[None, :] < lane[:, None]
    y = V[..., :L] + 0; cur = np.zeros((N, 8, L), np.int64) + lane; A = np.zeros((N, 8), np.int64)
    for t in range(T):
        u = mark(y)
        a = (((u * u) >> 5)[..., None] + kap * u[..., None] + A[:, :, None, None]) & (C - 1)
        a = a.reshape(N, 8, L * K); s = take(W, a, 2)
        xa = take(X, a[:, :, None, :], 3).reshape(N, 8, 16, L, K); vs = take(V, s[:, :, None, :], 3).reshape(N, 8, 16, L, K)
        es = take(E, s, 2).reshape(N, 8, L, K); hs = take(H, s, 2).reshape(N, 8, L, K)
        par = (es < take(E, cur, 2)[..., None]) != (hs < take(H, cur, 2)[..., None])
        hit = par & (np.sum(vs > xa, axis=2) >= R)
        race = np.any(hit, axis=3); f = np.argmax(hit, axis=3)
        ff = f[:, :, None, :, None]; vf = take(vs, ff, 4)[..., 0]; xf = take(xa, ff, 4)[..., 0]
        yn = np.where(race[:, :, None, :], np.abs(vf - xf), np.abs(np.max(xa, axis=4) - y))
        new = np.where(race, take(s.reshape(N, 8, L, K), f[..., None], 3)[..., 0], cur)
        lead = ~race & ~np.any((cur[..., :, None] == cur[..., None, :]) & ~race[..., None, :] & lower, axis=3)
        will = np.sum(yn >= thr[..., t:t + 1], axis=2) >= Q
        for r in range(N):
            for g in range(8):
                i = np.flatnonzero(lead[r, g] & ~will[r, g]); V[r, g][:, cur[r, g, i]] = yn[r, g][:, i]
                i = np.flatnonzero(lead[r, g] & will[r, g]); c = cur[r, g, i]; n = S0 + L * t + i
                V[r, g][:, n] = yn[r, g][:, i]; new[r, g, i] = n
                fe = np.zeros(S, np.int64); fe[E[r, g, c]] = 1; fh = np.zeros(S, np.int64); fh[H[r, g, c]] = 1
                old = np.flatnonzero(E[r, g] >= 0); pe = E[r, g, old]; ph = H[r, g, old]
                E[r, g, old] = pe + (np.add.accumulate(fe) - fe)[pe]; H[r, g, old] = ph + np.add.accumulate(fh)[ph]
                E[r, g, n] = E[r, g, c] + 1; H[r, g, n] = H[r, g, c] - 1
        q = (np.arange(N)[:, None, None] + ((mark(yn) >> 4) & (N - 1))) & (N - 1)
        ya = np.ascontiguousarray(yn[q, np.arange(8)[None, :, None], :, lane[None, None, :]].transpose(0, 1, 3, 2))
        b = M * lane + (mark(ya) & (M - 1))
        np.put_along_axis(X, b[:, :, None, :], ya, 3); np.put_along_axis(W, b, new, 2)
        A = np.sum(race, axis=2); y, cur = yn, new
    return {"yx": X.reshape(N, 128, C).astype(np.float32).astype(BF), "yv": V.reshape(N, 128, S).astype(np.float32).astype(BF), "yw": W.astype(np.float32), "ye": E.astype(np.float32), "yh": H.astype(np.float32)}

@@ -1,0 +1,584 @@
+import numpy as np
+from concourse.bass import DstId, RemoteDMATransfer
+from concourse.mybir import dt, AluOpType, AxisListType, ActivationFunctionType
+import comms_topo
+
+NL, NK, NCELL, NR, NS = 256, 16, 4096, 4, 1280
+NCH = 4
+CL = NL // NCH
+CJ = CL * NK
+DEAD = 4112
+TRASH = 4113
+VW = 4384
+MAGIC = 12582912.0
+CYC, PEC, GAT, SCA, WAKE, LAT = 0.001, 0.00085, 1.4, 3.0, 0.12, 2.8
+SHORT = 3.0
+VR = (0,)
+
+BFT, F32, I32, U16 = "bfloat16", "float32", "int32", "uint16"
+SCRATCH, PLACE, SEMAPHORES = {}, {}, ["qv", "qs", "qt", "qg"]
+for _n, _w, _d in (
+        ("X", NCELL, BFT), ("RT", NCELL, BFT), ("V", VW, BFT), ("RS", 2 * NCELL, BFT), ("XG", NCELL, BFT),
+        ("DS", 2 * NCELL, BFT), ("CM", NCELL, BFT), ("DM", NCELL, BFT), ("LOC", 4128, BFT),
+        ("Y0", NL, BFT), ("TH", 4, BFT), ("EHI", NL, I32), ("U", NL, I32), ("UT", NL, I32), ("WL", NL, U16),
+        ("SR", NL, BFT), ("KB", 2048, BFT), ("KX", 2048, BFT), ("KW", 2048, BFT),
+        ("LG", NS, F32), ("GE", NS, F32), ("GH", NS, F32), ("GV", NS, BFT), ("GW", NL, F32)):
+    SCRATCH[_n] = ("sbuf", [128, _w], _d)
+    PLACE[_n] = (_n, 0, _w, _d)
+_at = {BFT: 0, F32: 0, I32: 0, U16: 0}
+for _d, _w, _ns in (
+        (BFT, NL, "RN0 RN1 ZZ ZF HIT WC LD LDS S1 S2 MM DG DJ NM NMX NMB CKR ZERO LI LI0"),
+        (BFT, 128, "DMT BLE BGE B BGQ LTI WMK WM16 WEB WHB WFB WDG WBG ID IDK IDM IDN IDE IDH"),
+        (BFT, 128, "M8 M8B N8B CA CB CD2 CE2 WCA WCB ZA ZB YA YB PMA PMB"), (BFT, 32, "ML"),
+        (F32, NL, "Y2 SQ X1 X2 JLS MLS MZS WIS CUS HSC COLI RI THL THD T0 T1 PEI SZS SZH PHI PHS NEG LF LM HSQ CRA CRB"),
+        (F32, 288, "SZ RE RH"), (F32, 96, "EL"), (F32, 64, "CC CX O2A SPA EA EB"),
+        (F32, 32, "BSF ILF TRF JL2 CUM W1 O1 O3 LDL M1 M2 F1 F2 CT CD"),
+        (I32, NL, "A1 A2"), (I32, 96, "ELI KI"), (I32, 32, "PI I1 I2 I3 I4"),
+        (U16, NL, "LA LB E16"), (U16, 96, "ELU KLU"), (U16, 32, "JLU JL2U VO ZL XL E1L H0L")):
+    for _n in _ns.split():
+        PLACE[_n] = ("all_" + _d, _at[_d], {32: 16, 96: 80, 288: 264}.get(_w, _w), _d)
+        _at[_d] += _w
+for _d in _at:
+    SCRATCH["all_" + _d] = ("sbuf", [128, _at[_d]], _d)
+SCRATCH["EQ"] = ("sbuf", [128, 16, 256], BFT)
+PLACE["EQ"] = ("EQ", 0, 4096, BFT)
+for _t in range(NR):
+    SCRATCH["LAND%d" % _t] = ("sbuf", [128, 4 * NL], BFT)
+    PLACE["LAND%d" % _t] = ("LAND%d" % _t, 0, 4 * NL, BFT)
+    SEMAPHORES += ["ar%d" % _t, "lo%d" % _t]
+for _b in range(8):
+    SCRATCH["P%d" % _b] = ("psum", [128, 512], F32)
+    PLACE["P%d" % _b] = ("P%d" % _b, 0, 512, F32)
+SEMAPHORES += ["dth", "dv", "de", "dwy", "dws", "dx", "oyx", "oyv", "oyw", "oye", "oyh"]
+
+ADD, SUB, MUL, MAX, MIN = AluOpType.add, AluOpType.subtract, AluOpType.mult, AluOpType.max, AluOpType.min
+GE, GT, LE, LT, EQL = AluOpType.is_ge, AluOpType.is_gt, AluOpType.is_le, AluOpType.is_lt, AluOpType.is_equal
+SHR, AND = AluOpType.logical_shift_right, AluOpType.bitwise_and
+COPY, IDENT = ActivationFunctionType.Copy, ActivationFunctionType.Identity
+ABS, SQUARE = ActivationFunctionType.Abs, ActivationFunctionType.Square
+
+
+def rank_program(g, core, T, topo):
+    rank = T.rank_of(core)
+    if rank is None:
+        return
+    N = len(T.cores)
+    Q = {"v": g.vector, "s": g.scalar, "t": g.tensor, "g": g, "y": g.sync}
+    nodes, hist, bank = [], {}, {}
+
+    def view(n, lo=0, hi=None, step=1, ind=None, ap=None):
+        phys, off, w, d = PLACE[n]
+        if hi is None:
+            hi = w
+        if ap is None:
+            ap = T[phys][:, off + lo:off + hi:step] if step > 1 else T[phys][:, off + lo:off + hi]
+            if ind is not None:
+                p2, o2 = PLACE[ind[0]][:2]
+                ap = ap.indirect(T[p2][:, o2 + ind[1]:o2 + ind[2]])
+        n_el = 16 * (ind[2] - ind[1]) if ind is not None else -((lo - hi) // step)
+        return {"n": n, "lo": lo, "hi": hi, "ap": ap, "ind": ind, "el": n_el, "b2": d in (BFT, U16), "ps": n[0] == "P" and n[1:].isdigit()}
+
+    def node(q, calls, rd, wr, cost, sem=None, lat=0.0, wait=None):
+        i = len(nodes)
+        real, order = set(), set()
+        for v, w in [(v, False) for v in rd] + [(v, True) for v in wr]:
+            spans = [(v["n"], v["lo"], v["hi"], w)]
+            if v["ind"] is not None:
+                spans.append((v["ind"][0], v["ind"][1], v["ind"][2], False))
+            for (n, lo, hi, ww) in spans:
+                if n[0] == "P" and n[1:].isdigit():
+                    b = bank.setdefault(n, [None, None, None])
+                    if b[0] == q:
+                        if b[1] != i:
+                            order.add(b[1])
+                        if b[2] is not None:
+                            real.add(b[2])
+                        b[1] = i
+                    else:
+                        if b[1] is not None:
+                            real.add(b[1])
+                        b[0], b[1], b[2] = q, i, b[1]
+                    continue
+                h = hist.setdefault(n, [])
+                real.update(e[3] for e in h if (ww or e[2]) and e[0] < hi and lo < e[1] and e[3] != i)
+                if ww:
+                    h = [e for e in h if not (lo <= e[0] and e[1] <= hi)]
+                h.append((lo, hi, ww, i))
+                hist[n] = h
+        nodes.append({"q": q, "calls": calls, "real": real, "order": order - real, "cost": cost, "sem": sem, "lat": lat, "wait": wait})
+        return i
+
+    def flush():
+        n = len(nodes)
+        succ = [[] for _ in range(n)]
+        for i, x in enumerate(nodes):
+            for p in x["real"] | x["order"]:
+                succ[p].append(i)
+        prio = [0.0] * n
+        for i in range(n - 1, -1, -1):
+            prio[i] = nodes[i]["cost"] + nodes[i]["lat"] + max([prio[j] + WAKE for j in succ[i]] + [0.0])
+        left = [len(x["real"] | x["order"]) for x in nodes]
+        ready = {q: [] for q in Q}
+        rt = [0.0] * n
+        free = {q: 0.0 for q in Q}
+        for i in range(n):
+            if left[i] == 0:
+                ready[nodes[i]["q"]].append(i)
+        seq, end = [], [0.0] * n
+        while len(seq) < n:
+            best = None
+            for q in Q:
+                if not ready[q]:
+                    continue
+                e = min(max(free[q], rt[i]) for i in ready[q])
+                i = max((i for i in ready[q] if max(free[q], rt[i]) <= e + 0.02),
+                        key=lambda i: (prio[i] + (SHORT if nodes[i]["cost"] < 1 else 0), -i))
+                k = (max(free[q], rt[i]), -prio[i])
+                if best is None or k < best[0]:
+                    best = (k, q, i)
+            q, i = best[1], best[2]
+            ready[q].remove(i)
+            seq.append(i)
+            free[q] = best[0][0] + nodes[i]["cost"]
+            end[i] = free[q] + nodes[i]["lat"]
+            for j in succ[i]:
+                w = 0.05 if nodes[j]["q"] == q and not nodes[i]["lat"] else WAKE
+                if i in nodes[j]["order"]:
+                    w = 0.0
+                rt[j] = max(rt[j], end[i] + w)
+                left[j] -= 1
+                if left[j] == 0:
+                    ready[nodes[j]["q"]].append(j)
+        total, clocks, known, at = {}, {}, {q: {} for q in Q}, {}
+
+        def learn(q, key, cnt):
+            k = known[q]
+            if k.get(key, 0) < cnt:
+                Q[q].wait_ge(T.sem[key], cnt)
+                k[key] = cnt
+                for kk, nn in clocks[(key, cnt)].items():
+                    if k.get(kk, 0) < nn:
+                        k[kk] = nn
+        for i in seq:
+            x = nodes[i]
+            q = x["q"]
+            need = {}
+            for p in x["real"]:
+                if at[p] is not None:
+                    need[at[p][0]] = max(need.get(at[p][0], 0), at[p][1])
+            for key in sorted(need, key=lambda key: -need[key]):
+                learn(q, key, need[key])
+            if x["wait"] is not None:
+                Q[q].wait_ge(T.sem[x["wait"][0]], x["wait"][1])
+            key = x["sem"] or "q" + q
+            if key == "none":
+                x["calls"][0]()
+                at[i] = None
+                continue
+            for k, call in enumerate(x["calls"]):
+                ins = call()
+                if key[0] != "q":
+                    ins.then_inc(T.sem[key], 16)
+                    total[key] = total.get(key, 0) + 16
+                elif k == len(x["calls"]) - 1:
+                    ins.then_inc(T.sem[key], 1)
+                    total[key] = total.get(key, 0) + 1
+            at[i] = (key, total[key])
+            c = dict(known[q])
+            c[key] = total[key]
+            clocks[at[i]] = c
+        for key in sorted(total):
+            learn("g", key, total[key])
+
+    def sc(x):
+        return x["ap"] if isinstance(x, dict) else x
+
+    def scr(*xs):
+        return [x for x in xs if isinstance(x, dict)]
+
+    def cy(n):
+        return 0.02 + CYC * max(64, n)
+
+    def half(*vs):
+        return cy(vs[0]["el"] * (0.5 if all(v["b2"] for v in vs) else 1))
+
+    def ts(out, i0, s1, op0, s2=None, op1=None):
+        if op1 is None:
+            node("v", [lambda: g.vector.tensor_scalar(out["ap"], i0["ap"], sc(s1), None, op0)], [i0] + scr(s1), [out], half(out, i0))
+        else:
+            node("v", [lambda: g.vector.tensor_scalar(out["ap"], i0["ap"], sc(s1), sc(s2), op0, op1)], [i0] + scr(s1, s2), [out], half(out, i0))
+
+    def tt(out, a, b, op):
+        c = 0.06 + CYC * GAT * out["el"] if a["ind"] else cy(out["el"] * (1 if a["ps"] or b["ps"] else 2))
+        node("v", [lambda: g.vector.tensor_tensor(out["ap"], a["ap"], b["ap"], op)], [a, b], [out], c)
+
+    def tc(out, a):
+        c = 0.06 + CYC * GAT * out["el"] if a["ind"] else 0.06 + CYC * SCA * out["el"] if out["ind"] else half(out, a)
+        node("v", [lambda: g.vector.tensor_copy(out["ap"], a["ap"])], [a], [out], c)
+
+    def ms(out, c):
+        node("v", [lambda: g.vector.memset(out["ap"], c)], [], [out], half(out))
+
+    def scan(out, a, b, init, op0, op1):
+        node("v", [lambda: g.vector.tensor_tensor_scan(out["ap"], a["ap"], b["ap"], init, op0, op1)], [a, b], [out], half(out, a, b))
+
+    def act(out, a, func=COPY, bias=None, scale=None, wait=None):
+        kw = {}
+        if bias is not None:
+            kw["bias"] = sc(bias)
+        if scale is not None:
+            kw["scale"] = sc(scale)
+        c = 0.08 + CYC * GAT * out["el"] if a["ind"] else cy(a["el"])
+        node("s", [lambda: g.scalar.activation(out["ap"], a["ap"], func, **kw)], [a] + scr(bias, scale), [out], c, wait=wait)
+
+    def mms(out, pairs, start=True, stop=True):
+        n = len(pairs)
+
+        def one(k, l, r):
+            return lambda: g.tensor.matmul(out["ap"], l["ap"], r["ap"], start and k == 0, stop and k == n - 1)
+        node("t", [one(k, l, r) for k, (l, r) in enumerate(pairs)], [x for p in pairs for x in p], [out], n * (0.01 + PEC * max(64, out["el"])))
+
+    def mm(out, l, r, start=True, stop=True):
+        mms(out, [(l, r)], start, stop)
+
+    def gio(out, pat, base, cm=0):
+        kw = {} if PLACE[out["n"]][3] == I32 else {"allow_small_or_imprecise_dtypes": True}
+        node("g", [lambda: g.iota(out["ap"], pat, base, cm, **kw)], [], [out], 0.15 + 2 * CYC * out["el"])
+
+    def dma(q, pairs, sem, rd, wr, us=2.0):
+        node(q, [(lambda o=o, i=i: Q[q].dma_start(o, i)) for o, i in pairs], rd, wr, 0.06 * len(pairs), sem, us)
+
+    def kset(n, k):
+        return view(n, 128 * k, 128 * k + 128)
+
+    def every16(n):
+        return view(n, 15, NL, 16)
+
+    def lanes(pn, w, src, mask, out):
+        mm(view(pn, 0, NL), view("ID"), view(mask), True, False)
+        mm(view(pn, 0, NL), view(w), src, False, True)
+        scan(view(out), view("DJ"), view(pn, 0, NL), 0.0, MUL, MAX)
+
+    ms(view("EHI"), 0)
+    gio(view("PI", 0, 1), [[1, 1]], 0, 1)
+    gio(view("COLI"), [[1, NL]], 0)
+    gio(view("RI"), [[0, 16], [1, 16]], 0)
+    wl = [[(T.U[:, 32 * ip + 16 * ga:32 * ip + 16 * ga + 16], T.w0[ga::2, 512 * ip:512 * ip + 512]) for ip in range(8)] for ga in range(2)]
+    dma("s", [(T.Y0[:, :], T.v0[:, :])], "dv", [], [view("Y0")])
+    dma("y", wl[0], "dwy", [], [view("U", 0, 8)], 3.0)
+    dma("s", wl[1], "dws", [], [view("U", 8, NL)], 3.0)
+    dma("y", [(T.EHI[0::16, :], T.e0[:, :]), (T.EHI[1::16, :], T.h0[:, :])], "de", [], [view("EHI")])
+    dma("y", [(T.X[:, :], T.x0[:, :])], "dx", [view("U"), view("Y0")], [view("X")], 6.0)
+    dma("y", [(T.TH[:, :], T.th[:, :])], "dth", [], [view("TH")], 6.0)
+    gio(view("V", 0, DEAD), [[0, DEAD]], -1)
+    gio(view("V", DEAD, VW), [[0, VW - DEAD]], 0)
+    gio(view("DM"), [[0, 256], [16384, 16]], 0)
+    gio(view("RS", NCELL, 2 * NCELL), [[0, NCELL]], 0)
+    gio(view("ZERO"), [[0, NL]], 0)
+    gio(view("CT", 0, 4), [[1, 4]], 1)
+    for t in range(NR):
+        gio(view("CD", t, t + 1), [[0, 1]], 2 ** (3 - t))
+    gio(view("SZ"), [[0, 264]], 0)
+    gio(view("RE"), [[0, 264]], -1)
+    gio(view("RH"), [[0, 264]], -1)
+    gio(view("NEG"), [[0, NL]], -5)
+    gio(view("LOC", 0, 16), [[0, 16]], 0)
+    gio(view("LOC", DEAD, DEAD + 16), [[0, 16]], 0)
+
+    def cc(j):
+        return view("CC", j, j + 1)
+
+    def cx(j):
+        return view("CX", j, j + 1)
+    PQ, NP16, PF, WM, WE_, WH_, WF, KAP, KEEP, WWC, Q16, R3, R0, R2, R4, LO, NLO, BLO, QM8, QP8, L32, H32 = range(22)
+    A = [view("CC", 40 + t, 41 + t) for t in range(NR)]
+    ts(view("PI", 2, 3), view("PI", 0, 1), 15, AND)
+    ts(view("PI", 4, 5), view("PI", 0, 1), 4, SHR)
+    tc(cc(PQ), view("PI", 2, 3))
+    ts(cc(NP16), view("PI", 4, 5), -16.0, MUL)
+    tc(cc(PF), view("PI", 0, 1))
+    ts(view("DMT"), view("COLI", 0, 128), cc(NP16), ADD)
+    ts(view("BLE"), view("DMT"), 15.0, LE)
+    ts(view("BGE"), view("DMT"), 0.0, GE)
+    ts(cc(WM), cc(PQ), 2.0, MUL, 1.0, ADD)
+    tt(view("B"), view("BLE"), view("BGE"), MUL)
+    ts(view("WMK"), view("B"), cc(WM), MUL)
+    ts(cx(0), cc(PQ), 0.0, EQL, -2048.0, MUL)
+    ts(cx(1), cc(PQ), 1.0, EQL, 0.5, MUL)
+    tt(cx(2), cx(0), cx(1), ADD)
+    ts(view("CKR"), view("RI"), 0.0, MUL, cx(2), ADD)
+    ts(view("ID"), view("COLI", 0, 128), cc(PF), EQL)
+    ts(view("IDM"), view("ID"), -4096.0, MUL)
+    ts(cx(3), cc(PQ), cc(PQ), MUL, 1.0, ADD)
+    tt(cc(KAP), cx(3), cc(PQ), ADD)
+    ms(A[0], 0.0)
+    for k in range(16):
+        ts(kset("KB", k), view("DMT"), float(k), EQL)
+    for r, j in ((0, R0), (2, R2), (3, R3), (4, R4)):
+        ts(cc(j), cc(PQ), float(r), EQL)
+    ts(view("LI"), view("COLI"), cc(R3), MUL)
+    ts(view("LI0"), view("LI"), cc(R0), ADD)
+    ts(cx(4), cc(R0), 16.0, MUL)
+    tt(cc(WE_), cx(4), cc(R2), ADD)
+    ts(cx(6), cc(PQ), 1.0, EQL, 16.0, MUL)
+    tt(cc(WH_), cx(6), cc(R2), SUB)
+    ts(view("IDE"), view("ID"), cc(WE_), MUL)
+    ts(view("IDH"), view("ID"), cc(WH_), MUL)
+    for j in range(4):
+        j2 = (j + 2) % 4
+        pj = view("P%d" % (2 + j), 0, 512)
+        mms(pj, [(view("IDE"), view("KB", 512 * j, 512 * j + 512)), (view("IDH"), view("KB", 512 * j2, 512 * j2 + 512))])
+        act(view("KX", 512 * j, 512 * j + 512), pj)
+    ts(cc(LO), cc(PQ), 8.0, LT)
+    ts(cc(NLO), cc(LO), -8192.0, MUL)
+    ts(cc(BLO), cc(LO), 8193.0, MUL, -1.0, ADD)
+    ts(view("M8"), view("RI", 0, 128), 8.0, LT)
+    tt(view("M8B"), view("B"), view("M8"), MUL)
+    tt(view("N8B"), view("B"), view("M8B"), SUB)
+    ts(view("CA"), view("M8B"), cc(WE_), MUL)
+    ts(view("CB"), view("N8B"), cc(WH_), MUL)
+    tt(view("WCA"), view("CA"), view("CB"), ADD)
+    ts(view("CD2"), view("M8B"), cc(WH_), MUL)
+    ts(view("CE2"), view("N8B"), cc(WE_), MUL)
+    tt(view("WCB"), view("CD2"), view("CE2"), ADD)
+    ts(cx(10), cc(LO), 999.0, MUL, -8.0, ADD)
+    tt(cc(QM8), cc(PQ), cx(10), ADD)
+    ts(cx(11), cc(LO), -999.0, MUL, 1007.0, ADD)
+    tt(cc(QP8), cc(PQ), cx(11), ADD)
+    ts(cc(L32), cc(LO), 32.0, MUL)
+    ts(cc(H32), cc(LO), -32.0, MUL, 32.0, ADD)
+    ts(view("ZA"), view("DMT"), cc(QM8), EQL, 32.0, MUL)
+    ts(view("ZB"), view("DMT"), cc(QP8), EQL, 32.0, MUL)
+    ts(view("YA"), view("ID"), cc(L32), MUL)
+    ts(view("YB"), view("ID"), cc(H32), MUL)
+    tt(view("PMA"), view("YA"), view("ZA"), ADD)
+    tt(view("PMB"), view("YB"), view("ZB"), ADD)
+    ts(view("WEB"), view("B"), cc(WE_), MUL)
+    ts(view("WHB"), view("B"), cc(WH_), MUL)
+    ts(view("DG"), view("RI"), cc(PQ), EQL)
+    ts(view("T0"), view("DG"), 8192.0, MUL)
+    ts(view("NM"), view("T0"), -8192.0, ADD)
+    ts(view("NMX"), view("NM"), 256.0, MUL)
+    ms(view("DJ"), 1.0)
+    ms(view("DJ", 0, NL, 16), 0.0)
+    ts(view("IDN"), view("ID"), -1.0, MUL)
+    ts(view("BGQ"), view("DMT"), cc(PQ), GE)
+    tt(view("LTI"), view("BLE"), view("BGQ"), MUL)
+    ts(cx(7), cc(PQ), 15.0, EQL, 4095.0, MUL)
+    ts(cc(WF), cx(7), 1.0, ADD)
+    ts(view("WFB"), view("B"), cc(WF), MUL)
+    ts(view("T1"), view("COLI"), 16.0, MUL, 8192.0, ADD)
+    tt(view("HSC"), view("T1"), view("DG"), MUL)
+    ts(view("NMB"), view("HSC"), -8192.0, ADD)
+    ts(view("WM16"), view("WMK"), 16.0, MUL)
+    ts(cc(Q16), cc(PQ), 16.0, MUL)
+    ts(view("BSF"), view("COLI", 0, 16), 256.0, MUL, cc(Q16), ADD)
+    ts(view("ILF"), view("COLI", 0, 16), 16.0, MUL, cc(PQ), ADD)
+    ts(view("TRF"), view("ILF"), float(TRASH), ADD)
+    ts(cc(KEEP), cc(PQ), 2.0, LE)
+    ts(view("IDK"), view("ID"), cc(KEEP), MUL)
+    ts(view("CT", 4, 8), view("CT", 0, 4), cc(R4), MUL)
+    ts(view("CD", 4, 8), view("CD", 0, 4), cc(R2), MUL)
+    tt(view("CT", 8, 12), view("CT", 4, 8), view("CD", 4, 8), ADD)
+    ts(view("CX", 20, 36), view("COLI", 0, 16), cc(PQ), ADD, 15.0, LT)
+    ts(view("CX", 36, 52), view("CX", 20, 36), 1.0, ADD)
+    scan(view("PEI", 0, 16), view("CX", 36, 52), view("CX", 36, 52), 1.0, MUL, MAX)
+    ts(view("WDG"), view("B"), view("PEI", 15, 16), MUL)
+    ts(view("WBG"), view("B"), 65536.0, MUL)
+    ts(view("SZS"), view("DJ"), 0.5, MUL)
+    ts(view("SZH"), view("DJ"), 0.0, EQL, 65536.0, MUL)
+    scan(view("THL"), view("SZS"), view("SZH"), 0.0, MUL, MAX)
+    tt(view("THD"), view("THL"), view("DG"), MUL)
+    ts(cx(9), cc(R4), 256.0, MUL)
+    tt(cc(WWC), cx(9), cc(R3), ADD)
+    act(view("KW"), view("KB"), COPY, scale=cc(WWC))
+    tt(view("SR"), view("EHI"), view("LI0"), ADD)
+
+    def cells(y, more, a):
+        mms(view("P0", 0, NL), [(view("B"), view("CKR")), (view("WMK"), y)])
+        mm(view("P1", 0, NL), view("WMK"), y, True, False)
+        act(view("Y2"), view("P0", 0, NL), IDENT, bias=MAGIC, scale=1.0 / 4096)
+        act(view("MM"), view("Y2"), IDENT, bias=-MAGIC)
+        mm(view("P1", 0, NL), view("IDM"), view("MM"), False, True)
+        act(view("SQ"), view("P1", 0, NL), SQUARE)
+        act(view("X1"), view("SQ"), IDENT, bias=-0.4375, scale=1.0 / 32)
+        act(view("X2"), view("X1"), IDENT, bias=MAGIC + more)
+        act(view("P0", 0, NL), view("P1", 0, NL), IDENT, bias=a, scale=cc(KAP))
+        tt(view("A1"), view("X2"), view("P0", 0, NL), ADD)
+        ts(view("A2"), view("A1"), 4095, AND)
+        tc(view("LA"), view("A2"))
+
+    def current(rec):
+        mm(view("P6", 0, NL), view("WEB"), view(rec))
+        tc(view("E16"), view("P6", 0, NL))
+        lanes("P5", "WEB", view(rec), "NM", "CUS")
+        for n, w, o in (("CRA", "WCA", 0), ("CRB", "WCB", NL)):
+            mm(view("P7", o, o + NL), view(w), view(rec))
+            act(view(n), view("P7", o, o + NL))
+
+    cells(view("Y0"), 0.0, A[0])
+    node("v", [lambda: g.vector.transpose(T.UT[:, :], T.U[:, :])], [view("U")], [view("UT")], cy(NL))
+    tc(view("WL"), view("UT"))
+    for c in range(4):
+        (tc if c % 2 else act)(view("RT", 1024 * c, 1024 * c + 1024), view("SR", 0, NL, 1, ("WL", 64 * c, 64 * c + 64)))
+    current("SR")
+    tc(view("EL", 0, 16), every16("CUS"))
+    tc(view("VO"), every16("CUS"))
+    tc(view("V", 0, VW, 1, ("VO", 0, 16)), view("Y0"))
+    ts(view("E1L"), view("EL", 0, 16), 0.0625, MUL)
+    lanes("P7", "WHB", view("SR"), "NM", "PHS")
+    ts(view("H0L"), every16("PHS"), 0.0625, MUL)
+
+    rec = "SR"
+    y = view("Y0")
+    for t in range(NR):
+        newrec = "RN%d" % (t % 2)
+        land = "LAND%d" % t
+        O2 = view("O2A", 16 * t, 16 * t + 16)
+        SP = view("SPA", 16 * t, 16 * t + 16)
+        more = t + 1 < NR
+
+        def ch(n, c):
+            return view(n, CL * c, CL * c + CL)
+
+        def cj(n, c, off=0):
+            return view(n, off + CJ * c, off + CJ * c + CJ)
+
+        def cand(n, c, k, off=0):
+            return view(n, off + CJ * c + k, off + CJ * c + CJ, 16)
+
+        for c in range(NCH):
+            (tc if c in VR else act)(cj("RS", c), view("RT", 0, NCELL, 1, ("LA", CL * c, CL * c + CL)))
+            act(cj("XG", c), view("X", 0, NCELL, 1, ("LA", CL * c, CL * c + CL)))
+            pa, pb = view("P%d" % (c % 2), 0, CL), view("P%d" % (2 + c % 2), 0, CL)
+            pc, pn = view("P%d" % (7 if c % 2 else 4), 0, CL), view("P5", 0, CL)
+            mms(pa, [(kset("KX", k), cand("RS", c, k)) for k in range(8)])
+            mms(pb, [(kset("KX", k), cand("RS", c, k)) for k in range(8, 16)])
+            act(ch("LF", c), pa, IDENT, bias=cc(BLO), scale=cc(LO))
+            tt(ch("LM", c), ch("LF", c), pb, MAX)
+            ts(ch("LB", c), ch("LM", c), cc(NLO), ADD)
+            tt(ch("S1", c), pa, ch("CRA", c), LT)
+            tt(ch("S2", c), pb, ch("CRB", c), LT)
+            tt(cj("DS", c), view("V", 0, VW, 1, ("LB", CL * c, CL * c + CL)), cj("XG", c), SUB)
+            ts(cj("CM", c), cj("DS", c), 0.0, GT)
+            scan(cj("DS", c, NCELL), cj("DM", c), cj("XG", c), 0.0, MIN, MAX)
+            mms(pc, [(view("PMA"), ch("S1", c)), (view("PMB"), ch("S2", c))] + [(kset("KB", k), cand("CM", c, k)) for k in range(16)])
+            act(ch("HSQ", c), pc, SQUARE, bias=-45.5)
+            ts(ch("HIT", c), ch("HSQ", c), 9.0, LE)
+            mm(pn, view("LTI"), ch("HIT", c))
+            ts(ch("ZF", c), pn, 0.0, EQL)
+            mms(pn, [(view("ID"), ch("NMB", c)), (view("WFB"), ch("ZF", c))])
+            scan(ch("JLS", c), ch("DJ", c), pn, 0.0, MUL, MAX)
+            mms(view("P6", 0, CL), [(view("IDN"), view(y["n"], CL * c, CL * c + CL)), (view("ID"), cand("DS", c, 15, NCELL))])
+            act(cand("DS", c, 15, NCELL), view("P6", 0, CL))
+        act(view("RS", NCELL + 15, 2 * NCELL, 16), view(rec))
+        mms(view("P6", 0, NL), [(view("IDK"), view(rec)), (view("ID"), view("LI"))])
+        act(view("RS", NCELL + 14, 2 * NCELL, 16), view("P6", 0, NL), IDENT, bias=view("CT", 8 + t, 9 + t))
+        tc(view("JLU"), every16("JLS"))
+        ynew = view(land, 0, NL)
+        act(ynew, view("DS", 0, 2 * NCELL, 1, ("JLU", 0, 16)), ABS)
+
+        dsts, ids = [], []
+        for j in range(1, N):
+            r = (rank + j) % N
+            d = (rank - r) % N
+            a = topo.addr(T.cores[r])
+            ids.append(DstId(rid=a[0], pnc=a[1]))
+            dsts.append(T[land][:, d * NL:(d + 1) * NL])
+        msk = topo.mask(core, T.cores[(rank + 1) % N])
+        neng = len(topo.engines(core, T.cores[(rank + 1) % N]))
+
+        def send(ids=ids, dsts=dsts, msk=msk, t=t, src=ynew["ap"]):
+            return g.remote_dma_fused([RemoteDMATransfer(dst_ids=ids, dma_engine_mask=msk, remote_sem=T.sem["ar%d" % t],
+                                                         src=src, dsts=dsts)], local_sem=T.sem["lo%d" % t])
+        node("g", [send], [ynew], [view(land, NL, 4 * NL)], 0.1, "none", LAT)
+
+        ts(view("ML"), every16("JLS"), 4096.0, GE)
+        tt(view("CUM"), every16("CUS"), view("ML"), MUL)
+        mm(view("P2", 0, NL), view("WBG"), view("ZERO"), True, False)
+
+        def eq(c):
+            n = NL - 16 * c
+            p1, o1 = PLACE["E16"][:2]
+            p2, o2 = PLACE["CUM"][:2]
+            node("v", [lambda: g.vector.tensor_scalar(T.EQ[:, c, 0:n], T[p1][:, o1 + 16 * c:o1 + NL], T[p2][:, o2 + c:o2 + c + 1], None, EQL)],
+                 [view("E16", 16 * c, NL), view("CUM", c, c + 1)], [view("EQ", 256 * c, 256 * c + 256, ap=0)], cy(n / 2))
+        for c in range(16):
+            eq(c)
+            if c < 15:
+                mm(view("P2", 16 * c + 16, NL), view("WBG"), view("EQ", 256 * c, 256 * c + 256, ap=T.EQ[:, c, 16:NL - 16 * c]), False, False)
+        mm(view("P2", 0, NL), view("WDG"), view("EQ", 0, NCELL, ap=T.EQ[:, :, 0:16]), False, True)
+        lanes("P4", "WM16", ynew, "NMX", "MLS")
+        tc(view("I1"), every16("MLS"))
+        ts(view("I2"), view("I1"), 768, AND)
+        tt(view("F1"), view("I2"), view("ILF"), ADD)
+        tc(view("ZL"), view("F1"))
+        ts(view("WC"), ynew, view("TH", t, t + 1), GE)
+        lanes("P7", "B", view("WC"), "NM", "WIS")
+        ts(view("W1"), every16("WIS"), 9.0, GE)
+        if more:
+            mm(view("P3", 0, 16), view("B"), view("ML"))
+            an = A[t + 1]
+            node("v", [lambda an=an: g.vector.tensor_reduce(an["ap"], T.P3[:, 0:16], AxisListType.X, ADD, negate=True)],
+                 [view("P3", 0, 16)], [an], cy(16))
+            cells(ynew, 256.0, an)
+        tt(view("LD"), view("THD"), view("P2", 0, NL), GT)
+        scan(view("LDS"), view("DJ"), view("LD"), 0.0, MUL, MAX)
+        tt(view("LDL"), view("ML"), every16("LDS"), MUL)
+        tt(SP, view("LDL"), view("W1"), MUL)
+        tt(view("JL2"), every16("JLS"), SP, SUB)
+        tc(view("JL2U"), view("JL2"))
+        act(view(newrec), view("RS", 0, 2 * NCELL, 1, ("JL2U", 0, 16)))
+
+        act(view("ZZ"), view(land, 0, N * NL, 1, ("ZL", 0, 16)), wait=("ar%d" % t, (N - 1) * neng))
+        lanes("P4", "WM16", view("ZZ"), "NMX", "MZS")
+        tc(view("I3"), every16("MZS"))
+        ts(view("I4"), view("I3"), 4, SHR, 15, AND)
+        tt(view("F2"), view("I4"), view("BSF"), ADD)
+        tc(view("XL"), view("F2"))
+        tc(view("X", 0, NCELL, 1, ("XL", 0, 16)), view("ZZ"))
+        tc(view("RT", 0, NCELL, 1, ("XL", 0, 16)), view(newrec))
+        ts(view("O1"), view("W1"), float(2 ** (3 - t)), MUL)
+        tt(O2, view("O1"), every16("CUS"), ADD)
+        tt(view("O3"), O2, view("TRF"), SUB)
+        tt(view("M1"), view("LDL"), view("O3"), MUL)
+        tt(view("M2"), view("M1"), view("TRF"), ADD)
+        tc(view("VO"), view("M2"))
+        tc(view("V", 0, VW, 1, ("VO", 0, 16)), ynew)
+        if more:
+            current(newrec)
+        rec = newrec
+        y = ynew
+
+    dma("y", [(T.yx[:, :], T.X[:, :])], "oyx", [view("X")], [], 7.0)
+    ts(view("EA"), view("O2A"), float(-DEAD), ADD)
+    tt(view("EB"), view("EA"), view("SPA"), MUL)
+    ts(view("EL", 16, 80), view("EB"), float(DEAD), ADD)
+    tc(view("ELU"), view("EL"))
+    tc(view("ELI"), view("EL"))
+    ts(view("KI"), view("ELI"), 4, SHR)
+    tc(view("KLU"), view("KI"))
+    act(view("GV"), view("V", 0, VW, 1, ("ELU", 0, 80)))
+    dma("y", [(T.yv[:, :], T.GV[:, :])], "oyv", [view("GV")], [])
+    ts(view("CM"), view("V", 16, DEAD), 0.0, GE)
+    scan(view("LOC", 16, DEAD), view("DM"), view("CM"), 0.0, MIN, ADD)
+    act(view("LG"), view("LOC", 0, 4128, 1, ("ELU", 0, 80)))
+    mms(view("P0", 0, NL), [(kset("KW", q), view("RT", 256 * q, 256 * q + 256)) for q in range(16)])
+    act(view("GW"), view("P0", 0, NL))
+    dma("y", [(T.yw[:, :], T.GW[:, :])], "oyw", [view("GW")], [])
+    tc(view("SZ", 1, 257), view("LOC", 31, DEAD, 16))
+    tc(view("SZS"), view("SZ", 0, 264, 1, ("E1L", 0, 16)))
+    tc(view("SZH", 0, NL, 1, ("H0L", 0, 16)), view("SZS"))
+    scan(view("PHI"), view("SZH"), view("NEG"), 0.0, ADD, MAX)
+    tc(view("PHS"), view("PHI", 0, NL, 1, ("H0L", 0, 16)))
+    tc(view("RH", 0, 264, 1, ("E1L", 0, 16)), view("PHS"))
+    scan(view("PEI"), view("SZ", 1, 257), view("NEG"), -1.0, ADD, MAX)
+    tt(view("RE", 1, 257), view("PEI"), view("SZ", 1, 257), SUB)
+    tt(view("GE"), view("RE", 0, 264, 1, ("KLU", 0, 80)), view("LG"), ADD)
+    dma("y", [(T.ye[:, :], T.GE[0::16, :])], "oye", [view("GE")], [])
+    tt(view("GH"), view("RH", 0, 264, 1, ("KLU", 0, 80)), view("LG"), SUB)
+    dma("y", [(T.yh[:, :], T.GH[0::16, :])], "oyh", [view("GH")], [])
+
+    flush()
+    for t in range(NR):
+        g.wait_ge(T.sem["lo%d" % t], neng)

@@ -4,58 +4,68 @@ from concourse.mybir import dt, AluOpType, AxisListType, ActivationFunctionType
 import comms_topo
 
 NL, NK, NCELL, NR, NS = 256, 16, 4096, 4, 1280
-NCH = 4
-CL = NL // NCH
-CJ = CL * NK
-DEAD = 4112
-TRASH = 4113
-VW = 4384
+CHUNKS = (0, 64, 128, 192, 256)
+PARTS = (0, 256)
+LEADS = (0, 192, 256)
+CO = 256
+TRASH = 16
+LAB0 = 272
+DEAD = LAB0 + NCELL
+VW = DEAD + 16
 MAGIC = 12582912.0
-CYC, PEC, GAT, SCA, WAKE, LAT = 0.001, 0.00085, 1.4, 3.0, 0.12, 2.8
-SHORT = 3.0
-VR = (0,)
+CYC, PEC, GAT, SCA, WAKE, LAT = 0.00083, 0.00083, 1.56, 3.8, 0.15, 3.3
+SAME, SPARE, PASSES = 0.1, 1.0, 2
+BC, BL, BV = 2.5, 1.0, 4.0
+GL = 64
+WIN = [2 * CO * i + NK * l for i, l in enumerate(PARTS)]
+MAXC = max(b - a for a, b in zip(CHUNKS, CHUNKS[1:]))
 
 BFT, F32, I32, U16 = "bfloat16", "float32", "int32", "uint16"
 SCRATCH, PLACE, SEMAPHORES = {}, {}, ["qv", "qs", "qt", "qg"]
 for _n, _w, _d in (
-        ("X", NCELL, BFT), ("RT", NCELL, BFT), ("V", VW, BFT), ("RS", 2 * NCELL, BFT), ("XG", NCELL, BFT),
-        ("DS", 2 * NCELL, BFT), ("CM", NCELL, BFT), ("DM", NCELL, BFT), ("LOC", 4128, BFT),
-        ("Y0", NL, BFT), ("TH", 4, BFT), ("EHI", NL, I32), ("U", NL, I32), ("UT", NL, I32), ("WL", NL, U16),
-        ("SR", NL, BFT), ("KB", 2048, BFT), ("KX", 2048, BFT), ("KW", 2048, BFT),
-        ("LG", NS, F32), ("GE", NS, F32), ("GH", NS, F32), ("GV", NS, BFT), ("GW", NL, F32)):
+        ("X", NCELL, BFT), ("RT", NCELL, BFT), ("V", VW, BFT), ("RS0", WIN[-1], BFT), ("RS1", WIN[-1], BFT), ("XG", NCELL, BFT),
+        ("DS", WIN[-1], BFT), ("MX", NCELL, BFT), ("DM", NK * MAXC, BFT), ("LOC", VW, BFT), ("AL", NCELL, BFT),
+        ("Y0", NL, BFT), ("TH", 4, BFT), ("EHI", NL, I32), ("UT", NL, I32), ("WL", NL, U16),
+        ("SR", NL, BFT), ("LG", NS, F32), ("GE", NS, F32), ("GV", NS, BFT), ("GW", NL, F32)):
     SCRATCH[_n] = ("sbuf", [128, _w], _d)
     PLACE[_n] = (_n, 0, _w, _d)
 _at = {BFT: 0, F32: 0, I32: 0, U16: 0}
 for _d, _w, _ns in (
-        (BFT, NL, "RN0 RN1 ZZ ZF HIT WC LD LDS S1 S2 MM DG DJ NM NMX NMB CKR ZERO LI LI0"),
-        (BFT, 128, "DMT BLE BGE B BGQ LTI WMK WM16 WEB WHB WFB WDG WBG ID IDK IDM IDN IDE IDH"),
-        (BFT, 128, "M8 M8B N8B CA CB CD2 CE2 WCA WCB ZA ZB YA YB PMA PMB"), (BFT, 32, "ML"),
-        (F32, NL, "Y2 SQ X1 X2 JLS MLS MZS WIS CUS HSC COLI RI THL THD T0 T1 PEI SZS SZH PHI PHS NEG LF LM HSQ CRA CRB"),
-        (F32, 288, "SZ RE RH"), (F32, 96, "EL"), (F32, 64, "CC CX O2A SPA EA EB"),
-        (F32, 32, "BSF ILF TRF JL2 CUM W1 O1 O3 LDL M1 M2 F1 F2 CT CD"),
+        (BFT, NL, "ZZ WC S1 S2 MM DJ NM LI LI0 COLI RI TS PMA PMB BB"),
+        (BFT, 144, "DMT KB KW KXA KXB K1 K2"),
+        (BFT, 128, "B WMK WM16 WEB W1B WDG WBG ID IDK IDM IDN GRP H16 R8 M8B N8B PM8 WA WB WZ C1 C2 C3 C4 C5 C6"),
+        (BFT, 32, "ML"),
+        (F32, NL, "SQ X1 MLS MZS LV CUS TAS LF LM SZA SZB SZH PHB REA NEG"),
+        (F32, 288, "RR VAL JS"), (F32, 96, "EL"), (F32, 64, "CC CX O2A SPA EA EB"),
+        (F32, 32, "BSF ILF TRF JL2 CUM O1 M1 M2 F1 F2 CT CD NTH AD ML6 LV0"),
         (I32, NL, "A1 A2"), (I32, 96, "ELI KI"), (I32, 32, "PI I1 I2 I3 I4"),
-        (U16, NL, "LA LB E16"), (U16, 96, "ELU KLU"), (U16, 32, "JLU JL2U VO ZL XL E1L H0L")):
+        (U16, NL, "LA LB E16"), (U16, 96, "ELU KLU"), (U16, 32, "JLU JL2U VO ZL XL E0L TAU")):
     for _n in _ns.split():
-        PLACE[_n] = ("all_" + _d, _at[_d], {32: 16, 96: 80, 288: 264}.get(_w, _w), _d)
+        PLACE[_n] = ("all_" + _d, _at[_d], {32: 16, 96: 80}.get(_w, _w), _d)
         _at[_d] += _w
 for _d in _at:
     SCRATCH["all_" + _d] = ("sbuf", [128, _at[_d]], _d)
 SCRATCH["EQ"] = ("sbuf", [128, 16, 256], BFT)
 PLACE["EQ"] = ("EQ", 0, 4096, BFT)
+SCRATCH["CM"] = ("sbuf", [128, NL, NK + 1], BFT)
+PLACE["CM"] = ("CM", 0, NL * (NK + 1), BFT)
+SCRATCH["U"] = ("sbuf", [128, 2, 8, 16], I32)
+PLACE["U"] = ("U", 0, NL, I32)
 for _t in range(NR):
     SCRATCH["LAND%d" % _t] = ("sbuf", [128, 4 * NL], BFT)
     PLACE["LAND%d" % _t] = ("LAND%d" % _t, 0, 4 * NL, BFT)
-    SEMAPHORES += ["ar%d" % _t, "lo%d" % _t]
+    for _p in range(len(PARTS) - 1):
+        SEMAPHORES += ["ar%d_%d" % (_t, _p), "lo%d_%d" % (_t, _p)]
 for _b in range(8):
     SCRATCH["P%d" % _b] = ("psum", [128, 512], F32)
     PLACE["P%d" % _b] = ("P%d" % _b, 0, 512, F32)
-SEMAPHORES += ["dth", "dv", "de", "dwy", "dws", "dx", "oyx", "oyv", "oyw", "oye", "oyh"]
+SEMAPHORES += ["dth", "dv", "de", "dw", "dx", "oyx", "oyv", "oyw", "oye"]
 
 ADD, SUB, MUL, MAX, MIN = AluOpType.add, AluOpType.subtract, AluOpType.mult, AluOpType.max, AluOpType.min
-GE, GT, LE, LT, EQL = AluOpType.is_ge, AluOpType.is_gt, AluOpType.is_le, AluOpType.is_lt, AluOpType.is_equal
+GE, GT, LE, LT, EQL, NE = AluOpType.is_ge, AluOpType.is_gt, AluOpType.is_le, AluOpType.is_lt, AluOpType.is_equal, AluOpType.not_equal
 SHR, AND = AluOpType.logical_shift_right, AluOpType.bitwise_and
 COPY, IDENT = ActivationFunctionType.Copy, ActivationFunctionType.Identity
-ABS, SQUARE = ActivationFunctionType.Abs, ActivationFunctionType.Square
+ABS, SQUARE, SIGN = ActivationFunctionType.Abs, ActivationFunctionType.Square, ActivationFunctionType.Sign
 
 
 def rank_program(g, core, T, topo):
@@ -64,9 +74,9 @@ def rank_program(g, core, T, topo):
         return
     N = len(T.cores)
     Q = {"v": g.vector, "s": g.scalar, "t": g.tensor, "g": g, "y": g.sync}
-    nodes, hist, bank = [], {}, {}
+    nodes, hist, bank, eng, links = [], {}, {}, [], []
 
-    def view(n, lo=0, hi=None, step=1, ind=None, ap=None):
+    def view(n, lo=0, hi=None, step=1, ind=None, ap=None, el=None):
         phys, off, w, d = PLACE[n]
         if hi is None:
             hi = w
@@ -75,80 +85,95 @@ def rank_program(g, core, T, topo):
             if ind is not None:
                 p2, o2 = PLACE[ind[0]][:2]
                 ap = ap.indirect(T[p2][:, o2 + ind[1]:o2 + ind[2]])
-        n_el = 16 * (ind[2] - ind[1]) if ind is not None else -((lo - hi) // step)
+        n_el = el or (16 * (ind[2] - ind[1]) if ind is not None else -((lo - hi) // step))
         return {"n": n, "lo": lo, "hi": hi, "ap": ap, "ind": ind, "el": n_el, "b2": d in (BFT, U16), "ps": n[0] == "P" and n[1:].isdigit()}
 
-    def node(q, calls, rd, wr, cost, sem=None, lat=0.0, wait=None):
+    def node(q, calls, rd, wr, cost, sem=None, lat=0.0, wait=()):
         i = len(nodes)
-        real, order = set(), set()
+        real, banks = set(), {}
         for v, w in [(v, False) for v in rd] + [(v, True) for v in wr]:
             spans = [(v["n"], v["lo"], v["hi"], w)]
             if v["ind"] is not None:
                 spans.append((v["ind"][0], v["ind"][1], v["ind"][2], False))
             for (n, lo, hi, ww) in spans:
                 if n[0] == "P" and n[1:].isdigit():
-                    b = bank.setdefault(n, [None, None, None])
-                    if b[0] == q:
-                        if b[1] != i:
-                            order.add(b[1])
-                        if b[2] is not None:
-                            real.add(b[2])
-                        b[1] = i
-                    else:
-                        if b[1] is not None:
-                            real.add(b[1])
-                        b[0], b[1], b[2] = q, i, b[1]
+                    if n not in banks:
+                        banks[n] = bank.get(n)
+                        bank[n] = i
                     continue
                 h = hist.setdefault(n, [])
                 real.update(e[3] for e in h if (ww or e[2]) and e[0] < hi and lo < e[1] and e[3] != i)
-                if ww:
+                if ww and v["el"] == hi - lo and v["ind"] is None:
                     h = [e for e in h if not (lo <= e[0] and e[1] <= hi)]
                 h.append((lo, hi, ww, i))
                 hist[n] = h
-        nodes.append({"q": q, "calls": calls, "real": real, "order": order - real, "cost": cost, "sem": sem, "lat": lat, "wait": wait})
+        nodes.append({"alt": {q: (calls, cost)}, "real": real, "banks": banks, "order": set(b for b in banks.values() if b is not None),
+                      "sem": sem, "lat": lat, "wait": wait})
         return i
+
+    def either(on_v, on_s):
+        keep = (dict(bank), {n: list(h) for n, h in hist.items()})
+        on_s()
+        other = nodes.pop()
+        bank.clear()
+        bank.update(keep[0])
+        hist.clear()
+        hist.update(keep[1])
+        on_v()
+        nodes[-1]["alt"].update(other["alt"])
+        nodes[-1]["real"] |= other["real"]
+        nodes[-1]["wait"] = other["wait"]
+        return len(nodes) - 1
+
+    def deal(rank_of, preds, fixed, back):
+        n = len(nodes)
+        start, end, slots, on = [0.0] * n, [0.0] * n, {q: [] for q in Q}, [None] * n
+        for i in sorted(range(n), key=rank_of):
+            x, best = nodes[i], None
+            for q in ([fixed[i]] if fixed else sorted(x["alt"])):
+                c = x["alt"][q][1]
+                t = 0.0
+                for p, soft in preds[i]:
+                    lat = (x if back else nodes[p])["lat"]
+                    t = max(t, end[p] + (0.0 if soft and on[p] == q else lat + (SAME if on[p] == q and not lat else WAKE)))
+                k, sl = 0, slots[q]
+                while k < len(sl) and sl[k][0] < t + c - 1e-9:
+                    t = max(t, sl[k][1])
+                    k += 1
+                if best is None or t + c + (SPARE if q == "v" else 0) < best[0]:
+                    best = (t + c + (SPARE if q == "v" else 0), q, t, k, c)
+            q, t, k, c = best[1:]
+            slots[q].insert(k, (t, t + c))
+            start[i], end[i], on[i] = t, t + c, q
+        return max(end[i] + (0 if back else nodes[i]["lat"]) for i in range(n)), start, end, on
 
     def flush():
         n = len(nodes)
-        succ = [[] for _ in range(n)]
-        for i, x in enumerate(nodes):
-            for p in x["real"] | x["order"]:
-                succ[p].append(i)
+        preds = [[(p, False) for p in x["real"]] + [(p, True) for p in x["order"] - x["real"]] for x in nodes]
+        succs = [[] for _ in range(n)]
+        for i in range(n):
+            for p, soft in preds[i]:
+                succs[p].append((i, soft))
         prio = [0.0] * n
         for i in range(n - 1, -1, -1):
-            prio[i] = nodes[i]["cost"] + nodes[i]["lat"] + max([prio[j] + WAKE for j in succ[i]] + [0.0])
-        left = [len(x["real"] | x["order"]) for x in nodes]
-        ready = {q: [] for q in Q}
-        rt = [0.0] * n
-        free = {q: 0.0 for q in Q}
-        for i in range(n):
-            if left[i] == 0:
-                ready[nodes[i]["q"]].append(i)
-        seq, end = [], [0.0] * n
-        while len(seq) < n:
-            best = None
-            for q in Q:
-                if not ready[q]:
-                    continue
-                e = min(max(free[q], rt[i]) for i in ready[q])
-                i = max((i for i in ready[q] if max(free[q], rt[i]) <= e + 0.02),
-                        key=lambda i: (prio[i] + (SHORT if nodes[i]["cost"] < 1 else 0), -i))
-                k = (max(free[q], rt[i]), -prio[i])
-                if best is None or k < best[0]:
-                    best = (k, q, i)
-            q, i = best[1], best[2]
-            ready[q].remove(i)
-            seq.append(i)
-            free[q] = best[0][0] + nodes[i]["cost"]
-            end[i] = free[q] + nodes[i]["lat"]
-            for j in succ[i]:
-                w = 0.05 if nodes[j]["q"] == q and not nodes[i]["lat"] else WAKE
-                if i in nodes[j]["order"]:
-                    w = 0.0
-                rt[j] = max(rt[j], end[i] + w)
-                left[j] -= 1
-                if left[j] == 0:
-                    ready[nodes[j]["q"]].append(j)
+            prio[i] = min(a[1] for a in nodes[i]["alt"].values()) + nodes[i]["lat"] + nodes[i].get("boost", 0.0) + max([prio[j] + WAKE for j, s in succs[i]] + [0.0])
+        best = run = deal(lambda i: (-prio[i], i), preds, None, False)
+        for _ in range(PASSES):
+            late = deal(lambda i: (-run[2][i], -i), succs, run[3], True)
+            run = deal(lambda i: (-late[2][i], i), preds, None, False)
+            if run[0] < best[0]:
+                best = run
+        on = best[3]
+        eng.extend(on)
+        seq = sorted(range(n), key=lambda i: (best[1][i], best[2][i], i))
+        for i, x in enumerate(nodes):
+            x["q"] = on[i]
+            x["calls"] = x["alt"][on[i]][0]
+            for b, p in x["banks"].items():
+                while p is not None and on[p] == on[i]:
+                    p = nodes[p]["banks"][b]
+                if p is not None:
+                    x["real"].add(p)
         total, clocks, known, at = {}, {}, {q: {} for q in Q}, {}
 
         def learn(q, key, cnt):
@@ -168,8 +193,8 @@ def rank_program(g, core, T, topo):
                     need[at[p][0]] = max(need.get(at[p][0], 0), at[p][1])
             for key in sorted(need, key=lambda key: -need[key]):
                 learn(q, key, need[key])
-            if x["wait"] is not None:
-                Q[q].wait_ge(T.sem[x["wait"][0]], x["wait"][1])
+            for s, c in x["wait"]:
+                Q[q].wait_ge(T.sem[s], c)
             key = x["sem"] or "q" + q
             if key == "none":
                 x["calls"][0]()
@@ -197,7 +222,7 @@ def rank_program(g, core, T, topo):
         return [x for x in xs if isinstance(x, dict)]
 
     def cy(n):
-        return 0.02 + CYC * max(64, n)
+        return 0.03 + CYC * max(64, n)
 
     def half(*vs):
         return cy(vs[0]["el"] * (0.5 if all(v["b2"] for v in vs) else 1))
@@ -209,349 +234,394 @@ def rank_program(g, core, T, topo):
             node("v", [lambda: g.vector.tensor_scalar(out["ap"], i0["ap"], sc(s1), sc(s2), op0, op1)], [i0] + scr(s1, s2), [out], half(out, i0))
 
     def tt(out, a, b, op):
-        c = 0.06 + CYC * GAT * out["el"] if a["ind"] else cy(out["el"] * (1 if a["ps"] or b["ps"] else 2))
+        c = 0.05 + CYC * GAT * out["el"] if a["ind"] else cy(out["el"] * (1 if a["ps"] or b["ps"] else 2))
         node("v", [lambda: g.vector.tensor_tensor(out["ap"], a["ap"], b["ap"], op)], [a, b], [out], c)
 
     def tc(out, a):
-        c = 0.06 + CYC * GAT * out["el"] if a["ind"] else 0.06 + CYC * SCA * out["el"] if out["ind"] else half(out, a)
+        c = 0.05 + CYC * GAT * out["el"] if a["ind"] else 0.05 + CYC * SCA * out["el"] if out["ind"] else half(out, a)
         node("v", [lambda: g.vector.tensor_copy(out["ap"], a["ap"])], [a], [out], c)
 
     def ms(out, c):
         node("v", [lambda: g.vector.memset(out["ap"], c)], [], [out], half(out))
 
     def scan(out, a, b, init, op0, op1):
-        node("v", [lambda: g.vector.tensor_tensor_scan(out["ap"], a["ap"], b["ap"], init, op0, op1)], [a, b], [out], half(out, a, b))
+        node("v", [lambda: g.vector.tensor_tensor_scan(out["ap"], a["ap"], b["ap"], sc(init), op0, op1)], [a, b] + scr(init), [out], half(out, a, b))
 
-    def act(out, a, func=COPY, bias=None, scale=None, wait=None):
+    def act(out, a, func=COPY, bias=None, scale=None, wait=(), acc=None):
         kw = {}
         if bias is not None:
             kw["bias"] = sc(bias)
         if scale is not None:
             kw["scale"] = sc(scale)
-        c = 0.08 + CYC * GAT * out["el"] if a["ind"] else cy(a["el"])
-        node("s", [lambda: g.scalar.activation(out["ap"], a["ap"], func, **kw)], [a] + scr(bias, scale), [out], c, wait=wait)
+        if acc is not None:
+            kw["accum_out"] = acc["ap"]
+        c = 0.065 + CYC * GAT * out["el"] if a["ind"] else cy(a["el"])
+        node("s", [lambda: g.scalar.activation(out["ap"], a["ap"], func, **kw)], [a] + scr(bias, scale), [out] + scr(acc), c, wait=wait)
 
     def mms(out, pairs, start=True, stop=True):
         n = len(pairs)
 
         def one(k, l, r):
-            return lambda: g.tensor.matmul(out["ap"], l["ap"], r["ap"], start and k == 0, stop and k == n - 1)
-        node("t", [one(k, l, r) for k, (l, r) in enumerate(pairs)], [x for p in pairs for x in p], [out], n * (0.01 + PEC * max(64, out["el"])))
+            return lambda: g.tensor.matmul(out["ap"], l["pick"]() if "pick" in l else l["ap"], r["ap"], start and k == 0, stop and k == n - 1)
+        node("t", [one(k, l, r) for k, (l, r) in enumerate(pairs)], [x for p in pairs for x in p], [out], n * (0.005 + PEC * max(64, out["el"])))
 
     def mm(out, l, r, start=True, stop=True):
         mms(out, [(l, r)], start, stop)
 
     def gio(out, pat, base, cm=0):
         kw = {} if PLACE[out["n"]][3] == I32 else {"allow_small_or_imprecise_dtypes": True}
-        node("g", [lambda: g.iota(out["ap"], pat, base, cm, **kw)], [], [out], 0.15 + 2 * CYC * out["el"])
+        node("g", [lambda: g.iota(out["ap"], pat, base, cm, **kw)], [], [out], 0.13 + 2 * CYC * out["el"])
 
     def dma(q, pairs, sem, rd, wr, us=2.0):
         node(q, [(lambda o=o, i=i: Q[q].dma_start(o, i)) for o, i in pairs], rd, wr, 0.06 * len(pairs), sem, us)
 
-    def kset(n, k):
-        return view(n, 128 * k, 128 * k + 128)
+    def copy(out, a, wait=()):
+        either(lambda: tc(out, a), lambda: act(out, a, wait=wait))
 
-    def every16(n):
-        return view(n, 15, NL, 16)
+    def affine(out, a, scale, bias):
+        either(lambda: ts(out, a, scale, MUL, bias, ADD), lambda: act(out, a, IDENT, bias=bias, scale=scale))
 
-    def lanes(pn, w, src, mask, out):
-        mm(view(pn, 0, NL), view("ID"), view(mask), True, False)
-        mm(view(pn, 0, NL), view(w), src, False, True)
+    def sign(out, a, at, below, w):
+        i = either(lambda: ts(out, a, at, GE, 0.5, SUB), lambda: act(out, a, SIGN, bias=below))
+        v = view(w)
+        v["pick"] = lambda: view(w, 0, 128)["ap"] if eng[i] == "s" else view(w, 128, 256)["ap"]
+        return v
+
+    def chain():
+        if links:
+            nodes[-1]["order"].add(links[-1])
+        links.append(len(nodes) - 1)
+
+    def boost(us):
+        nodes[-1]["boost"] = us
+
+    def slide(n, top, k):
+        return view(n, top - k, top - k + 128)
+
+    def every16(n, l0=0, l1=NL):
+        return view(n, l0 + 15, l1, 16)
+
+    def lanes(pn, w, src, out):
+        mm(view(pn, 0, NL), view("ID"), view("NM"), True, False)
+        for k, s in enumerate(src):
+            mm(view(pn, s[0], s[1]), view(w), s[2], False, k == len(src) - 1)
         scan(view(out), view("DJ"), view(pn, 0, NL), 0.0, MUL, MAX)
 
+    parts = list(zip(PARTS, PARTS[1:], WIN))
+
+    def place(l):
+        l0, l1, w = [p for p in parts if p[0] <= l < p[1]][0]
+        return w + l - l0, w + 2 * CO + NK * (l - l0)
+
+    def own(n, l0, l1, off=0):
+        return view(n, place(l0)[0] + off, place(l0)[0] + off + l1 - l0)
+
+    def cands(n, l0, l1, k=None):
+        a = place(l0)[1]
+        return view(n, a, a + NK * (l1 - l0)) if k is None else view(n, a + k, a + NK * (l1 - l0), NK)
+
+    def window(n, p, lst):
+        l0, l1, w = p
+        return view(n, w, w + 2 * CO + NK * (l1 - l0), 1, (lst, l0 // 16, l1 // 16))
+
+    def by_part(rec):
+        return [(l0, l1, own(rec, l0, l1)) for l0, l1, w in parts]
+
     ms(view("EHI"), 0)
+    dma("s", [(T.Y0[:, :], T.v0[:, :])], "dv", [], [view("Y0")])
+    dma("y", [(T.U[:, ga], T.w0[ga::2, :]) for ga in range(2)], "dw", [], [view("U", ap=0)], 2.3)
+    dma("y", [(T.EHI[0::16, :], T.e0[:, :]), (T.EHI[1::16, :], T.h0[:, :])], "de", [], [view("EHI")], 2.3)
+    first = len(nodes) - 1
+    dma("y", [(T.X[:, :], T.x0[:, :])], "dx", [], [view("X")], 5.5)
+    nodes[-1]["order"].add(first)
+    dma("s", [(T.TH[:, :], T.th[:, :])], "dth", [], [view("TH")], 6.0)
     gio(view("PI", 0, 1), [[1, 1]], 0, 1)
     gio(view("COLI"), [[1, NL]], 0)
+    gio(view("GRP"), [[1, 8], [0, 16]], 0)
     gio(view("RI"), [[0, 16], [1, 16]], 0)
-    wl = [[(T.U[:, 32 * ip + 16 * ga:32 * ip + 16 * ga + 16], T.w0[ga::2, 512 * ip:512 * ip + 512]) for ip in range(8)] for ga in range(2)]
-    dma("s", [(T.Y0[:, :], T.v0[:, :])], "dv", [], [view("Y0")])
-    dma("y", wl[0], "dwy", [], [view("U", 0, 8)], 3.0)
-    dma("s", wl[1], "dws", [], [view("U", 8, NL)], 3.0)
-    dma("y", [(T.EHI[0::16, :], T.e0[:, :]), (T.EHI[1::16, :], T.h0[:, :])], "de", [], [view("EHI")])
-    dma("y", [(T.X[:, :], T.x0[:, :])], "dx", [view("U"), view("Y0")], [view("X")], 6.0)
-    dma("y", [(T.TH[:, :], T.th[:, :])], "dth", [], [view("TH")], 6.0)
-    gio(view("V", 0, DEAD), [[0, DEAD]], -1)
-    gio(view("V", DEAD, VW), [[0, VW - DEAD]], 0)
-    gio(view("DM"), [[0, 256], [16384, 16]], 0)
-    gio(view("RS", NCELL, 2 * NCELL), [[0, NCELL]], 0)
-    gio(view("ZERO"), [[0, NL]], 0)
+    gio(view("H16"), [[1, 16], [0, 8]], 0)
+    gio(view("R8"), [[0, 16], [1, 8]], 0)
+    gio(view("DM"), [[0, MAXC], [16384, 16]], 0)
+    gio(view("V", 0, 2048), [[0, 2048]], -1)
+    ms(view("V", 2048, DEAD), -1.0)
+    ms(view("V", DEAD, VW), 0.0)
+    for l0, l1, w in parts:
+        gio(view("VAL", 17 * l0 // 16, 17 * l1 // 16), [[256, (l1 - l0) // 16], [1, 17]], 2 * CO - 1)
+        for n in ("RS0", "RS1", "DS"):
+            gio(view(n, w + l1 - l0, w + 2 * CO), [[0, 2 * CO - l1 + l0]], 0)
     gio(view("CT", 0, 4), [[1, 4]], 1)
     for t in range(NR):
         gio(view("CD", t, t + 1), [[0, 1]], 2 ** (3 - t))
-    gio(view("SZ"), [[0, 264]], 0)
-    gio(view("RE"), [[0, 264]], -1)
-    gio(view("RH"), [[0, 264]], -1)
+    gio(view("RR"), [[0, 288]], -1)
     gio(view("NEG"), [[0, NL]], -5)
-    gio(view("LOC", 0, 16), [[0, 16]], 0)
-    gio(view("LOC", DEAD, DEAD + 16), [[0, 16]], 0)
+    gio(view("LOC", 0, LAB0), [[0, LAB0]], 0)
+    gio(view("LOC", DEAD, VW), [[0, 16]], 0)
+    ms(view("CM", ap=T.CM[:, :, 0], el=NL), 1.0)
 
     def cc(j):
         return view("CC", j, j + 1)
 
     def cx(j):
         return view("CX", j, j + 1)
-    PQ, NP16, PF, WM, WE_, WH_, WF, KAP, KEEP, WWC, Q16, R3, R0, R2, R4, LO, NLO, BLO, QM8, QP8, L32, H32 = range(22)
+    (PQ, PG, NP16, PF, WM, WE_, WH_, NWE, NWH, WE2, LOW, KEEP, WWC, Q16, R0, R1, R2, R3, R4, R5, G2, G21, P8, KAP, B16, BK,
+     SGN, NR0, LO, BLO) = range(30)
     A = [view("CC", 40 + t, 41 + t) for t in range(NR)]
     ts(view("PI", 2, 3), view("PI", 0, 1), 15, AND)
     ts(view("PI", 4, 5), view("PI", 0, 1), 4, SHR)
+    ts(view("PI", 6, 7), view("PI", 0, 1), 7, AND)
     tc(cc(PQ), view("PI", 2, 3))
-    ts(cc(NP16), view("PI", 4, 5), -16.0, MUL)
+    tc(cc(PG), view("PI", 4, 5))
+    tc(cc(P8), view("PI", 6, 7))
     tc(cc(PF), view("PI", 0, 1))
-    ts(view("DMT"), view("COLI", 0, 128), cc(NP16), ADD)
-    ts(view("BLE"), view("DMT"), 15.0, LE)
-    ts(view("BGE"), view("DMT"), 0.0, GE)
     ts(cc(WM), cc(PQ), 2.0, MUL, 1.0, ADD)
-    tt(view("B"), view("BLE"), view("BGE"), MUL)
-    ts(view("WMK"), view("B"), cc(WM), MUL)
-    ts(cx(0), cc(PQ), 0.0, EQL, -2048.0, MUL)
-    ts(cx(1), cc(PQ), 1.0, EQL, 0.5, MUL)
-    tt(cx(2), cx(0), cx(1), ADD)
-    ts(view("CKR"), view("RI"), 0.0, MUL, cx(2), ADD)
+    ts(view("WMK"), view("GRP"), cc(PG), EQL, cc(WM), MUL)
     ts(view("ID"), view("COLI", 0, 128), cc(PF), EQL)
-    ts(view("IDM"), view("ID"), -4096.0, MUL)
-    ts(cx(3), cc(PQ), cc(PQ), MUL, 1.0, ADD)
-    tt(cc(KAP), cx(3), cc(PQ), ADD)
-    ms(A[0], 0.0)
-    for k in range(16):
-        ts(kset("KB", k), view("DMT"), float(k), EQL)
-    for r, j in ((0, R0), (2, R2), (3, R3), (4, R4)):
+    ts(view("IDM"), view("COLI", 0, 128), cc(PF), EQL, -4096.0, MUL)
+    act(cx(0), cc(PQ), SQUARE, bias=15.5, scale=-1.0)
+    act(cc(B16), cx(0), IDENT, bias=12.0 + 129 * 4096, scale=16.0)
+    act(cc(KAP), cx(0), SQUARE, bias=0.75)
+    act(cc(BK), cc(KAP), IDENT, bias=-0.375, scale=-8.0)
+    ms(A[0], MAGIC)
+    ts(view("B"), view("GRP"), cc(PG), EQL)
+    ts(cc(NP16), cc(PG), -16.0, MUL)
+    ts(view("DMT"), view("COLI", 0, 144), cc(NP16), ADD)
+    ts(view("KB"), view("DMT"), 15.0, EQL, 32768.0, MUL)
+    for r, j in ((0, R0), (1, R1), (2, R2), (3, R3), (4, R4), (5, R5)):
         ts(cc(j), cc(PQ), float(r), EQL)
+    tt(cx(1), cc(R5), cc(R0), ADD)
     ts(view("LI"), view("COLI"), cc(R3), MUL)
-    ts(view("LI0"), view("LI"), cc(R0), ADD)
-    ts(cx(4), cc(R0), 16.0, MUL)
-    tt(cc(WE_), cx(4), cc(R2), ADD)
-    ts(cx(6), cc(PQ), 1.0, EQL, 16.0, MUL)
-    tt(cc(WH_), cx(6), cc(R2), SUB)
-    ts(view("IDE"), view("ID"), cc(WE_), MUL)
-    ts(view("IDH"), view("ID"), cc(WH_), MUL)
-    for j in range(4):
-        j2 = (j + 2) % 4
-        pj = view("P%d" % (2 + j), 0, 512)
-        mms(pj, [(view("IDE"), view("KB", 512 * j, 512 * j + 512)), (view("IDH"), view("KB", 512 * j2, 512 * j2 + 512))])
-        act(view("KX", 512 * j, 512 * j + 512), pj)
+    ts(view("LI0"), view("COLI"), cc(R3), MUL, cc(R5), ADD)
+    act(cc(WE_), cc(R0), IDENT, bias=cc(R2), scale=16.0)
+    act(cc(NWH), cc(R1), IDENT, bias=cc(R2), scale=-16.0)
+    act(cc(NWE), cc(WE_), COPY, scale=-1.0)
+    act(cc(WH_), cc(NWH), COPY, scale=-1.0)
+    act(cc(WE2), cc(R5), IDENT, bias=cc(WE_), scale=float(LAB0))
+    act(cc(LOW), cc(R5), IDENT, bias=cc(WE_), scale=-16384.0)
+    for n, w7, w15 in (("KXA", WE_, WH_), ("KXB", WH_, WE_)):
+        ts(view("K1"), view("DMT"), 7.0, EQL, cc(w7), MUL)
+        ts(view("K2"), view("DMT"), 15.0, EQL, cc(w15), MUL)
+        tt(view(n), view("K1"), view("K2"), ADD)
+    act(cc(G2), cc(PG), COPY, scale=2.0)
+    act(cc(G21), cc(PG), IDENT, bias=1.0, scale=2.0)
     ts(cc(LO), cc(PQ), 8.0, LT)
-    ts(cc(NLO), cc(LO), -8192.0, MUL)
-    ts(cc(BLO), cc(LO), 8193.0, MUL, -1.0, ADD)
-    ts(view("M8"), view("RI", 0, 128), 8.0, LT)
-    tt(view("M8B"), view("B"), view("M8"), MUL)
-    tt(view("N8B"), view("B"), view("M8B"), SUB)
-    ts(view("CA"), view("M8B"), cc(WE_), MUL)
-    ts(view("CB"), view("N8B"), cc(WH_), MUL)
-    tt(view("WCA"), view("CA"), view("CB"), ADD)
-    ts(view("CD2"), view("M8B"), cc(WH_), MUL)
-    ts(view("CE2"), view("N8B"), cc(WE_), MUL)
-    tt(view("WCB"), view("CD2"), view("CE2"), ADD)
-    ts(cx(10), cc(LO), 999.0, MUL, -8.0, ADD)
-    tt(cc(QM8), cc(PQ), cx(10), ADD)
-    ts(cx(11), cc(LO), -999.0, MUL, 1007.0, ADD)
-    tt(cc(QP8), cc(PQ), cx(11), ADD)
-    ts(cc(L32), cc(LO), 32.0, MUL)
-    ts(cc(H32), cc(LO), -32.0, MUL, 32.0, ADD)
-    ts(view("ZA"), view("DMT"), cc(QM8), EQL, 32.0, MUL)
-    ts(view("ZB"), view("DMT"), cc(QP8), EQL, 32.0, MUL)
-    ts(view("YA"), view("ID"), cc(L32), MUL)
-    ts(view("YB"), view("ID"), cc(H32), MUL)
-    tt(view("PMA"), view("YA"), view("ZA"), ADD)
-    tt(view("PMB"), view("YB"), view("ZB"), ADD)
-    ts(view("WEB"), view("B"), cc(WE_), MUL)
-    ts(view("WHB"), view("B"), cc(WH_), MUL)
-    ts(view("DG"), view("RI"), cc(PQ), EQL)
-    ts(view("T0"), view("DG"), 8192.0, MUL)
-    ts(view("NM"), view("T0"), -8192.0, ADD)
-    ts(view("NMX"), view("NM"), 256.0, MUL)
-    ms(view("DJ"), 1.0)
-    ms(view("DJ", 0, NL, 16), 0.0)
-    ts(view("IDN"), view("ID"), -1.0, MUL)
-    ts(view("BGQ"), view("DMT"), cc(PQ), GE)
-    tt(view("LTI"), view("BLE"), view("BGQ"), MUL)
-    ts(cx(7), cc(PQ), 15.0, EQL, 4095.0, MUL)
-    ts(cc(WF), cx(7), 1.0, ADD)
-    ts(view("WFB"), view("B"), cc(WF), MUL)
-    ts(view("T1"), view("COLI"), 16.0, MUL, 8192.0, ADD)
-    tt(view("HSC"), view("T1"), view("DG"), MUL)
-    ts(view("NMB"), view("HSC"), -8192.0, ADD)
-    ts(view("WM16"), view("WMK"), 16.0, MUL)
-    ts(cc(Q16), cc(PQ), 16.0, MUL)
-    ts(view("BSF"), view("COLI", 0, 16), 256.0, MUL, cc(Q16), ADD)
-    ts(view("ILF"), view("COLI", 0, 16), 16.0, MUL, cc(PQ), ADD)
-    ts(view("TRF"), view("ILF"), float(TRASH), ADD)
-    ts(cc(KEEP), cc(PQ), 2.0, LE)
-    ts(view("IDK"), view("ID"), cc(KEEP), MUL)
+    act(cc(BLO), cc(LO), IDENT, bias=-16384.0, scale=32768.0 + LAB0)
+    for n, lo, hi, c in (("WA", NWE, NWH, "C1"), ("WB", NWH, NWE, "C2"), ("WZ", LOW, WE2, "C3")):
+        ts(view(c), view("H16"), cc(G2), EQL, cc(lo), MUL)
+        ts(view(n), view("H16"), cc(G21), EQL, cc(hi), MUL)
+        tt(view(n), view(n), view(c), ADD)
+    ts(view("M8B"), view("H16"), cc(G2), EQL)
+    ts(view("N8B"), view("H16"), cc(G21), EQL)
+    ts(view("PM8"), view("R8"), cc(P8), EQL, 4096.0, MUL)
+    tt(view("PMA", 0, 128), view("PM8"), view("M8B"), MUL)
+    tt(view("PMB", 0, 128), view("PM8"), view("N8B"), MUL)
+    copy(view("BB", 0, 128), view("B"))
+    for n in ("PMA", "PMB", "BB"):
+        affine(view(n, 128, 256), view(n, 0, 128), 2.0, 0.0)
+    act(view("WEB"), view("B"), COPY, scale=cc(WE2))
+    act(view("W1B"), view("B"), COPY, scale=cc(R1))
+    ts(view("NM"), view("RI"), cc(PQ), NE, -2.0 ** 21, MUL)
+    ts(view("DJ"), view("RI"), 0.0, GT)
+    act(view("IDN"), view("ID"), COPY, scale=-1.0)
+    act(view("WM16"), view("WMK"), COPY, scale=16.0)
+    act(cc(Q16), cc(PQ), COPY, scale=16.0)
+    act(view("BSF"), view("COLI", 0, 16), IDENT, bias=cc(Q16), scale=256.0)
+    act(view("ILF"), view("COLI", 0, 16), IDENT, bias=cc(PQ), scale=16.0)
+    act(view("TRF"), view("ILF"), IDENT, bias=float(TRASH))
+    act(view("VAL", 0, 272), view("VAL", 0, 272), IDENT, bias=cc(Q16))
+    for l0, l1, w in parts:
+        act(view("VAL", 17 * l0 // 16, 17 * l1 // 16, 17), view("ILF", l0 // 16, l1 // 16), IDENT, bias=float(-l0))
+    ts(cx(2), cc(PQ), 2.0, LE, cc(R5), ADD)
+    act(view("IDK"), view("ID"), COPY, scale=cx(2))
     ts(view("CT", 4, 8), view("CT", 0, 4), cc(R4), MUL)
     ts(view("CD", 4, 8), view("CD", 0, 4), cc(R2), MUL)
     tt(view("CT", 8, 12), view("CT", 4, 8), view("CD", 4, 8), ADD)
-    ts(view("CX", 20, 36), view("COLI", 0, 16), cc(PQ), ADD, 15.0, LT)
-    ts(view("CX", 36, 52), view("CX", 20, 36), 1.0, ADD)
-    scan(view("PEI", 0, 16), view("CX", 36, 52), view("CX", 36, 52), 1.0, MUL, MAX)
-    ts(view("WDG"), view("B"), view("PEI", 15, 16), MUL)
-    ts(view("WBG"), view("B"), 65536.0, MUL)
-    ts(view("SZS"), view("DJ"), 0.5, MUL)
-    ts(view("SZH"), view("DJ"), 0.0, EQL, 65536.0, MUL)
-    scan(view("THL"), view("SZS"), view("SZH"), 0.0, MUL, MAX)
-    tt(view("THD"), view("THL"), view("DG"), MUL)
-    ts(cx(9), cc(R4), 256.0, MUL)
-    tt(cc(WWC), cx(9), cc(R3), ADD)
-    act(view("KW"), view("KB"), COPY, scale=cc(WWC))
+    act(view("WBG"), view("B"), COPY, scale=-2.0 ** 18)
+    ts(view("C5"), view("DMT", 0, 128), cc(PQ), GT, -2.0 ** 18, MUL)
+    tt(view("C5"), view("C5"), view("B"), MUL)
+    act(view("C6"), view("ID"), COPY, scale=65536.0)
+    tt(view("WDG"), view("C5"), view("C6"), ADD)
+    act(cc(WWC), cc(R4), IDENT, bias=cc(R3), scale=256.0)
+    ts(view("KW"), view("DMT"), 15.0, EQL, cc(WWC), MUL)
+    act(view("NTH", 0, 4), view("TH"), IDENT, bias=0.5, scale=-1.0)
+    act(cc(SGN), cc(R1), IDENT, bias=cc(R0), scale=-1.0)
+    act(cc(NR0), cc(R0), COPY, scale=-1.0)
     tt(view("SR"), view("EHI"), view("LI0"), ADD)
 
-    def cells(y, more, a):
-        mms(view("P0", 0, NL), [(view("B"), view("CKR")), (view("WMK"), y)])
-        mm(view("P1", 0, NL), view("WMK"), y, True, False)
-        act(view("Y2"), view("P0", 0, NL), IDENT, bias=MAGIC, scale=1.0 / 4096)
-        act(view("MM"), view("Y2"), IDENT, bias=-MAGIC)
-        mm(view("P1", 0, NL), view("IDM"), view("MM"), False, True)
-        act(view("SQ"), view("P1", 0, NL), SQUARE)
-        act(view("X1"), view("SQ"), IDENT, bias=-0.4375, scale=1.0 / 32)
-        act(view("X2"), view("X1"), IDENT, bias=MAGIC + more)
-        act(view("P0", 0, NL), view("P1", 0, NL), IDENT, bias=a, scale=cc(KAP))
-        tt(view("A1"), view("X2"), view("P0", 0, NL), ADD)
+    def cells(y, a):
+        p = view("P1", 0, NL)
+        mm(view("P0", 0, NL), view("WMK"), y)
+        mm(p, view("WMK"), y, True, False)
+        affine(view("MM"), view("P0", 0, NL), 1.0 / 4096, 128.5 + 1.0 / 8192)
+        mm(p, view("IDM"), view("MM"), False, True)
+        act(view("SQ"), p, SQUARE, bias=cc(B16))
+        affine(view("X1"), view("SQ"), 1.0 / 32, cc(BK))
+        ts(view("A1"), view("X1"), a, ADD)
         ts(view("A2"), view("A1"), 4095, AND)
         tc(view("LA"), view("A2"))
+        boost(BL)
 
-    def current(rec):
-        mm(view("P6", 0, NL), view("WEB"), view(rec))
-        tc(view("E16"), view("P6", 0, NL))
-        lanes("P5", "WEB", view(rec), "NM", "CUS")
-        for n, w, o in (("CRA", "WCA", 0), ("CRB", "WCB", NL)):
-            mm(view("P7", o, o + NL), view(w), view(rec))
-            act(view(n), view("P7", o, o + NL))
+    def current(rec, t):
+        if t > 0:
+            for l0, l1, r in by_part(rec):
+                mm(view("P5", l0, l1), view("WEB"), r)
+            tc(view("E16"), view("P5", 0, NL))
+        lanes("P4", "WEB", by_part(rec), "CUS")
+        for l0, l1, r in by_part(rec):
+            mms(view("P7", l0, l1), [(view("IDK"), r), (view("ID"), view("LI", l0, l1))])
+        for l0, l1, r in by_part(rec):
+            affine(own(rec, l0, l1, CO), view("P7", l0, l1), 1.0, view("CT", 8 + t, 9 + t))
 
-    cells(view("Y0"), 0.0, A[0])
-    node("v", [lambda: g.vector.transpose(T.UT[:, :], T.U[:, :])], [view("U")], [view("UT")], cy(NL))
+    cells(view("Y0"), A[0])
+    for ip in range(8):
+        node("v", [lambda ip=ip: g.vector.transpose(T.UT[:, ip::8], T.U[:, :, ip, :])], [view("U", ap=0)], [view("UT", ip, NL, 8)], cy(32))
     tc(view("WL"), view("UT"))
-    for c in range(4):
-        (tc if c % 2 else act)(view("RT", 1024 * c, 1024 * c + 1024), view("SR", 0, NL, 1, ("WL", 64 * c, 64 * c + 64)))
-    current("SR")
+    for a in range(0, NL, GL):
+        copy(view("RT", NK * a, NK * (a + GL)), view("SR", 0, NL, 1, ("WL", a, a + GL)))
+    for l0, l1, r in by_part("RS0"):
+        copy(r, view("SR", l0, l1))
+    current("RS0", 0)
     tc(view("EL", 0, 16), every16("CUS"))
     tc(view("VO"), every16("CUS"))
     tc(view("V", 0, VW, 1, ("VO", 0, 16)), view("Y0"))
-    ts(view("E1L"), view("EL", 0, 16), 0.0625, MUL)
-    lanes("P7", "WHB", view("SR"), "NM", "PHS")
-    ts(view("H0L"), every16("PHS"), 0.0625, MUL)
+    ts(view("E0L"), view("EL", 0, 16), float(-LAB0), ADD, 0.0625, MUL)
+    tc(view("TS", 0, NL, 1, ("E0L", 0, 16)), view("SR"))
+    lanes("P7", "W1B", [(0, NL, view("TS"))], "TAS")
+    tc(view("TAU"), every16("TAS"))
 
-    rec = "SR"
     y = view("Y0")
     for t in range(NR):
-        newrec = "RN%d" % (t % 2)
+        rs, rn = "RS%d" % (t % 2), "RS%d" % ((t + 1) % 2)
         land = "LAND%d" % t
         O2 = view("O2A", 16 * t, 16 * t + 16)
         SP = view("SPA", 16 * t, 16 * t + 16)
         more = t + 1 < NR
-
-        def ch(n, c):
-            return view(n, CL * c, CL * c + CL)
-
-        def cj(n, c, off=0):
-            return view(n, off + CJ * c, off + CJ * c + CJ)
-
-        def cand(n, c, k, off=0):
-            return view(n, off + CJ * c + k, off + CJ * c + CJ, 16)
-
-        for c in range(NCH):
-            (tc if c in VR else act)(cj("RS", c), view("RT", 0, NCELL, 1, ("LA", CL * c, CL * c + CL)))
-            act(cj("XG", c), view("X", 0, NCELL, 1, ("LA", CL * c, CL * c + CL)))
-            pa, pb = view("P%d" % (c % 2), 0, CL), view("P%d" % (2 + c % 2), 0, CL)
-            pc, pn = view("P%d" % (7 if c % 2 else 4), 0, CL), view("P5", 0, CL)
-            mms(pa, [(kset("KX", k), cand("RS", c, k)) for k in range(8)])
-            mms(pb, [(kset("KX", k), cand("RS", c, k)) for k in range(8, 16)])
-            act(ch("LF", c), pa, IDENT, bias=cc(BLO), scale=cc(LO))
-            tt(ch("LM", c), ch("LF", c), pb, MAX)
-            ts(ch("LB", c), ch("LM", c), cc(NLO), ADD)
-            tt(ch("S1", c), pa, ch("CRA", c), LT)
-            tt(ch("S2", c), pb, ch("CRB", c), LT)
-            tt(cj("DS", c), view("V", 0, VW, 1, ("LB", CL * c, CL * c + CL)), cj("XG", c), SUB)
-            ts(cj("CM", c), cj("DS", c), 0.0, GT)
-            scan(cj("DS", c, NCELL), cj("DM", c), cj("XG", c), 0.0, MIN, MAX)
-            mms(pc, [(view("PMA"), ch("S1", c)), (view("PMB"), ch("S2", c))] + [(kset("KB", k), cand("CM", c, k)) for k in range(16)])
-            act(ch("HSQ", c), pc, SQUARE, bias=-45.5)
-            ts(ch("HIT", c), ch("HSQ", c), 9.0, LE)
-            mm(pn, view("LTI"), ch("HIT", c))
-            ts(ch("ZF", c), pn, 0.0, EQL)
-            mms(pn, [(view("ID"), ch("NMB", c)), (view("WFB"), ch("ZF", c))])
-            scan(ch("JLS", c), ch("DJ", c), pn, 0.0, MUL, MAX)
-            mms(view("P6", 0, CL), [(view("IDN"), view(y["n"], CL * c, CL * c + CL)), (view("ID"), cand("DS", c, 15, NCELL))])
-            act(cand("DS", c, 15, NCELL), view("P6", 0, CL))
-        act(view("RS", NCELL + 15, 2 * NCELL, 16), view(rec))
-        mms(view("P6", 0, NL), [(view("IDK"), view(rec)), (view("ID"), view("LI"))])
-        act(view("RS", NCELL + 14, 2 * NCELL, 16), view("P6", 0, NL), IDENT, bias=view("CT", 8 + t, 9 + t))
-        tc(view("JLU"), every16("JLS"))
         ynew = view(land, 0, NL)
-        act(ynew, view("DS", 0, 2 * NCELL, 1, ("JLU", 0, 16)), ABS)
-
-        dsts, ids = [], []
-        for j in range(1, N):
-            r = (rank + j) % N
-            d = (rank - r) % N
-            a = topo.addr(T.cores[r])
-            ids.append(DstId(rid=a[0], pnc=a[1]))
-            dsts.append(T[land][:, d * NL:(d + 1) * NL])
         msk = topo.mask(core, T.cores[(rank + 1) % N])
         neng = len(topo.engines(core, T.cores[(rank + 1) % N]))
+        JL = view("JS", 16, 272, 17)
+        mm(view("P7", 0, NL), view("ID"), view("NM"), True, False)
 
-        def send(ids=ids, dsts=dsts, msk=msk, t=t, src=ynew["ap"]):
-            return g.remote_dma_fused([RemoteDMATransfer(dst_ids=ids, dma_engine_mask=msk, remote_sem=T.sem["ar%d" % t],
-                                                         src=src, dsts=dsts)], local_sem=T.sem["lo%d" % t])
-        node("g", [send], [ynew], [view(land, NL, 4 * NL)], 0.1, "none", LAT)
+        for c, (l0, l1) in enumerate(zip(CHUNKS, CHUNKS[1:])):
+            n = l1 - l0
+            xg = view("XG", NK * l0, NK * l1)
+            for a in range(l0, l1, GL):
+                b = min(l1, a + GL)
+                copy(cands(rs, a, b), view("RT", 0, NCELL, 1, ("LA", a, b)))
+            for a in range(l0, l1, GL):
+                b = min(l1, a + GL)
+                copy(view("XG", NK * a, NK * b), view("X", 0, NCELL, 1, ("LA", a, b)))
+            pa, pb = view("P%d" % (c % 2), 0, n), view("P%d" % (2 + c % 2), 0, n)
+            pc = view("P%d" % (4 + c % 2), 0, 17 * n // 16)
+            cur = own(rs, l0, l1)
+            mms(pa, [(view("WA"), cur)] + [(slide("KXA", 7, k), cands(rs, l0, l1, k)) for k in range(8)])
+            mms(pb, [(view("WB"), cur)] + [(slide("KXB", 7, k), cands(rs, l0, l1, 8 + k)) for k in range(8)])
+            wa = sign(view("S1", l0, l1), pa, 0.0, 0.5, "PMA")
+            affine(view("LF", l0, l1), pa, cc(LO), cc(BLO))
+            wb = sign(view("S2", l0, l1), pb, 0.0, 0.5, "PMB")
+            tt(view("LM", l0, l1), view("LF", l0, l1), pb, MAX)
+            pz = view("P6", 0, n)
+            mms(pz, [(view("WZ"), cur), (wa, view("S1", l0, l1)), (wb, view("S2", l0, l1))])
+            tt(view("LF", l0, l1), view("LM", l0, l1), pz, ADD)
+            ts(view("LB", l0, l1), view("LF", l0, l1), float(DEAD), MIN, 0.0, MAX)
+            if c == 0:
+                scan(view("MX", NK * l0, NK * l1), view("DM", 0, NK * n), xg, 0.0, MIN, MAX)
+                chain()
+            tt(cands("DS", l0, l1), view("V", 0, VW, 1, ("LB", l0, l1)), xg, SUB)
+            chain()
+            ts(view("CM", 17 * l0, 17 * l1, ap=T.CM[:, l0:l1, 1:17], el=NK * n), cands("DS", l0, l1), 0.0, GT, 10.5 / 16, SUB)
+            chain()
+            if c > 0:
+                scan(view("MX", NK * l0, NK * l1), view("DM", 0, NK * n), xg, 0.0, MIN, MAX)
+                chain()
+            mms(pc, [(slide("KB", 15, q), view("CM", 17 * l0, 17 * l1, ap=T.CM[:, l0 + q:l1:16, :])) for q in range(16)])
+            boost(BC * (NL - l1) / 64)
+            scan(view("JS", 17 * l0 // 16, 17 * l1 // 16), pc, view("VAL", 17 * l0 // 16, 17 * l1 // 16), 0.0, MAX, MIN)
+            pm = view("P%d" % (c % 2), 256, 256 + n)
+            mms(pm, [(view("IDN"), view(y["n"], l0, l1)), (view("ID"), view("MX", NK * l0 + 15, NK * l1, 16))])
+            copy(own("DS", l0, l1), pm)
 
-        ts(view("ML"), every16("JLS"), 4096.0, GE)
-        tt(view("CUM"), every16("CUS"), view("ML"), MUL)
-        mm(view("P2", 0, NL), view("WBG"), view("ZERO"), True, False)
+            if l1 in LEADS:
+                p0 = LEADS[LEADS.index(l1) - 1]
+                c0, c1 = p0 // 16, l1 // 16
+                ts(view("ML", c0, c1), view("JS", 17 * c0 + 16, 17 * c1, 17), float(2 * CO), LT)
+                if t > 0:
+                    tt(view("CUM", c0, c1), every16("CUS", p0, l1), view("ML", c0, c1), MUL)
+                    for b in range(c0, c1):
+                        w = NL - 16 * b
+                        ts(view("EQ", 256 * b, 256 * b + w, ap=T.EQ[:, b, 0:w]), view("E16", 16 * b, NL), view("CUM", b, b + 1), EQL)
+                        if b < 15:
+                            mm(view("P7", 16 * b + 16, NL), view("WBG"), view("EQ", 256 * b, 256 * b + w, ap=T.EQ[:, b, 16:w]), False, False)
+                    mm(view("P7", p0, l1), view("WDG"), view("EQ", 256 * c0, 256 * c1, ap=T.EQ[:, c0:c1, 0:16]), False, False)
+            if l1 not in PARTS:
+                continue
 
-        def eq(c):
-            n = NL - 16 * c
-            p1, o1 = PLACE["E16"][:2]
-            p2, o2 = PLACE["CUM"][:2]
-            node("v", [lambda: g.vector.tensor_scalar(T.EQ[:, c, 0:n], T[p1][:, o1 + 16 * c:o1 + NL], T[p2][:, o2 + c:o2 + c + 1], None, EQL)],
-                 [view("E16", 16 * c, NL), view("CUM", c, c + 1)], [view("EQ", 256 * c, 256 * c + 256, ap=0)], cy(n / 2))
-        for c in range(16):
-            eq(c)
-            if c < 15:
-                mm(view("P2", 16 * c + 16, NL), view("WBG"), view("EQ", 256 * c, 256 * c + 256, ap=T.EQ[:, c, 16:NL - 16 * c]), False, False)
-        mm(view("P2", 0, NL), view("WDG"), view("EQ", 0, NCELL, ap=T.EQ[:, :, 0:16]), False, True)
-        lanes("P4", "WM16", ynew, "NMX", "MLS")
+            ip = PARTS.index(l1) - 1
+            p0 = PARTS[ip]
+            c0, c1 = p0 // 16, l1 // 16
+            jl = view("JS", 17 * c0 + 16, 17 * c1, 17)
+            tc(view("JLU", c0, c1), jl)
+            act(view(land, p0, l1), window("DS", parts[ip], "JLU"), ABS)
+            dsts, ids = [], []
+            for j in range(1, N):
+                r = (rank + j) % N
+                d = (rank - r) % N
+                a = topo.addr(T.cores[r])
+                ids.append(DstId(rid=a[0], pnc=a[1]))
+                dsts.append(T[land][:, d * NL + p0:d * NL + l1])
+
+            def send(ids=ids, dsts=dsts, key="%d_%d" % (t, ip), src=T[land][:, p0:l1]):
+                return g.remote_dma_fused([RemoteDMATransfer(dst_ids=ids, dma_engine_mask=msk, remote_sem=T.sem["ar" + key],
+                                                             src=src, dsts=dsts)], local_sem=T.sem["lo" + key])
+            node("g", [send], [view(land, p0, l1)], [view(land, d * NL + p0, d * NL + l1) for d in range(1, N)], 0.1, "none",
+                 LAT + (3.0 if t + ip == 0 else 0.0))
+
+        wc = sign(view("WC"), ynew, view("TH", t, t + 1), view("NTH", t, t + 1), "BB")
+        mm(view("P7", 0, NL), wc, view("WC"), False, True)
+        scan(view("LV"), view("DJ"), view("P7", 0, NL), 0.0, MUL, MAX)
+        lv = every16("LV")
+        if t == 0:
+            ts(view("ML6"), JL, float(2 * CO), LT, 65536.0, MUL)
+            tt(view("LV0"), view("ML6"), lv, ADD)
+            lv = view("LV0")
+        lanes("P4", "WM16", [(0, NL, ynew)], "MLS")
         tc(view("I1"), every16("MLS"))
         ts(view("I2"), view("I1"), 768, AND)
         tt(view("F1"), view("I2"), view("ILF"), ADD)
         tc(view("ZL"), view("F1"))
-        ts(view("WC"), ynew, view("TH", t, t + 1), GE)
-        lanes("P7", "B", view("WC"), "NM", "WIS")
-        ts(view("W1"), every16("WIS"), 9.0, GE)
         if more:
-            mm(view("P3", 0, 16), view("B"), view("ML"))
-            an = A[t + 1]
-            node("v", [lambda an=an: g.vector.tensor_reduce(an["ap"], T.P3[:, 0:16], AxisListType.X, ADD, negate=True)],
-                 [view("P3", 0, 16)], [an], cy(16))
-            cells(ynew, 256.0, an)
-        tt(view("LD"), view("THD"), view("P2", 0, NL), GT)
-        scan(view("LDS"), view("DJ"), view("LD"), 0.0, MUL, MAX)
-        tt(view("LDL"), view("ML"), every16("LDS"), MUL)
-        tt(SP, view("LDL"), view("W1"), MUL)
-        tt(view("JL2"), every16("JLS"), SP, SUB)
+            mm(view("P5", 0, 16), view("B"), view("ML"))
+            act(view("AD"), view("P5", 0, 16), IDENT, bias=16.0 + MAGIC / 16, scale=-1.0, acc=A[t + 1])
+            cells(ynew, A[t + 1])
+        ts(SP, lv, 65538.0, GE, float(CO), MUL)
+        tt(view("JL2"), JL, SP, ADD)
         tc(view("JL2U"), view("JL2"))
-        act(view(newrec), view("RS", 0, 2 * NCELL, 1, ("JL2U", 0, 16)))
+        for p in parts:
+            copy(own(rn, p[0], p[1]), window(rs, p, "JL2U"))
 
-        act(view("ZZ"), view(land, 0, N * NL, 1, ("ZL", 0, 16)), wait=("ar%d" % t, (N - 1) * neng))
-        lanes("P4", "WM16", view("ZZ"), "NMX", "MZS")
+        copy(view("ZZ"), view(land, 0, N * NL, 1, ("ZL", 0, 16)), wait=[("ar%d_%d" % (t, ip), (N - 1) * neng) for ip in range(len(parts))])
+        lanes("P5", "WM16", [(0, NL, view("ZZ"))], "MZS")
         tc(view("I3"), every16("MZS"))
         ts(view("I4"), view("I3"), 4, SHR, 15, AND)
         tt(view("F2"), view("I4"), view("BSF"), ADD)
         tc(view("XL"), view("F2"))
+        for l0, l1, r in by_part(rn):
+            tc(view("RT", 0, NCELL, 1, ("XL", l0 // 16, l1 // 16)), r)
         tc(view("X", 0, NCELL, 1, ("XL", 0, 16)), view("ZZ"))
-        tc(view("RT", 0, NCELL, 1, ("XL", 0, 16)), view(newrec))
-        ts(view("O1"), view("W1"), float(2 ** (3 - t)), MUL)
+        ts(view("O1"), lv, 65538.0, GE, float(2 ** (3 - t)), MUL)
         tt(O2, view("O1"), every16("CUS"), ADD)
-        tt(view("O3"), O2, view("TRF"), SUB)
-        tt(view("M1"), view("LDL"), view("O3"), MUL)
-        tt(view("M2"), view("M1"), view("TRF"), ADD)
+        tt(view("M1"), lv, O2, MIN)
+        tt(view("M2"), view("M1"), view("TRF"), MAX)
         tc(view("VO"), view("M2"))
         tc(view("V", 0, VW, 1, ("VO", 0, 16)), ynew)
+        boost(BV)
         if more:
-            current(newrec)
-        rec = newrec
+            current(rn, t + 1)
+        if t == NR - 2:
+            act(view("AL", 0, NCELL, 2), view("V", LAB0, DEAD, 2), SIGN, bias=1.0)
         y = ynew
 
-    dma("y", [(T.yx[:, :], T.X[:, :])], "oyx", [view("X")], [], 7.0)
-    ts(view("EA"), view("O2A"), float(-DEAD), ADD)
+    dma("y", [(T.yx[:, :], T.X[:, :])], "oyx", [view("X")], [], 5.5)
+    ts(view("EA"), view("O2A"), float(-DEAD), ADD, 1.0 / CO, MUL)
     tt(view("EB"), view("EA"), view("SPA"), MUL)
     ts(view("EL", 16, 80), view("EB"), float(DEAD), ADD)
     tc(view("ELU"), view("EL"))
@@ -560,25 +630,27 @@ def rank_program(g, core, T, topo):
     tc(view("KLU"), view("KI"))
     act(view("GV"), view("V", 0, VW, 1, ("ELU", 0, 80)))
     dma("y", [(T.yv[:, :], T.GV[:, :])], "oyv", [view("GV")], [])
-    ts(view("CM"), view("V", 16, DEAD), 0.0, GE)
-    scan(view("LOC", 16, DEAD), view("DM"), view("CM"), 0.0, MIN, ADD)
-    act(view("LG"), view("LOC", 0, 4128, 1, ("ELU", 0, 80)))
-    mms(view("P0", 0, NL), [(kset("KW", q), view("RT", 256 * q, 256 * q + 256)) for q in range(16)])
+    ts(view("AL", 1, NCELL, 2), view("V", LAB0 + 1, DEAD, 2), 0.0, GE)
+    dw = NK * MAXC
+    for a in range(0, NCELL, dw):
+        b = min(NCELL, a + dw)
+        scan(view("LOC", LAB0 + a, LAB0 + b), view("DM", 0, b - a), view("AL", a, b), 0.0, MIN, ADD)
+    act(view("LG"), view("LOC", 0, VW, 1, ("ELU", 0, 80)), COPY, scale=cc(SGN))
+    mms(view("P0", 0, NL), [(slide("KW", 15, q), view("RT", 256 * q, 256 * q + 256)) for q in range(16)])
     act(view("GW"), view("P0", 0, NL))
     dma("y", [(T.yw[:, :], T.GW[:, :])], "oyw", [view("GW")], [])
-    tc(view("SZ", 1, 257), view("LOC", 31, DEAD, 16))
-    tc(view("SZS"), view("SZ", 0, 264, 1, ("E1L", 0, 16)))
-    tc(view("SZH", 0, NL, 1, ("H0L", 0, 16)), view("SZS"))
-    scan(view("PHI"), view("SZH"), view("NEG"), 0.0, ADD, MAX)
-    tc(view("PHS"), view("PHI", 0, NL, 1, ("H0L", 0, 16)))
-    tc(view("RH", 0, 264, 1, ("E1L", 0, 16)), view("PHS"))
-    scan(view("PEI"), view("SZ", 1, 257), view("NEG"), -1.0, ADD, MAX)
-    tt(view("RE", 1, 257), view("PEI"), view("SZ", 1, 257), SUB)
-    tt(view("GE"), view("RE", 0, 264, 1, ("KLU", 0, 80)), view("LG"), ADD)
-    dma("y", [(T.ye[:, :], T.GE[0::16, :])], "oye", [view("GE")], [])
-    tt(view("GH"), view("RH", 0, 264, 1, ("KLU", 0, 80)), view("LG"), SUB)
-    dma("y", [(T.yh[:, :], T.GH[0::16, :])], "oyh", [view("GH")], [])
+    sizes = view("LOC", LAB0 + 15, DEAD, 16)
+    ts(view("SZB"), sizes, cc(R1), MUL)
+    act(view("SZA"), view("LOC", LAB0 - 1, DEAD - 16, 16), COPY, scale=cc(R0))
+    tc(view("SZH", 0, NL, 1, ("TAU", 0, 16)), view("SZB"))
+    scan(view("PHB"), view("SZH"), view("SZH"), 0.0, ADD, MAX)
+    scan(view("REA"), view("SZA"), view("NEG"), cc(NR0), ADD, MAX)
+    k0 = LAB0 // 16
+    tt(view("RR", k0, k0 + NL), view("PHB", 0, NL, 1, ("TAU", 0, 16)), view("REA"), ADD)
+    tt(view("GE"), view("RR", 0, 288, 1, ("KLU", 0, 80)), view("LG"), ADD)
+    dma("y", [(T.ye[:, :], T.GE[0::16, :]), (T.yh[:, :], T.GE[1::16, :])], "oye", [view("GE")], [])
 
     flush()
     for t in range(NR):
-        g.wait_ge(T.sem["lo%d" % t], neng)
+        for ip in range(len(parts)):
+            g.wait_ge(T.sem["lo%d_%d" % (t, ip)], neng)

@@ -4,7 +4,13 @@ from concourse.mybir import dt, AluOpType, AxisListType, ActivationFunctionType
 import comms_topo
 
 NL, NK, NCELL, NR, NS = 256, 16, 4096, 4, 1280
-CHUNKS = (0, 64, 128, 192, 256)
+RCH = (0, 64, 128, 192, 256)
+LCH = (0, 64, 128, 192, 256)
+XCH = (0, 64, 128, 192, 224, 256)
+VCH = (0, 64, 128, 192, 224, 256)
+CCH = (0, 64, 128, 192, 256)
+MCH = (0, 64, 128, 192, 256)
+SENDS = ((0, 128, 256), (0, 256), (0, 256), (0, 256))
 PARTS = (0, 256)
 LEADS = (0, 192, 256)
 CO = 256
@@ -15,10 +21,26 @@ VW = DEAD + 16
 MAGIC = 12582912.0
 CYC, PEC, GAT, SCA, WAKE, LAT = 0.00083, 0.00083, 1.56, 3.8, 0.15, 3.3
 SAME, SPARE, PASSES = 0.1, 1.0, 2
-BC, BL, BV = 2.5, 1.0, 4.0
-GL = 64
+CA = (2,)
+ORDER = {
+    "v": "-T0 -A1' -A2' -LA' -T1 -RT -X -CUS X0 VS Sa0 LF0 Sb0 -E16 LM0 M0 LP0 LB0 V0 LM1 LP1 C0 LB1 V1 LM2 C1 LP2 M1 LB2 J0 V2 LM3 J1 M2 LP3 LB3 Y128 V3 V4 C3 J2 C4 "
+         "ML0 M3 CU0 D Q0 J3 ML1 Y Q1 CU1 Q2 Q3 LV MLS O0 Z0 O1 Z1 O2 Z2 O3 Z3 O4 N0 O5 N1 A1 N2 A2 LA MZS W0 W1 W2 W3",
+    "s": "-T2 -T3 R0 R1 X1 Sa1 LF1 Sb1 R2 X2 Sa2 LF2 Sb2 R3 X3 X4 Sa3 LF3 Sb3 D128 Y128 C2 D192 Y WC AD MM SQ FL ZZ N3 AL kid",
+    "t": "a0 b0 z0 a1 b1 z1 a2 b2 n0 z2 m0 n1 a3 b3 m1 z3 D128 n2 m2 D192 n3 m3 Q0 Q1 Q2 Q3 WC MLS AD mark mark2 mod MZS CUS E16 kid",
+}
+TCH = (0, 64, 112, 184, 256)
+VG = 3200
+DU, DX = 3.2, 5.5
 WIN = [2 * CO * i + NK * l for i, l in enumerate(PARTS)]
-MAXC = max(b - a for a, b in zip(CHUNKS, CHUNKS[1:]))
+MAXC = max(b - a for a, b in zip(MCH, MCH[1:]))
+
+
+DEALT = []
+
+
+def spans(b):
+    return list(zip(b, b[1:]))
+
 
 BFT, F32, I32, U16 = "bfloat16", "float32", "int32", "uint16"
 SCRATCH, PLACE, SEMAPHORES = {}, {}, ["qv", "qs", "qt", "qg"]
@@ -32,8 +54,8 @@ for _n, _w, _d in (
 _at = {BFT: 0, F32: 0, I32: 0, U16: 0}
 for _d, _w, _ns in (
         (BFT, NL, "ZZ WC S1 S2 MM DJ NM LI LI0 COLI RI TS PMA PMB BB"),
-        (BFT, 144, "DMT KB KW KXA KXB K1 K2"),
-        (BFT, 128, "B WMK WM16 WEB W1B WDG WBG ID IDK IDM IDN GRP H16 R8 M8B N8B PM8 WA WB WZ C1 C2 C3 C4 C5 C6"),
+        (BFT, 144, "DMT ONE"), (BFT, 576, "KK"),
+        (BFT, 128, "ID5 B WMK WM16 WEB W1B WDG WBG ID IDK IDM IDN GRP H16 R8 M8B N8B PM8 WA WB WZ C1 C2 C3 C4 C5 C6 C7 C8"),
         (BFT, 32, "ML"),
         (F32, NL, "SQ X1 MLS MZS LV CUS TAS LF LM SZA SZB SZH PHB REA NEG"),
         (F32, 288, "RR VAL JS"), (F32, 96, "EL"), (F32, 64, "CC CX O2A SPA EA EB"),
@@ -54,7 +76,7 @@ PLACE["U"] = ("U", 0, NL, I32)
 for _t in range(NR):
     SCRATCH["LAND%d" % _t] = ("sbuf", [128, 4 * NL], BFT)
     PLACE["LAND%d" % _t] = ("LAND%d" % _t, 0, 4 * NL, BFT)
-    for _p in range(len(PARTS) - 1):
+    for _p in range(len(SENDS[_t]) - 1):
         SEMAPHORES += ["ar%d_%d" % (_t, _p), "lo%d_%d" % (_t, _p)]
 for _b in range(8):
     SCRATCH["P%d" % _b] = ("psum", [128, 512], F32)
@@ -74,7 +96,7 @@ def rank_program(g, core, T, topo):
         return
     N = len(T.cores)
     Q = {"v": g.vector, "s": g.scalar, "t": g.tensor, "g": g, "y": g.sync}
-    nodes, hist, bank, eng, links = [], {}, {}, [], []
+    nodes, hist, bank, eng, names = [], {}, {}, [], {}
 
     def view(n, lo=0, hi=None, step=1, ind=None, ap=None, el=None):
         phys, off, w, d = PLACE[n]
@@ -149,20 +171,38 @@ def rank_program(g, core, T, topo):
 
     def flush():
         n = len(nodes)
+        for q in ORDER:
+            row = [i for t in range(NR + 1) for w in ORDER[q].split() for i in names.get((w.strip("-"), t - (w[0] == "-")), [])
+                   if q in nodes[i]["alt"]]
+            for i in row:
+                nodes[i]["alt"] = {q: nodes[i]["alt"][q]}
+            for a, b in zip(row, row[1:]):
+                nodes[b]["order"].add(a)
         preds = [[(p, False) for p in x["real"]] + [(p, True) for p in x["order"] - x["real"]] for x in nodes]
         succs = [[] for _ in range(n)]
         for i in range(n):
             for p, soft in preds[i]:
                 succs[p].append((i, soft))
+        left = [len(p) for p in preds]
+        topo_order = [i for i in range(n) if not left[i]]
+        for i in topo_order:
+            for j, s in succs[i]:
+                left[j] -= 1
+                if not left[j]:
+                    topo_order.append(j)
+        assert len(topo_order) == n, [w for w in names if left[names[w][0]]][:8]
         prio = [0.0] * n
-        for i in range(n - 1, -1, -1):
+        for i in reversed(topo_order):
             prio[i] = min(a[1] for a in nodes[i]["alt"].values()) + nodes[i]["lat"] + nodes[i].get("boost", 0.0) + max([prio[j] + WAKE for j, s in succs[i]] + [0.0])
-        best = run = deal(lambda i: (-prio[i], i), preds, None, False)
-        for _ in range(PASSES):
-            late = deal(lambda i: (-run[2][i], -i), succs, run[3], True)
-            run = deal(lambda i: (-late[2][i], i), preds, None, False)
-            if run[0] < best[0]:
-                best = run
+        if not DEALT:
+            best = run = deal(lambda i: (-prio[i], i), preds, None, False)
+            for _ in range(PASSES):
+                late = deal(lambda i: (-run[2][i], -i), succs, run[3], True)
+                run = deal(lambda i: (-late[2][i], i), preds, None, False)
+                if run[0] < best[0]:
+                    best = run
+            DEALT.append(best)
+        best = DEALT[0]
         on = best[3]
         eng.extend(on)
         seq = sorted(range(n), key=lambda i: (best[1][i], best[2][i], i))
@@ -287,16 +327,15 @@ def rank_program(g, core, T, topo):
         v["pick"] = lambda: view(w, 0, 128)["ap"] if eng[i] == "s" else view(w, 128, 256)["ap"]
         return v
 
-    def chain():
-        if links:
-            nodes[-1]["order"].add(links[-1])
-        links.append(len(nodes) - 1)
+    def name(w, t, k=1):
+        names.setdefault((w, t), []).extend(range(len(nodes) - k, len(nodes)))
 
     def boost(us):
         nodes[-1]["boost"] = us
 
     def slide(n, top, k):
-        return view(n, top - k, top - k + 128)
+        a = 144 * ("KB", "KXA", "KXB", "KW").index(n) + top - k
+        return view("KK", a, a + 128)
 
     def every16(n, l0=0, l1=NL):
         return view(n, l0 + 15, l1, 16)
@@ -327,28 +366,29 @@ def rank_program(g, core, T, topo):
     def by_part(rec):
         return [(l0, l1, own(rec, l0, l1)) for l0, l1, w in parts]
 
-    ms(view("EHI"), 0)
+    gio(view("PI", 0, 1), [[1, 1]], 0, 1)
+    gio(view("EHI"), [[1, NL]], 0)
+    nodes[-1]["order"].add(0)
     dma("s", [(T.Y0[:, :], T.v0[:, :])], "dv", [], [view("Y0")])
-    dma("y", [(T.U[:, ga], T.w0[ga::2, :]) for ga in range(2)], "dw", [], [view("U", ap=0)], 2.3)
-    dma("y", [(T.EHI[0::16, :], T.e0[:, :]), (T.EHI[1::16, :], T.h0[:, :])], "de", [], [view("EHI")], 2.3)
+    dma("y", [(T.U[:, ga], T.w0[ga::2, :]) for ga in range(2)], "dw", [], [view("U", ap=0)], DU)
+    dma("y", [(T.EHI[0::16, :], T.e0[:, :]), (T.EHI[1::16, :], T.h0[:, :])], "de", [], [view("EHI")], DU - 0.2)
     first = len(nodes) - 1
-    dma("y", [(T.X[:, :], T.x0[:, :])], "dx", [], [view("X")], 5.5)
+    dma("y", [(T.X[:, :], T.x0[:, :])], "dx", [], [view("X")], DX)
     nodes[-1]["order"].add(first)
     dma("s", [(T.TH[:, :], T.th[:, :])], "dth", [], [view("TH")], 6.0)
-    gio(view("PI", 0, 1), [[1, 1]], 0, 1)
     gio(view("COLI"), [[1, NL]], 0)
     gio(view("GRP"), [[1, 8], [0, 16]], 0)
     gio(view("RI"), [[0, 16], [1, 16]], 0)
     gio(view("H16"), [[1, 16], [0, 8]], 0)
-    gio(view("R8"), [[0, 16], [1, 8]], 0)
     gio(view("DM"), [[0, MAXC], [16384, 16]], 0)
-    gio(view("V", 0, 2048), [[0, 2048]], -1)
-    ms(view("V", 2048, DEAD), -1.0)
+    nodes[-1]["order"].update(range(first + 3, len(nodes) - 1))
+    gio(view("V", 0, VG), [[0, VG]], -1)
+    nodes[-1]["order"].update(range(first + 3, len(nodes) - 2))
+    for a in range(VG, DEAD, 608):
+        ms(view("V", a, min(DEAD, a + 608)), -1.0)
     ms(view("V", DEAD, VW), 0.0)
-    for l0, l1, w in parts:
-        gio(view("VAL", 17 * l0 // 16, 17 * l1 // 16), [[256, (l1 - l0) // 16], [1, 17]], 2 * CO - 1)
-        for n in ("RS0", "RS1", "DS"):
-            gio(view(n, w + l1 - l0, w + 2 * CO), [[0, 2 * CO - l1 + l0]], 0)
+    gio(view("VAL", 0, 272), [[256, 16], [1, 17]], 2 * CO - 1)
+    gio(view("DS", SENDS[0][1], 2 * CO), [[0, 2 * CO - SENDS[0][1]]], 0)
     gio(view("CT", 0, 4), [[1, 4]], 1)
     for t in range(NR):
         gio(view("CD", t, t + 1), [[0, 1]], 2 ** (3 - t))
@@ -364,7 +404,7 @@ def rank_program(g, core, T, topo):
     def cx(j):
         return view("CX", j, j + 1)
     (PQ, PG, NP16, PF, WM, WE_, WH_, NWE, NWH, WE2, LOW, KEEP, WWC, Q16, R0, R1, R2, R3, R4, R5, G2, G21, P8, KAP, B16, BK,
-     SGN, NR0, LO, BLO) = range(30)
+     SGN, NR0, LO, BLO, P88) = range(31)
     A = [view("CC", 40 + t, 41 + t) for t in range(NR)]
     ts(view("PI", 2, 3), view("PI", 0, 1), 15, AND)
     ts(view("PI", 4, 5), view("PI", 0, 1), 4, SHR)
@@ -372,6 +412,7 @@ def rank_program(g, core, T, topo):
     tc(cc(PQ), view("PI", 2, 3))
     tc(cc(PG), view("PI", 4, 5))
     tc(cc(P8), view("PI", 6, 7))
+    act(cc(P88), cc(P8), IDENT, bias=8.0)
     tc(cc(PF), view("PI", 0, 1))
     ts(cc(WM), cc(PQ), 2.0, MUL, 1.0, ADD)
     ts(view("WMK"), view("GRP"), cc(PG), EQL, cc(WM), MUL)
@@ -385,35 +426,39 @@ def rank_program(g, core, T, topo):
     ts(view("B"), view("GRP"), cc(PG), EQL)
     ts(cc(NP16), cc(PG), -16.0, MUL)
     ts(view("DMT"), view("COLI", 0, 144), cc(NP16), ADD)
-    ts(view("KB"), view("DMT"), 15.0, EQL, 32768.0, MUL)
+    ms(view("KK"), 0.0)
+
+    def spot(n, at, w):
+        ts(view("KK", 144 * n + at, 144 * n + 144, 16), view("COLI", 0, 9), cc(PG), EQL, w, MUL)
+    spot(0, 15, 32768.0)
     for r, j in ((0, R0), (1, R1), (2, R2), (3, R3), (4, R4), (5, R5)):
         ts(cc(j), cc(PQ), float(r), EQL)
-    tt(cx(1), cc(R5), cc(R0), ADD)
     ts(view("LI"), view("COLI"), cc(R3), MUL)
-    ts(view("LI0"), view("COLI"), cc(R3), MUL, cc(R5), ADD)
+    ts(cx(1), cc(PQ), 1.0, LE, cc(R3), ADD)
     act(cc(WE_), cc(R0), IDENT, bias=cc(R2), scale=16.0)
     act(cc(NWH), cc(R1), IDENT, bias=cc(R2), scale=-16.0)
     act(cc(NWE), cc(WE_), COPY, scale=-1.0)
     act(cc(WH_), cc(NWH), COPY, scale=-1.0)
     act(cc(WE2), cc(R5), IDENT, bias=cc(WE_), scale=float(LAB0))
     act(cc(LOW), cc(R5), IDENT, bias=cc(WE_), scale=-16384.0)
-    for n, w7, w15 in (("KXA", WE_, WH_), ("KXB", WH_, WE_)):
-        ts(view("K1"), view("DMT"), 7.0, EQL, cc(w7), MUL)
-        ts(view("K2"), view("DMT"), 15.0, EQL, cc(w15), MUL)
-        tt(view(n), view("K1"), view("K2"), ADD)
+    for n, w7, w15 in ((1, WE_, WH_), (2, WH_, WE_)):
+        spot(n, 7, cc(w7))
+        spot(n, 15, cc(w15))
     act(cc(G2), cc(PG), COPY, scale=2.0)
     act(cc(G21), cc(PG), IDENT, bias=1.0, scale=2.0)
     ts(cc(LO), cc(PQ), 8.0, LT)
     act(cc(BLO), cc(LO), IDENT, bias=-16384.0, scale=32768.0 + LAB0)
-    for n, lo, hi, c in (("WA", NWE, NWH, "C1"), ("WB", NWH, NWE, "C2"), ("WZ", LOW, WE2, "C3")):
-        ts(view(c), view("H16"), cc(G2), EQL, cc(lo), MUL)
-        ts(view(n), view("H16"), cc(G21), EQL, cc(hi), MUL)
-        tt(view(n), view(n), view(c), ADD)
     ts(view("M8B"), view("H16"), cc(G2), EQL)
     ts(view("N8B"), view("H16"), cc(G21), EQL)
-    ts(view("PM8"), view("R8"), cc(P8), EQL, 4096.0, MUL)
-    tt(view("PMA", 0, 128), view("PM8"), view("M8B"), MUL)
-    tt(view("PMB", 0, 128), view("PM8"), view("N8B"), MUL)
+    for k, (n, lo, hi) in enumerate((("WA", NWE, NWH), ("WB", NWH, NWE), ("WZ", LOW, WE2))):
+        c, d, p = view("C%d" % (2 * k + 1)), view("C%d" % (2 * k + 2)), view("P%d" % (2 + k % 2), 0, 128)
+        act(c, view("M8B"), COPY, scale=cc(lo))
+        act(d, view("N8B"), COPY, scale=cc(hi))
+        mms(p, [(view("ID"), c), (view("ID"), d)])
+        act(view(n), p)
+    ts(view("PM8"), view("DMT", 0, 128), cc(P8), EQL, 4096.0, MUL)
+    copy(view("PMA", 0, 128), view("PM8"))
+    ts(view("PMB", 0, 128), view("DMT", 0, 128), cc(P88), EQL, 4096.0, MUL)
     copy(view("BB", 0, 128), view("B"))
     for n in ("PMA", "PMB", "BB"):
         affine(view(n, 128, 256), view(n, 0, 128), 2.0, 0.0)
@@ -422,6 +467,9 @@ def rank_program(g, core, T, topo):
     ts(view("NM"), view("RI"), cc(PQ), NE, -2.0 ** 21, MUL)
     ts(view("DJ"), view("RI"), 0.0, GT)
     act(view("IDN"), view("ID"), COPY, scale=-1.0)
+    act(view("ID5"), view("ID"), COPY, scale=-5.0 * 32768)
+    ms(view("ONE"), 1.0)
+    ms(view("ONE", 0, 144, 17), 0.0)
     act(view("WM16"), view("WMK"), COPY, scale=16.0)
     act(cc(Q16), cc(PQ), COPY, scale=16.0)
     act(view("BSF"), view("COLI", 0, 16), IDENT, bias=cc(Q16), scale=256.0)
@@ -436,57 +484,74 @@ def rank_program(g, core, T, topo):
     ts(view("CD", 4, 8), view("CD", 0, 4), cc(R2), MUL)
     tt(view("CT", 8, 12), view("CT", 4, 8), view("CD", 4, 8), ADD)
     act(view("WBG"), view("B"), COPY, scale=-2.0 ** 18)
-    ts(view("C5"), view("DMT", 0, 128), cc(PQ), GT, -2.0 ** 18, MUL)
-    tt(view("C5"), view("C5"), view("B"), MUL)
-    act(view("C6"), view("ID"), COPY, scale=65536.0)
-    tt(view("WDG"), view("C5"), view("C6"), ADD)
+    ts(view("C7"), view("DMT", 0, 128), cc(PQ), GT, -2.0 ** 18, MUL)
+    tt(view("C7"), view("C7"), view("B"), MUL)
+    name("Q0", 0, 2)
+    act(view("C8"), view("ID"), COPY, scale=65536.0)
+    tt(view("WDG"), view("C7"), view("C8"), ADD)
+    name("Q2", 0)
     act(cc(WWC), cc(R4), IDENT, bias=cc(R3), scale=256.0)
-    ts(view("KW"), view("DMT"), 15.0, EQL, cc(WWC), MUL)
+    spot(3, 15, cc(WWC))
     act(view("NTH", 0, 4), view("TH"), IDENT, bias=0.5, scale=-1.0)
     act(cc(SGN), cc(R1), IDENT, bias=cc(R0), scale=-1.0)
     act(cc(NR0), cc(R0), COPY, scale=-1.0)
-    tt(view("SR"), view("EHI"), view("LI0"), ADD)
+    ts(view("SR"), view("EHI"), cx(1), MUL, cc(R5), ADD)
 
-    def cells(y, a):
+    def cells(y, a, t):
         p = view("P1", 0, NL)
         mm(view("P0", 0, NL), view("WMK"), y)
+        name("mark", t)
         mm(p, view("WMK"), y, True, False)
+        name("mark2", t)
         affine(view("MM"), view("P0", 0, NL), 1.0 / 4096, 128.5 + 1.0 / 8192)
+        name("MM", t)
         mm(p, view("IDM"), view("MM"), False, True)
+        name("mod", t)
         act(view("SQ"), p, SQUARE, bias=cc(B16))
+        name("SQ", t)
         affine(view("X1"), view("SQ"), 1.0 / 32, cc(BK))
+        name("FL", t)
         ts(view("A1"), view("X1"), a, ADD)
+        name("A1", t)
         ts(view("A2"), view("A1"), 4095, AND)
+        name("A2", t)
         tc(view("LA"), view("A2"))
-        boost(BL)
+        name("LA", t)
 
     def current(rec, t):
+        r = own(rec, 0, NL)
         if t > 0:
-            for l0, l1, r in by_part(rec):
-                mm(view("P5", l0, l1), view("WEB"), r)
+            mm(view("P5", 0, NL), view("WEB"), r)
             tc(view("E16"), view("P5", 0, NL))
-        lanes("P4", "WEB", by_part(rec), "CUS")
-        for l0, l1, r in by_part(rec):
-            mms(view("P7", l0, l1), [(view("IDK"), r), (view("ID"), view("LI", l0, l1))])
-        for l0, l1, r in by_part(rec):
-            affine(own(rec, l0, l1, CO), view("P7", l0, l1), 1.0, view("CT", 8 + t, 9 + t))
+            name("E16", t - 1, 2)
+        lanes("P4", "WEB", [(0, NL, r)], "CUS")
+        name("CUS", t - 1, 3)
+        mms(view("P7", 0, NL), [(view("IDK"), r), (view("ID"), view("LI"))])
+        affine(own(rec, 0, NL, CO), view("P7", 0, NL), 1.0, view("CT", 8 + t, 9 + t))
+        name("kid", t - 1, 2)
 
-    cells(view("Y0"), A[0])
-    for ip in range(8):
-        node("v", [lambda ip=ip: g.vector.transpose(T.UT[:, ip::8], T.U[:, :, ip, :])], [view("U", ap=0)], [view("UT", ip, NL, 8)], cy(32))
+    cells(view("Y0"), A[0], -9)
+    for w in ("A1", "A2", "LA"):
+        names[(w + "'", -1)] = names[(w, -9)]
+    node("v", [lambda ip=ip: g.vector.transpose(T.UT[:, ip::8], T.U[:, :, ip, :]) for ip in range(8)], [view("U", ap=0)], [view("UT")], 8 * cy(32))
     tc(view("WL"), view("UT"))
-    for a in range(0, NL, GL):
-        copy(view("RT", NK * a, NK * (a + GL)), view("SR", 0, NL, 1, ("WL", a, a + GL)))
-    for l0, l1, r in by_part("RS0"):
-        copy(r, view("SR", l0, l1))
+    for c, (a, b) in enumerate(spans(TCH)):
+        copy(view("RT", NK * a, NK * b), view("SR", 0, NL, 1, ("WL", a, b)))
+        name("T%d" % c, -1)
+    copy(own("RS0", 0, NL), view("SR"))
     current("RS0", 0)
-    tc(view("EL", 0, 16), every16("CUS"))
     tc(view("VO"), every16("CUS"))
     tc(view("V", 0, VW, 1, ("VO", 0, 16)), view("Y0"))
-    ts(view("E0L"), view("EL", 0, 16), float(-LAB0), ADD, 0.0625, MUL)
-    tc(view("TS", 0, NL, 1, ("E0L", 0, 16)), view("SR"))
-    lanes("P7", "W1B", [(0, NL, view("TS"))], "TAS")
-    tc(view("TAU"), every16("TAS"))
+    name("VS", 0, 2)
+    tc(view("EL", 0, 16), every16("CUS"))
+
+    def second_order():
+        ts(view("E0L"), view("EL", 0, 16), float(-LAB0), ADD, 0.0625, MUL)
+        tc(view("TS", 0, NL, 1, ("E0L", 0, 16)), view("SR"))
+        name("Q1", 0, 2)
+        lanes("P6", "W1B", [(0, NL, view("TS"))], "TAS")
+        tc(view("TAU"), every16("TAS"))
+        name("Q3", 0, 4)
 
     y = view("Y0")
     for t in range(NR):
@@ -501,66 +566,97 @@ def rank_program(g, core, T, topo):
         JL = view("JS", 16, 272, 17)
         mm(view("P7", 0, NL), view("ID"), view("NM"), True, False)
 
-        for c, (l0, l1) in enumerate(zip(CHUNKS, CHUNKS[1:])):
+        name("nm", t)
+        for c, (l0, l1) in enumerate(spans(RCH)):
+            copy(cands(rs, l0, l1), view("RT", 0, NCELL, 1, ("LA", l0, l1)))
+            name("R%d" % c, t)
+        for c, (l0, l1) in enumerate(spans(XCH)):
+            copy(view("XG", NK * l0, NK * l1), view("X", 0, NCELL, 1, ("LA", l0, l1)))
+            name("X%d" % c, t)
+        for c, (l0, l1) in enumerate(spans(LCH)):
             n = l1 - l0
-            xg = view("XG", NK * l0, NK * l1)
-            for a in range(l0, l1, GL):
-                b = min(l1, a + GL)
-                copy(cands(rs, a, b), view("RT", 0, NCELL, 1, ("LA", a, b)))
-            for a in range(l0, l1, GL):
-                b = min(l1, a + GL)
-                copy(view("XG", NK * a, NK * b), view("X", 0, NCELL, 1, ("LA", a, b)))
             pa, pb = view("P%d" % (c % 2), 0, n), view("P%d" % (2 + c % 2), 0, n)
-            pc = view("P%d" % (4 + c % 2), 0, 17 * n // 16)
             cur = own(rs, l0, l1)
             mms(pa, [(view("WA"), cur)] + [(slide("KXA", 7, k), cands(rs, l0, l1, k)) for k in range(8)])
+            name("a%d" % c, t)
             mms(pb, [(view("WB"), cur)] + [(slide("KXB", 7, k), cands(rs, l0, l1, 8 + k)) for k in range(8)])
+            name("b%d" % c, t)
             wa = sign(view("S1", l0, l1), pa, 0.0, 0.5, "PMA")
+            name("Sa%d" % c, t)
             affine(view("LF", l0, l1), pa, cc(LO), cc(BLO))
+            name("LF%d" % c, t)
             wb = sign(view("S2", l0, l1), pb, 0.0, 0.5, "PMB")
+            name("Sb%d" % c, t)
             tt(view("LM", l0, l1), view("LF", l0, l1), pb, MAX)
+            name("LM%d" % c, t)
             pz = view("P6", 0, n)
             mms(pz, [(view("WZ"), cur), (wa, view("S1", l0, l1)), (wb, view("S2", l0, l1))])
+            name("z%d" % c, t)
             tt(view("LF", l0, l1), view("LM", l0, l1), pz, ADD)
+            name("LP%d" % c, t)
             ts(view("LB", l0, l1), view("LF", l0, l1), float(DEAD), MIN, 0.0, MAX)
-            if c == 0:
-                scan(view("MX", NK * l0, NK * l1), view("DM", 0, NK * n), xg, 0.0, MIN, MAX)
-                chain()
-            tt(cands("DS", l0, l1), view("V", 0, VW, 1, ("LB", l0, l1)), xg, SUB)
-            chain()
-            ts(view("CM", 17 * l0, 17 * l1, ap=T.CM[:, l0:l1, 1:17], el=NK * n), cands("DS", l0, l1), 0.0, GT, 10.5 / 16, SUB)
-            chain()
-            if c > 0:
-                scan(view("MX", NK * l0, NK * l1), view("DM", 0, NK * n), xg, 0.0, MIN, MAX)
-                chain()
-            mms(pc, [(slide("KB", 15, q), view("CM", 17 * l0, 17 * l1, ap=T.CM[:, l0 + q:l1:16, :])) for q in range(16)])
-            boost(BC * (NL - l1) / 64)
+            name("LB%d" % c, t)
+        for c, (l0, l1) in enumerate(spans(MCH)):
+            scan(view("MX", NK * l0, NK * l1), view("DM", 0, NK * (l1 - l0)), view("XG", NK * l0, NK * l1), 0.0, MIN, MAX)
+            name("M%d" % c, t)
+        for c, (l0, l1) in enumerate(spans(VCH)):
+            tt(cands("DS", l0, l1), view("V", 0, VW, 1, ("LB", l0, l1)), view("XG", NK * l0, NK * l1), SUB)
+            name("V%d" % c, t)
+            cm = view("CM", 17 * l0, 17 * l1, ap=T.CM[:, l0:l1, 1:17], el=NK * (l1 - l0))
+            if [k for k in CA if CCH[k] <= l0 < CCH[k + 1]]:
+                act(cm, cands("DS", l0, l1), SIGN, bias=-0.5)
+            else:
+                ts(cm, cands("DS", l0, l1), 0.0, GT, 10.5 / 16, SUB)
+            name("C%d" % c, t)
+        for c, (l0, l1) in enumerate(spans(CCH)):
+            n = l1 - l0
+            pc = view("P%d" % (4 + c % 2), 0, 17 * n // 16)
+            rows = [(slide("KB", 15, q), view("CM", 17 * l0, 17 * l1, ap=T.CM[:, l0 + q:l1:16, :])) for q in range(16)]
+            mms(pc, [(view("ID5"), view("ONE", 0, 17 * n // 16))] * (c in CA) + rows[:8], True, False)
+            name("n%d" % c, t)
+            mms(pc, rows[8:], False, True)
+            name("m%d" % c, t)
             scan(view("JS", 17 * l0 // 16, 17 * l1 // 16), pc, view("VAL", 17 * l0 // 16, 17 * l1 // 16), 0.0, MAX, MIN)
-            pm = view("P%d" % (c % 2), 256, 256 + n)
-            mms(pm, [(view("IDN"), view(y["n"], l0, l1)), (view("ID"), view("MX", NK * l0 + 15, NK * l1, 16))])
-            copy(own("DS", l0, l1), pm)
+            name("J%d" % c, t)
+            for m0, m1 in spans(sorted(set(SENDS[t] + MCH[-2:]))):
+                most = view("MX", NK * m0 + 15, NK * m1, 16)
+                if m1 == NL == l1:
+                    tt(own("DS", m0, m1), most, view(y["n"], m0, m1), SUB)
+                    name("D", t)
+                elif l0 < m1 <= l1:
+                    pm = view("P6" if m1 == MCH[-2] else "P%d" % (4 + c % 2), 256, 256 + m1 - m0)
+                    mms(pm, [(view("IDN"), view(y["n"], m0, m1)), (view("ID"), most)])
+                    copy(own("DS", m0, m1), pm)
+                    name("D%d" % m1, t, 2)
 
             if l1 in LEADS:
-                p0 = LEADS[LEADS.index(l1) - 1]
+                k = LEADS.index(l1) - 1
+                p0 = LEADS[k]
                 c0, c1 = p0 // 16, l1 // 16
                 ts(view("ML", c0, c1), view("JS", 17 * c0 + 16, 17 * c1, 17), float(2 * CO), LT)
+                name("ML%d" % k, t)
                 if t > 0:
                     tt(view("CUM", c0, c1), every16("CUS", p0, l1), view("ML", c0, c1), MUL)
+                    name("CU%d" % k, t)
                     for b in range(c0, c1):
                         w = NL - 16 * b
                         ts(view("EQ", 256 * b, 256 * b + w, ap=T.EQ[:, b, 0:w]), view("E16", 16 * b, NL), view("CUM", b, b + 1), EQL)
+                        name("Q%d" % (b // 4), t)
                         if b < 15:
                             mm(view("P7", 16 * b + 16, NL), view("WBG"), view("EQ", 256 * b, 256 * b + w, ap=T.EQ[:, b, 16:w]), False, False)
+                            name("Q%d" % (b // 4), t)
                     mm(view("P7", p0, l1), view("WDG"), view("EQ", 256 * c0, 256 * c1, ap=T.EQ[:, c0:c1, 0:16]), False, False)
-            if l1 not in PARTS:
+                    name("Q%d" % (b // 4), t)
+            if l1 not in SENDS[t]:
                 continue
 
-            ip = PARTS.index(l1) - 1
-            p0 = PARTS[ip]
+            ip = SENDS[t].index(l1) - 1
+            p0 = SENDS[t][ip]
             c0, c1 = p0 // 16, l1 // 16
             jl = view("JS", 17 * c0 + 16, 17 * c1, 17)
             tc(view("JLU", c0, c1), jl)
-            act(view(land, p0, l1), window("DS", parts[ip], "JLU"), ABS)
+            act(view(land, p0, l1), view("DS", 0, 2 * CO + NK * l1, 1, ("JLU", c0, c1)), ABS)
+            name("Y" if l1 == NL else "Y%d" % l1, t, 2)
             dsts, ids = [], []
             for j in range(1, N):
                 r = (rank + j) % N
@@ -577,47 +673,51 @@ def rank_program(g, core, T, topo):
 
         wc = sign(view("WC"), ynew, view("TH", t, t + 1), view("NTH", t, t + 1), "BB")
         mm(view("P7", 0, NL), wc, view("WC"), False, True)
+        name("WC", t, 2)
         scan(view("LV"), view("DJ"), view("P7", 0, NL), 0.0, MUL, MAX)
+        name("LV", t)
         lv = every16("LV")
         if t == 0:
+            second_order()
             ts(view("ML6"), JL, float(2 * CO), LT, 65536.0, MUL)
             tt(view("LV0"), view("ML6"), lv, ADD)
+            name("LV", t, 2)
             lv = view("LV0")
+
+        def steps(w, *calls):
+            for k, c in enumerate(calls):
+                c()
+                name("%s%d" % (w, k), t)
         lanes("P4", "WM16", [(0, NL, ynew)], "MLS")
-        tc(view("I1"), every16("MLS"))
-        ts(view("I2"), view("I1"), 768, AND)
-        tt(view("F1"), view("I2"), view("ILF"), ADD)
-        tc(view("ZL"), view("F1"))
+        name("MLS", t, 2)
+        steps("Z", lambda: tc(view("I1"), every16("MLS")), lambda: ts(view("I2"), view("I1"), 768, AND),
+              lambda: tt(view("F1"), view("I2"), view("ILF"), ADD), lambda: tc(view("ZL"), view("F1")))
         if more:
             mm(view("P5", 0, 16), view("B"), view("ML"))
             act(view("AD"), view("P5", 0, 16), IDENT, bias=16.0 + MAGIC / 16, scale=-1.0, acc=A[t + 1])
-            cells(ynew, A[t + 1])
-        ts(SP, lv, 65538.0, GE, float(CO), MUL)
-        tt(view("JL2"), JL, SP, ADD)
-        tc(view("JL2U"), view("JL2"))
-        for p in parts:
-            copy(own(rn, p[0], p[1]), window(rs, p, "JL2U"))
+            name("AD", t, 2)
+            cells(ynew, A[t + 1], t)
+        steps("N", lambda: ts(SP, lv, 65538.0, GE, float(CO), MUL), lambda: tt(view("JL2"), JL, SP, ADD), lambda: tc(view("JL2U"), view("JL2")),
+              lambda: copy(own(rn, 0, NL), window(rs, parts[0], "JL2U")))
 
-        copy(view("ZZ"), view(land, 0, N * NL, 1, ("ZL", 0, 16)), wait=[("ar%d_%d" % (t, ip), (N - 1) * neng) for ip in range(len(parts))])
+        copy(view("ZZ"), view(land, 0, N * NL, 1, ("ZL", 0, 16)), wait=[("ar%d_%d" % (t, ip), (N - 1) * neng) for ip in range(len(SENDS[t]) - 1)])
+        name("ZZ", t)
         lanes("P5", "WM16", [(0, NL, view("ZZ"))], "MZS")
-        tc(view("I3"), every16("MZS"))
-        ts(view("I4"), view("I3"), 4, SHR, 15, AND)
-        tt(view("F2"), view("I4"), view("BSF"), ADD)
-        tc(view("XL"), view("F2"))
-        for l0, l1, r in by_part(rn):
-            tc(view("RT", 0, NCELL, 1, ("XL", l0 // 16, l1 // 16)), r)
+        name("MZS", t, 2)
+        steps("W", lambda: tc(view("I3"), every16("MZS")), lambda: ts(view("I4"), view("I3"), 4, SHR, 15, AND),
+              lambda: tt(view("F2"), view("I4"), view("BSF"), ADD), lambda: tc(view("XL"), view("F2")))
+        tc(view("RT", 0, NCELL, 1, ("XL", 0, 16)), own(rn, 0, NL))
+        name("RT", t)
         tc(view("X", 0, NCELL, 1, ("XL", 0, 16)), view("ZZ"))
-        ts(view("O1"), lv, 65538.0, GE, float(2 ** (3 - t)), MUL)
-        tt(O2, view("O1"), every16("CUS"), ADD)
-        tt(view("M1"), lv, O2, MIN)
-        tt(view("M2"), view("M1"), view("TRF"), MAX)
-        tc(view("VO"), view("M2"))
-        tc(view("V", 0, VW, 1, ("VO", 0, 16)), ynew)
-        boost(BV)
+        name("X", t)
+        steps("O", lambda: ts(view("O1"), lv, 65538.0, GE, float(2 ** (3 - t)), MUL), lambda: tt(O2, view("O1"), every16("CUS"), ADD),
+              lambda: tt(view("M1"), lv, O2, MIN), lambda: tt(view("M2"), view("M1"), view("TRF"), MAX), lambda: tc(view("VO"), view("M2")),
+              lambda: tc(view("V", 0, VW, 1, ("VO", 0, 16)), ynew))
         if more:
             current(rn, t + 1)
         if t == NR - 2:
             act(view("AL", 0, NCELL, 2), view("V", LAB0, DEAD, 2), SIGN, bias=1.0)
+            name("AL", t)
         y = ynew
 
     dma("y", [(T.yx[:, :], T.X[:, :])], "oyx", [view("X")], [], 5.5)
@@ -630,10 +730,11 @@ def rank_program(g, core, T, topo):
     tc(view("KLU"), view("KI"))
     act(view("GV"), view("V", 0, VW, 1, ("ELU", 0, 80)))
     dma("y", [(T.yv[:, :], T.GV[:, :])], "oyv", [view("GV")], [])
-    ts(view("AL", 1, NCELL, 2), view("V", LAB0 + 1, DEAD, 2), 0.0, GE)
     dw = NK * MAXC
     for a in range(0, NCELL, dw):
         b = min(NCELL, a + dw)
+        either(lambda: ts(view("AL", a + 1, b, 2), view("V", LAB0 + a + 1, LAB0 + b, 2), 0.0, GE),
+               lambda: act(view("AL", a + 1, b, 2), view("V", LAB0 + a + 1, LAB0 + b, 2), SIGN, bias=1.0))
         scan(view("LOC", LAB0 + a, LAB0 + b), view("DM", 0, b - a), view("AL", a, b), 0.0, MIN, ADD)
     act(view("LG"), view("LOC", 0, VW, 1, ("ELU", 0, 80)), COPY, scale=cc(SGN))
     mms(view("P0", 0, NL), [(slide("KW", 15, q), view("RT", 256 * q, 256 * q + 256)) for q in range(16)])
@@ -652,5 +753,5 @@ def rank_program(g, core, T, topo):
 
     flush()
     for t in range(NR):
-        for ip in range(len(parts)):
+        for ip in range(len(SENDS[t]) - 1):
             g.wait_ge(T.sem["lo%d_%d" % (t, ip)], neng)

@@ -4,38 +4,41 @@ from concourse.mybir import dt, AluOpType, AxisListType, ActivationFunctionType
 import comms_topo
 
 NL, NK, NCELL, NR, NS = 256, 16, 4096, 4, 1280
-RCH = (0, 64, 128, 192, 256)
+RCH = (0, 32, 64, 128, 192, 256)
 LCH = (0, 64, 128, 192, 256)
 XCH = (0, 64, 128, 192, 224, 256)
 VCH = (0, 64, 128, 192, 224, 256)
 CCH = (0, 64, 128, 192, 256)
 MCH = (0, 64, 128, 192, 256)
-SENDS = ((0, 128, 256), (0, 256), (0, 256), (0, 256))
-PARTS = (0, 256)
+YCH = (0, 192, 256)
 LEADS = (0, 192, 256)
+SENDS = ((0, 128, 256), (0, 256), (0, 256), (0, 128, 256))
+TCH = (0, 64, 112, 184, 256)
+ECH = (0, 64, 128, 192, 256)
+CA = (1, 2)
 CO = 256
+WW = 2 * CO + NCELL
 TRASH = 16
 LAB0 = 272
 DEAD = LAB0 + NCELL
 VW = DEAD + 16
-MAGIC = 12582912.0
-CYC, PEC, GAT, SCA, WAKE, LAT = 0.00083, 0.00083, 1.56, 3.8, 0.15, 3.3
-SAME, SPARE, PASSES = 0.1, 1.0, 2
-CA = (2,)
-ORDER = {
-    "v": "-T0 -A1' -A2' -LA' -T1 -RT -X -CUS X0 VS Sa0 LF0 Sb0 -E16 LM0 M0 LP0 LB0 V0 LM1 LP1 C0 LB1 V1 LM2 C1 LP2 M1 LB2 J0 V2 LM3 J1 M2 LP3 LB3 Y128 V3 V4 C3 J2 C4 "
-         "ML0 M3 CU0 D Q0 J3 ML1 Y Q1 CU1 Q2 Q3 LV MLS O0 Z0 O1 Z1 O2 Z2 O3 Z3 O4 N0 O5 N1 A1 N2 A2 LA MZS W0 W1 W2 W3",
-    "s": "-T2 -T3 R0 R1 X1 Sa1 LF1 Sb1 R2 X2 Sa2 LF2 Sb2 R3 X3 X4 Sa3 LF3 Sb3 D128 Y128 C2 D192 Y WC AD MM SQ FL ZZ N3 AL kid",
-    "t": "a0 b0 z0 a1 b1 z1 a2 b2 n0 z2 m0 n1 a3 b3 m1 z3 D128 n2 m2 D192 n3 m3 Q0 Q1 Q2 Q3 WC MLS AD mark mark2 mod MZS CUS E16 kid",
-}
-TCH = (0, 64, 112, 184, 256)
 VG = 3200
-DU, DX = 3.2, 5.5
-WIN = [2 * CO * i + NK * l for i, l in enumerate(PARTS)]
+LW = 1024
+MAGIC = 12582912.0
+CYC, PEC, GAT, SCA, WAKE, SAME, LAT, DU, DX = 0.00083, 0.00083, 1.5, 3.8, 0.12, 0.19, 3.7, 4.1, 8.4
+ORDER = {
+    "v": "-k0 -TR -SR -WL -A1' -T1 -own -A2' -T0 -LA' -E16 -RT -CUS R1 VS -X Sa0 X0 LM0 LP0 M0 LB0 LM1 V0 LP1 -kb LM2 LB1 C0 LP2 V1 "
+         "LB2 M1 V2 LM3 M2 LP3 -kc LB3 J0 J1 V3 Y128 V4 C3 C4 M3 J2 H0 ML0 D MLSa CU0 Y192 Za0 Q0 J3 Y H1 Q1 Q2 ML1 Za1 Za2 CU1 Q3 Za3 H2 "
+         "LV MZSa MLS O0 N0 Wa0 O1 N1 Wa1 Z0 O2 H3 E0 Wa2 Z1 O3 N2 Wa3 Z2 E1 O4 x1 Z3 O5 A1 MZS x0 A2 W0 E2 W1 E4 E3 W2 LA al3 W3 "
+         "rt0 x3 L1 E5 rt1 L3 L0 L2 rt2 G1 E6 x2 G4 rt3 G3 G5 G7",
+    "s": "-k0 -MM' -k1 -k3 -SQ' -k7 -k9 -k2 -FL' -k5 -k6 -k4 -T3 -T2 R0 R2 LF0 Sb0 R3 Sb1 Sa1 LF1 X1 Sa2 LF2 Sb2 R4 X2 C1 Sa3 Sb3 LF3 X3 X4 "
+         "C2 D128 -k8 Y128 D192 -kid' Y192 Y WC MM SQ FL AD ZZa ZZ N3 AL al0 al2 kid al1 GV G0 G2 GW G6",
+    "t": "-mark' -mark2' -mod' -k3 -k2 -k1 -CUS' a0 b0 b1 z0 a1 a2 b2 z1 z2 n0 b3 a3 m0 n1 z3 m1 nmAa nmBa D192 D128 n2 m2 MLSa n3 m3 "
+         "-kid' H1 nmA nm Q0 Q1 Q2 Q3 WC MLS H3 AD MZSa mark mark2 mod nmB MZS CUS E16 kid",
+    "g": "-k0 -kd",
+    "y": "-k0",
+}
 MAXC = max(b - a for a, b in zip(MCH, MCH[1:]))
-
-
-DEALT = []
 
 
 def spans(b):
@@ -45,23 +48,22 @@ def spans(b):
 BFT, F32, I32, U16 = "bfloat16", "float32", "int32", "uint16"
 SCRATCH, PLACE, SEMAPHORES = {}, {}, ["qv", "qs", "qt", "qg"]
 for _n, _w, _d in (
-        ("X", NCELL, BFT), ("RT", NCELL, BFT), ("V", VW, BFT), ("RS0", WIN[-1], BFT), ("RS1", WIN[-1], BFT), ("XG", NCELL, BFT),
-        ("DS", WIN[-1], BFT), ("MX", NCELL, BFT), ("DM", NK * MAXC, BFT), ("LOC", VW, BFT), ("AL", NCELL, BFT),
+        ("X", NCELL, BFT), ("RT", NCELL, BFT), ("V", VW, BFT), ("RS0", WW, BFT), ("RS1", WW, BFT), ("XG", NCELL, BFT),
+        ("DS", WW, BFT), ("MX", NCELL, BFT), ("DM", NK * MAXC, BFT), ("LOC", VW, BFT), ("AL", NCELL, BFT),
         ("Y0", NL, BFT), ("TH", 4, BFT), ("EHI", NL, I32), ("UT", NL, I32), ("WL", NL, U16),
         ("SR", NL, BFT), ("LG", NS, F32), ("GE", NS, F32), ("GV", NS, BFT), ("GW", NL, F32)):
     SCRATCH[_n] = ("sbuf", [128, _w], _d)
     PLACE[_n] = (_n, 0, _w, _d)
 _at = {BFT: 0, F32: 0, I32: 0, U16: 0}
 for _d, _w, _ns in (
-        (BFT, NL, "ZZ WC S1 S2 MM DJ NM LI LI0 COLI RI TS PMA PMB BB"),
-        (BFT, 144, "DMT ONE"), (BFT, 576, "KK"),
-        (BFT, 128, "ID5 B WMK WM16 WEB W1B WDG WBG ID IDK IDM IDN GRP H16 R8 M8B N8B PM8 WA WB WZ C1 C2 C3 C4 C5 C6 C7 C8"),
+        (BFT, NL, "ZZ WC S1 S2 MM DJ NM LI COLI RI TS PMA PMB BB"), (BFT, 144, "ONE"), (BFT, 576, "KK"),
+        (BFT, 128, "DMT ID5 B WMK WM16 WEB W1B WDG WBG ID IDK IDM IDN GRP H16 M8B N8B WA WB WZ C1 C2 C3 C4 C5 C6 C7"),
         (BFT, 32, "ML"),
-        (F32, NL, "SQ X1 MLS MZS LV CUS TAS LF LM SZA SZB SZH PHB REA NEG"),
+        (F32, NL, "SQ X1 MLS MZS LV CUS TAS LF LM SZA SZH PHB REA NEG"),
         (F32, 288, "RR VAL JS"), (F32, 96, "EL"), (F32, 64, "CC CX O2A SPA EA EB"),
-        (F32, 32, "BSF ILF TRF JL2 CUM O1 M1 M2 F1 F2 CT CD NTH AD ML6 LV0"),
+        (F32, 32, "BSF BSE ILF TRF JL2 CUM O1 M1 M2 F1 F2 CT CD NTH AD ML6 LV0"),
         (I32, NL, "A1 A2"), (I32, 96, "ELI KI"), (I32, 32, "PI I1 I2 I3 I4"),
-        (U16, NL, "LA LB E16"), (U16, 96, "ELU KLU"), (U16, 32, "JLU JL2U VO ZL XL E0L TAU")):
+        (U16, NL, "LA LB E16"), (U16, 96, "ELU KLU"), (U16, 32, "JLU JL2U VO ZL XL E0L TAU SIG")):
     for _n in _ns.split():
         PLACE[_n] = ("all_" + _d, _at[_d], {32: 16, 96: 80}.get(_w, _w), _d)
         _at[_d] += _w
@@ -81,7 +83,7 @@ for _t in range(NR):
 for _b in range(8):
     SCRATCH["P%d" % _b] = ("psum", [128, 512], F32)
     PLACE["P%d" % _b] = ("P%d" % _b, 0, 512, F32)
-SEMAPHORES += ["dth", "dv", "de", "dw", "dx", "oyx", "oyv", "oyw", "oye"]
+SEMAPHORES += ["dth", "dv", "de", "dw", "dx", "oyv", "oyw", "oye"] + ["oyx%d" % _c for _c in range(len(ECH) - 1)]
 
 ADD, SUB, MUL, MAX, MIN = AluOpType.add, AluOpType.subtract, AluOpType.mult, AluOpType.max, AluOpType.min
 GE, GT, LE, LT, EQL, NE = AluOpType.is_ge, AluOpType.is_gt, AluOpType.is_le, AluOpType.is_lt, AluOpType.is_equal, AluOpType.not_equal
@@ -114,10 +116,10 @@ def rank_program(g, core, T, topo):
         i = len(nodes)
         real, banks = set(), {}
         for v, w in [(v, False) for v in rd] + [(v, True) for v in wr]:
-            spans = [(v["n"], v["lo"], v["hi"], w)]
+            touched = [(v["n"], v["lo"], v["hi"], w)]
             if v["ind"] is not None:
-                spans.append((v["ind"][0], v["ind"][1], v["ind"][2], False))
-            for (n, lo, hi, ww) in spans:
+                touched.append((v["ind"][0], v["ind"][1], v["ind"][2], False))
+            for (n, lo, hi, ww) in touched:
                 if n[0] == "P" and n[1:].isdigit():
                     if n not in banks:
                         banks[n] = bank.get(n)
@@ -147,28 +149,6 @@ def rank_program(g, core, T, topo):
         nodes[-1]["wait"] = other["wait"]
         return len(nodes) - 1
 
-    def deal(rank_of, preds, fixed, back):
-        n = len(nodes)
-        start, end, slots, on = [0.0] * n, [0.0] * n, {q: [] for q in Q}, [None] * n
-        for i in sorted(range(n), key=rank_of):
-            x, best = nodes[i], None
-            for q in ([fixed[i]] if fixed else sorted(x["alt"])):
-                c = x["alt"][q][1]
-                t = 0.0
-                for p, soft in preds[i]:
-                    lat = (x if back else nodes[p])["lat"]
-                    t = max(t, end[p] + (0.0 if soft and on[p] == q else lat + (SAME if on[p] == q and not lat else WAKE)))
-                k, sl = 0, slots[q]
-                while k < len(sl) and sl[k][0] < t + c - 1e-9:
-                    t = max(t, sl[k][1])
-                    k += 1
-                if best is None or t + c + (SPARE if q == "v" else 0) < best[0]:
-                    best = (t + c + (SPARE if q == "v" else 0), q, t, k, c)
-            q, t, k, c = best[1:]
-            slots[q].insert(k, (t, t + c))
-            start[i], end[i], on[i] = t, t + c, q
-        return max(end[i] + (0 if back else nodes[i]["lat"]) for i in range(n)), start, end, on
-
     def flush():
         n = len(nodes)
         for q in ORDER:
@@ -178,39 +158,29 @@ def rank_program(g, core, T, topo):
                 nodes[i]["alt"] = {q: nodes[i]["alt"][q]}
             for a, b in zip(row, row[1:]):
                 nodes[b]["order"].add(a)
+        eng.extend(min(x["alt"]) for x in nodes)
         preds = [[(p, False) for p in x["real"]] + [(p, True) for p in x["order"] - x["real"]] for x in nodes]
         succs = [[] for _ in range(n)]
         for i in range(n):
             for p, soft in preds[i]:
-                succs[p].append((i, soft))
+                succs[p].append(i)
         left = [len(p) for p in preds]
-        topo_order = [i for i in range(n) if not left[i]]
-        for i in topo_order:
-            for j, s in succs[i]:
+        seq = [i for i in range(n) if not left[i]]
+        start, end = [0.0] * n, [0.0] * n
+        for i in seq:
+            for p, soft in preds[i]:
+                lat, same = nodes[p]["lat"], eng[p] == eng[i]
+                start[i] = max(start[i], end[p] + (0.0 if soft and same else lat + (SAME if same and not lat else WAKE)))
+            end[i] = start[i] + nodes[i]["alt"][eng[i]][1]
+            for j in succs[i]:
                 left[j] -= 1
                 if not left[j]:
-                    topo_order.append(j)
-        assert len(topo_order) == n, [w for w in names if left[names[w][0]]][:8]
-        prio = [0.0] * n
-        for i in reversed(topo_order):
-            prio[i] = min(a[1] for a in nodes[i]["alt"].values()) + nodes[i]["lat"] + nodes[i].get("boost", 0.0) + max([prio[j] + WAKE for j, s in succs[i]] + [0.0])
-        if not DEALT:
-            best = run = deal(lambda i: (-prio[i], i), preds, None, False)
-            for _ in range(PASSES):
-                late = deal(lambda i: (-run[2][i], -i), succs, run[3], True)
-                run = deal(lambda i: (-late[2][i], i), preds, None, False)
-                if run[0] < best[0]:
-                    best = run
-            DEALT.append(best)
-        best = DEALT[0]
-        on = best[3]
-        eng.extend(on)
-        seq = sorted(range(n), key=lambda i: (best[1][i], best[2][i], i))
+                    seq.append(j)
+        assert len(seq) == n, [w for w in names if left[names[w][0]]][:8]
+        seq.sort(key=lambda i: (start[i], i))
         for i, x in enumerate(nodes):
-            x["q"] = on[i]
-            x["calls"] = x["alt"][on[i]][0]
             for b, p in x["banks"].items():
-                while p is not None and on[p] == on[i]:
+                while p is not None and eng[p] == eng[i]:
                     p = nodes[p]["banks"][b]
                 if p is not None:
                     x["real"].add(p)
@@ -225,8 +195,8 @@ def rank_program(g, core, T, topo):
                     if k.get(kk, 0) < nn:
                         k[kk] = nn
         for i in seq:
-            x = nodes[i]
-            q = x["q"]
+            x, q = nodes[i], eng[i]
+            calls = x["alt"][q][0]
             need = {}
             for p in x["real"]:
                 if at[p] is not None:
@@ -234,18 +204,20 @@ def rank_program(g, core, T, topo):
             for key in sorted(need, key=lambda key: -need[key]):
                 learn(q, key, need[key])
             for s, c in x["wait"]:
-                Q[q].wait_ge(T.sem[s], c)
+                if known[q].get(s, 0) < c:
+                    Q[q].wait_ge(T.sem[s], c)
+                    known[q][s] = c
             key = x["sem"] or "q" + q
             if key == "none":
-                x["calls"][0]()
+                calls[0]()
                 at[i] = None
                 continue
-            for k, call in enumerate(x["calls"]):
+            for k, call in enumerate(calls):
                 ins = call()
                 if key[0] != "q":
                     ins.then_inc(T.sem[key], 16)
                     total[key] = total.get(key, 0) + 16
-                elif k == len(x["calls"]) - 1:
+                elif k == len(calls) - 1:
                     ins.then_inc(T.sem[key], 1)
                     total[key] = total.get(key, 0) + 1
             at[i] = (key, total[key])
@@ -262,14 +234,15 @@ def rank_program(g, core, T, topo):
         return [x for x in xs if isinstance(x, dict)]
 
     def cy(n):
-        return 0.03 + CYC * max(64, n)
+        return 0.015 + CYC * max(64, n)
 
     def half(*vs):
         return cy(vs[0]["el"] * (0.5 if all(v["b2"] for v in vs) else 1))
 
     def ts(out, i0, s1, op0, s2=None, op1=None):
         if op1 is None:
-            node("v", [lambda: g.vector.tensor_scalar(out["ap"], i0["ap"], sc(s1), None, op0)], [i0] + scr(s1), [out], half(out, i0))
+            c = 0.05 + CYC * GAT * out["el"] if i0["ind"] else half(out, i0)
+            node("v", [lambda: g.vector.tensor_scalar(out["ap"], i0["ap"], sc(s1), None, op0)], [i0] + scr(s1), [out], c)
         else:
             node("v", [lambda: g.vector.tensor_scalar(out["ap"], i0["ap"], sc(s1), sc(s2), op0, op1)], [i0] + scr(s1, s2), [out], half(out, i0))
 
@@ -330,243 +303,269 @@ def rank_program(g, core, T, topo):
     def name(w, t, k=1):
         names.setdefault((w, t), []).extend(range(len(nodes) - k, len(nodes)))
 
-    def boost(us):
-        nodes[-1]["boost"] = us
+    def steps(w, t, *calls):
+        for k, c in enumerate(calls):
+            c()
+            name("%s%d" % (w, k), t)
 
     def slide(n, top, k):
         a = 144 * ("KB", "KXA", "KXB", "KW").index(n) + top - k
         return view("KK", a, a + 128)
 
+    def picked(c0, c1):
+        return view("JS", 17 * c0 + 16, 17 * c1, 17)
+
     def every16(n, l0=0, l1=NL):
         return view(n, l0 + 15, l1, 16)
 
-    def lanes(pn, w, src, out):
-        mm(view(pn, 0, NL), view("ID"), view("NM"), True, False)
-        for k, s in enumerate(src):
-            mm(view(pn, s[0], s[1]), view(w), s[2], False, k == len(src) - 1)
-        scan(view(out), view("DJ"), view(pn, 0, NL), 0.0, MUL, MAX)
-
-    parts = list(zip(PARTS, PARTS[1:], WIN))
-
-    def place(l):
-        l0, l1, w = [p for p in parts if p[0] <= l < p[1]][0]
-        return w + l - l0, w + 2 * CO + NK * (l - l0)
-
-    def own(n, l0, l1, off=0):
-        return view(n, place(l0)[0] + off, place(l0)[0] + off + l1 - l0)
+    def lanes(pn, w, src, out, t, first, l0=0, l1=NL, s=""):
+        n = l1 - l0
+        mm(view(pn, 0, n), view("ID"), view("NM", 0, n), True, False)
+        name(first + s, t)
+        mm(view(pn, 0, n), view(w), src, False, True)
+        scan(view(out, l0, l1), view("DJ", 0, n), view(pn, 0, n), 0.0, MUL, MAX)
+        name(out + s, t, 2)
 
     def cands(n, l0, l1, k=None):
-        a = place(l0)[1]
+        a = 2 * CO + NK * l0
         return view(n, a, a + NK * (l1 - l0)) if k is None else view(n, a + k, a + NK * (l1 - l0), NK)
-
-    def window(n, p, lst):
-        l0, l1, w = p
-        return view(n, w, w + 2 * CO + NK * (l1 - l0), 1, (lst, l0 // 16, l1 // 16))
-
-    def by_part(rec):
-        return [(l0, l1, own(rec, l0, l1)) for l0, l1, w in parts]
-
-    gio(view("PI", 0, 1), [[1, 1]], 0, 1)
-    gio(view("EHI"), [[1, NL]], 0)
-    nodes[-1]["order"].add(0)
-    dma("s", [(T.Y0[:, :], T.v0[:, :])], "dv", [], [view("Y0")])
-    dma("y", [(T.U[:, ga], T.w0[ga::2, :]) for ga in range(2)], "dw", [], [view("U", ap=0)], DU)
-    dma("y", [(T.EHI[0::16, :], T.e0[:, :]), (T.EHI[1::16, :], T.h0[:, :])], "de", [], [view("EHI")], DU - 0.2)
-    first = len(nodes) - 1
-    dma("y", [(T.X[:, :], T.x0[:, :])], "dx", [], [view("X")], DX)
-    nodes[-1]["order"].add(first)
-    dma("s", [(T.TH[:, :], T.th[:, :])], "dth", [], [view("TH")], 6.0)
-    gio(view("COLI"), [[1, NL]], 0)
-    gio(view("GRP"), [[1, 8], [0, 16]], 0)
-    gio(view("RI"), [[0, 16], [1, 16]], 0)
-    gio(view("H16"), [[1, 16], [0, 8]], 0)
-    gio(view("DM"), [[0, MAXC], [16384, 16]], 0)
-    nodes[-1]["order"].update(range(first + 3, len(nodes) - 1))
-    gio(view("V", 0, VG), [[0, VG]], -1)
-    nodes[-1]["order"].update(range(first + 3, len(nodes) - 2))
-    for a in range(VG, DEAD, 608):
-        ms(view("V", a, min(DEAD, a + 608)), -1.0)
-    ms(view("V", DEAD, VW), 0.0)
-    gio(view("VAL", 0, 272), [[256, 16], [1, 17]], 2 * CO - 1)
-    gio(view("DS", SENDS[0][1], 2 * CO), [[0, 2 * CO - SENDS[0][1]]], 0)
-    gio(view("CT", 0, 4), [[1, 4]], 1)
-    for t in range(NR):
-        gio(view("CD", t, t + 1), [[0, 1]], 2 ** (3 - t))
-    gio(view("RR"), [[0, 288]], -1)
-    gio(view("NEG"), [[0, NL]], -5)
-    gio(view("LOC", 0, LAB0), [[0, LAB0]], 0)
-    gio(view("LOC", DEAD, VW), [[0, 16]], 0)
-    ms(view("CM", ap=T.CM[:, :, 0], el=NL), 1.0)
 
     def cc(j):
         return view("CC", j, j + 1)
 
     def cx(j):
         return view("CX", j, j + 1)
-    (PQ, PG, NP16, PF, WM, WE_, WH_, NWE, NWH, WE2, LOW, KEEP, WWC, Q16, R0, R1, R2, R3, R4, R5, G2, G21, P8, KAP, B16, BK,
-     SGN, NR0, LO, BLO, P88) = range(31)
-    A = [view("CC", 40 + t, 41 + t) for t in range(NR)]
-    ts(view("PI", 2, 3), view("PI", 0, 1), 15, AND)
-    ts(view("PI", 4, 5), view("PI", 0, 1), 4, SHR)
-    ts(view("PI", 6, 7), view("PI", 0, 1), 7, AND)
-    tc(cc(PQ), view("PI", 2, 3))
-    tc(cc(PG), view("PI", 4, 5))
-    tc(cc(P8), view("PI", 6, 7))
-    act(cc(P88), cc(P8), IDENT, bias=8.0)
-    tc(cc(PF), view("PI", 0, 1))
-    ts(cc(WM), cc(PQ), 2.0, MUL, 1.0, ADD)
-    ts(view("WMK"), view("GRP"), cc(PG), EQL, cc(WM), MUL)
-    ts(view("ID"), view("COLI", 0, 128), cc(PF), EQL)
-    ts(view("IDM"), view("COLI", 0, 128), cc(PF), EQL, -4096.0, MUL)
-    act(cx(0), cc(PQ), SQUARE, bias=15.5, scale=-1.0)
-    act(cc(B16), cx(0), IDENT, bias=12.0 + 129 * 4096, scale=16.0)
-    act(cc(KAP), cx(0), SQUARE, bias=0.75)
-    act(cc(BK), cc(KAP), IDENT, bias=-0.375, scale=-8.0)
-    ms(A[0], MAGIC)
-    ts(view("B"), view("GRP"), cc(PG), EQL)
-    ts(cc(NP16), cc(PG), -16.0, MUL)
-    ts(view("DMT"), view("COLI", 0, 144), cc(NP16), ADD)
-    ms(view("KK"), 0.0)
 
     def spot(n, at, w):
-        ts(view("KK", 144 * n + at, 144 * n + 144, 16), view("COLI", 0, 9), cc(PG), EQL, w, MUL)
-    spot(0, 15, 32768.0)
-    for r, j in ((0, R0), (1, R1), (2, R2), (3, R3), (4, R4), (5, R5)):
-        ts(cc(j), cc(PQ), float(r), EQL)
-    ts(view("LI"), view("COLI"), cc(R3), MUL)
+        ts(view("KK", 144 * n + at, 144 * n + 128, 16), view("GRP", 0, 128, 16), cc(PG), EQL, w, MUL)
+
+    def stage(w):
+        name(w, -1, len(nodes) - staged[0])
+        staged[0] = len(nodes)
+    staged = [0]
+    (PF, PQ, PG, P8, R0, R1, R2, R3, R4, R5, NP16, WM, WE_, WH_, NWE, NWH, WE2, LOW, WWC, Q16, G2, G21, KAP, B16, BK,
+     SGN, NR0, LO, BLO, P88) = range(30)
+    A = [view("CC", 40 + t, 41 + t) for t in range(NR)]
+    gio(view("PI", 0, 1), [[1, 1]], 0, 1)
+    gio(view("EHI"), [[1, NL]], 0)
+    dma("s", [(T.Y0[:, :], T.v0[:, :])], "dv", [], [view("Y0")], 2.2)
+    dma("s", [(T.TH[:, :], T.th[:, :])], "dth", [], [view("TH")], 3.0)
+    dma("y", [(T.U[:, ga], T.w0[ga::2, :]) for ga in range(2)], "dw", [], [view("U", ap=0)], DU)
+    dma("y", [(T.EHI[0::16, :], T.e0[:, :]), (T.EHI[1::16, :], T.h0[:, :])], "de", [], [view("EHI")], DU - 0.6)
+    dma("y", [(T.X[:, :], T.x0[:, :])], "dx", [], [view("X")], DX)
+    gio(view("GRP"), [[1, 8], [0, 16]], 0)
+    gio(view("COLI"), [[1, NL]], 0)
+    gio(view("H16"), [[1, 16], [0, 8]], 0)
+    gio(view("RI"), [[0, 16], [1, 16]], 0)
+    gio(view("VAL", 0, 272), [[256, 16], [1, 17]], 2 * CO - 1)
+    gio(view("V", 0, VG), [[0, VG]], -1)
+    gio(view("DM"), [[0, MAXC], [16384, 16]], 0)
+    gio(view("DS", SENDS[0][1], 2 * CO), [[0, 2 * CO - SENDS[0][1]]], 0)
+    gio(view("CT", 0, 4), [[1, 4]], 1)
+    for t in range(NR):
+        gio(view("CD", t, t + 1), [[0, 1]], 2 ** (3 - t))
+    ms(view("KK"), 0.0)
+    ts(view("PI", 1, 2), view("PI", 0, 1), 15, AND)
+    ts(view("PI", 2, 3), view("PI", 0, 1), 4, SHR)
+    ts(view("PI", 3, 4), view("PI", 0, 1), 7, AND)
+    ms(A[0], MAGIC)
+    tc(view("CC", PF, P8 + 1), view("PI", 0, 4))
+    ms(view("ONE"), 1.0)
+    ts(cc(WM), cc(PQ), 2.0, MUL, 1.0, ADD)
+    ts(cc(LO), cc(PQ), 8.0, LT)
+    ms(view("ONE", 0, 144, 17), 0.0)
+    ms(view("V", DEAD, VW), 0.0)
+    ms(view("CM", ap=T.CM[:, :, 0], el=NL), 1.0)
+    act(cx(0), cc(PQ), SQUARE, bias=15.5, scale=-1.0)
+    act(cc(G2), cc(PG), COPY, scale=2.0)
+    act(cc(NP16), cc(PG), COPY, scale=-16.0)
+    act(cc(G21), cc(PG), IDENT, bias=1.0, scale=2.0)
+    act(cc(B16), cx(0), IDENT, bias=12.0 + 129 * 4096, scale=16.0)
+    act(cc(KAP), cx(0), SQUARE, bias=0.75)
+    act(cc(P88), cc(P8), IDENT, bias=8.0)
+    act(cc(Q16), cc(PQ), COPY, scale=16.0)
+    ts(view("CC", R0, R5 + 1), view("GRP", 0, 96, 16), cc(PQ), EQL)
+    ts(view("WMK"), view("GRP"), cc(PG), EQL, cc(WM), MUL)
+    ts(view("B"), view("GRP"), cc(PG), EQL)
     ts(cx(1), cc(PQ), 1.0, LE, cc(R3), ADD)
+    ts(cx(2), cc(PQ), 2.0, LE, cc(R5), ADD)
+    for k in range(2):
+        ts(view("BB", 128 * k, 128 * k + 128), view("GRP"), cc(PG), EQL, k + 1.0, MUL)
+    spot(0, 15, 32768.0)
+    act(cc(BK), cc(KAP), IDENT, bias=-0.375, scale=-8.0)
     act(cc(WE_), cc(R0), IDENT, bias=cc(R2), scale=16.0)
     act(cc(NWH), cc(R1), IDENT, bias=cc(R2), scale=-16.0)
+    act(cc(BLO), cc(LO), IDENT, bias=-16384.0, scale=32768.0 + LAB0)
     act(cc(NWE), cc(WE_), COPY, scale=-1.0)
     act(cc(WH_), cc(NWH), COPY, scale=-1.0)
     act(cc(WE2), cc(R5), IDENT, bias=cc(WE_), scale=float(LAB0))
     act(cc(LOW), cc(R5), IDENT, bias=cc(WE_), scale=-16384.0)
+    ts(view("IDM"), view("COLI", 0, 128), cc(PF), EQL, -4096.0, MUL)
+    ts(view("ID"), view("COLI", 0, 128), cc(PF), EQL)
+    ts(view("DMT"), view("COLI", 0, 128), cc(NP16), ADD)
+    act(view("ILF"), view("COLI", 0, 16), IDENT, bias=cc(PQ), scale=16.0)
+    act(view("WEB"), view("B"), COPY, scale=cc(WE2))
+    ts(view("M8B"), view("H16"), cc(G2), EQL)
+    ts(view("N8B"), view("H16"), cc(G21), EQL)
     for n, w7, w15 in ((1, WE_, WH_), (2, WH_, WE_)):
         spot(n, 7, cc(w7))
         spot(n, 15, cc(w15))
-    act(cc(G2), cc(PG), COPY, scale=2.0)
-    act(cc(G21), cc(PG), IDENT, bias=1.0, scale=2.0)
-    ts(cc(LO), cc(PQ), 8.0, LT)
-    act(cc(BLO), cc(LO), IDENT, bias=-16384.0, scale=32768.0 + LAB0)
-    ts(view("M8B"), view("H16"), cc(G2), EQL)
-    ts(view("N8B"), view("H16"), cc(G21), EQL)
+    for k in range(2):
+        ts(view("PMA", 128 * k, 128 * k + 128), view("DMT"), cc(P8), EQL, 4096.0 * (k + 1), MUL)
+        ts(view("PMB", 128 * k, 128 * k + 128), view("DMT"), cc(P88), EQL, 4096.0 * (k + 1), MUL)
+    ts(view("NM"), view("RI"), cc(PQ), NE, -2.0 ** 21, MUL)
+    ts(view("DJ"), view("RI"), 0.0, GT)
+    for a in range(VG, DEAD, 608):
+        ms(view("V", a, min(DEAD, a + 608)), -1.0)
+    stage("k0")
     for k, (n, lo, hi) in enumerate((("WA", NWE, NWH), ("WB", NWH, NWE), ("WZ", LOW, WE2))):
-        c, d, p = view("C%d" % (2 * k + 1)), view("C%d" % (2 * k + 2)), view("P%d" % (2 + k % 2), 0, 128)
+        c, d, p = view("C%d" % (2 * k + 1)), view("C%d" % (2 * k + 2)), view("P%d" % (2 + k), 0, 128)
         act(c, view("M8B"), COPY, scale=cc(lo))
         act(d, view("N8B"), COPY, scale=cc(hi))
         mms(p, [(view("ID"), c), (view("ID"), d)])
+        stage("k%d" % (1 + k))
         act(view(n), p)
-    ts(view("PM8"), view("DMT", 0, 128), cc(P8), EQL, 4096.0, MUL)
-    copy(view("PMA", 0, 128), view("PM8"))
-    ts(view("PMB", 0, 128), view("DMT", 0, 128), cc(P88), EQL, 4096.0, MUL)
-    copy(view("BB", 0, 128), view("B"))
-    for n in ("PMA", "PMB", "BB"):
-        affine(view(n, 128, 256), view(n, 0, 128), 2.0, 0.0)
-    act(view("WEB"), view("B"), COPY, scale=cc(WE2))
-    act(view("W1B"), view("B"), COPY, scale=cc(R1))
-    ts(view("NM"), view("RI"), cc(PQ), NE, -2.0 ** 21, MUL)
-    ts(view("DJ"), view("RI"), 0.0, GT)
+        stage("k4")
+    act(view("VAL", 0, 272), view("VAL", 0, 272), IDENT, bias=cc(Q16))
+    stage("k5")
+    act(view("VAL", 0, 272, 17), view("ILF"))
+    stage("k6")
+    ts(view("SR"), view("EHI"), cx(1), MUL, cc(R5), ADD)
+    stage("SR")
     act(view("IDN"), view("ID"), COPY, scale=-1.0)
     act(view("ID5"), view("ID"), COPY, scale=-5.0 * 32768)
-    ms(view("ONE"), 1.0)
-    ms(view("ONE", 0, 144, 17), 0.0)
-    act(view("WM16"), view("WMK"), COPY, scale=16.0)
-    act(cc(Q16), cc(PQ), COPY, scale=16.0)
-    act(view("BSF"), view("COLI", 0, 16), IDENT, bias=cc(Q16), scale=256.0)
-    act(view("ILF"), view("COLI", 0, 16), IDENT, bias=cc(PQ), scale=16.0)
-    act(view("TRF"), view("ILF"), IDENT, bias=float(TRASH))
-    act(view("VAL", 0, 272), view("VAL", 0, 272), IDENT, bias=cc(Q16))
-    for l0, l1, w in parts:
-        act(view("VAL", 17 * l0 // 16, 17 * l1 // 16, 17), view("ILF", l0 // 16, l1 // 16), IDENT, bias=float(-l0))
-    ts(cx(2), cc(PQ), 2.0, LE, cc(R5), ADD)
+    stage("k7")
+    act(view("LI"), view("COLI"), COPY, scale=cc(R3))
     act(view("IDK"), view("ID"), COPY, scale=cx(2))
-    ts(view("CT", 4, 8), view("CT", 0, 4), cc(R4), MUL)
-    ts(view("CD", 4, 8), view("CD", 0, 4), cc(R2), MUL)
-    tt(view("CT", 8, 12), view("CT", 4, 8), view("CD", 4, 8), ADD)
+    act(view("W1B"), view("B"), COPY, scale=cc(R1))
     act(view("WBG"), view("B"), COPY, scale=-2.0 ** 18)
-    ts(view("C7"), view("DMT", 0, 128), cc(PQ), GT, -2.0 ** 18, MUL)
-    tt(view("C7"), view("C7"), view("B"), MUL)
-    name("Q0", 0, 2)
-    act(view("C8"), view("ID"), COPY, scale=65536.0)
-    tt(view("WDG"), view("C7"), view("C8"), ADD)
-    name("Q2", 0)
-    act(cc(WWC), cc(R4), IDENT, bias=cc(R3), scale=256.0)
-    spot(3, 15, cc(WWC))
+    act(view("WM16"), view("WMK"), COPY, scale=16.0)
     act(view("NTH", 0, 4), view("TH"), IDENT, bias=0.5, scale=-1.0)
+    act(view("TRF"), view("ILF"), IDENT, bias=float(TRASH))
+    act(view("BSF"), view("COLI", 0, 16), IDENT, bias=cc(Q16), scale=256.0)
+    for l0, l1 in spans(ECH):
+        act(view("BSE", l0 // 16, l1 // 16), view("COLI", 0, (l1 - l0) // 16), IDENT, bias=cc(Q16), scale=256.0)
     act(cc(SGN), cc(R1), IDENT, bias=cc(R0), scale=-1.0)
     act(cc(NR0), cc(R0), COPY, scale=-1.0)
-    ts(view("SR"), view("EHI"), cx(1), MUL, cc(R5), ADD)
+    stage("k8")
+    act(cc(WWC), cc(R4), IDENT, bias=cc(R3), scale=256.0)
+    stage("k9")
+    spot(3, 15, cc(WWC))
+    ts(view("CT", 4, 8), view("CT", 0, 4), cc(R4), MUL)
+    ts(view("CD", 4, 8), view("CD", 0, 4), cc(R2), MUL)
+    stage("kb")
+    tt(view("CT", 8, 12), view("CT", 4, 8), view("CD", 4, 8), ADD)
+    stage("kc")
+    gio(view("RR"), [[0, 288]], -1)
+    gio(view("NEG"), [[0, NL]], -5)
+    gio(view("LOC", 0, LAB0), [[0, LAB0]], 0)
+    gio(view("LOC", DEAD, VW), [[0, 16]], 0)
+    stage("kd")
 
-    def cells(y, a, t):
+    def lead_weights():
+        for o, a, op, fill in (("C7", "WBG", GT, 0.0), ("WDG", "C7", NE, 65536.0)):
+            node("g", [lambda o=o, a=a, op=op, fill=fill: g.affine_select(view(o)["ap"], view(a)["ap"], [[1, 128]], op, fill, 0, -1)],
+                 [view(a)], [view(o)], 0.17 + 2 * CYC * 128)
+
+    def cells(y, a, t, s=""):
         p = view("P1", 0, NL)
         mm(view("P0", 0, NL), view("WMK"), y)
-        name("mark", t)
+        name("mark" + s, t)
         mm(p, view("WMK"), y, True, False)
-        name("mark2", t)
+        name("mark2" + s, t)
         affine(view("MM"), view("P0", 0, NL), 1.0 / 4096, 128.5 + 1.0 / 8192)
-        name("MM", t)
+        name("MM" + s, t)
         mm(p, view("IDM"), view("MM"), False, True)
-        name("mod", t)
+        name("mod" + s, t)
         act(view("SQ"), p, SQUARE, bias=cc(B16))
-        name("SQ", t)
+        name("SQ" + s, t)
         affine(view("X1"), view("SQ"), 1.0 / 32, cc(BK))
-        name("FL", t)
+        name("FL" + s, t)
         ts(view("A1"), view("X1"), a, ADD)
-        name("A1", t)
+        name("A1" + s, t)
         ts(view("A2"), view("A1"), 4095, AND)
-        name("A2", t)
+        name("A2" + s, t)
         tc(view("LA"), view("A2"))
-        name("LA", t)
+        name("LA" + s, t)
 
-    def current(rec, t):
-        r = own(rec, 0, NL)
-        if t > 0:
-            mm(view("P5", 0, NL), view("WEB"), r)
+    def current(rec, t, s=""):
+        if t >= 0:
+            mm(view("P5", 0, NL), view("WEB"), view(rec, 0, NL))
             tc(view("E16"), view("P5", 0, NL))
-            name("E16", t - 1, 2)
-        lanes("P4", "WEB", [(0, NL, r)], "CUS")
-        name("CUS", t - 1, 3)
-        mms(view("P7", 0, NL), [(view("IDK"), r), (view("ID"), view("LI"))])
-        affine(own(rec, 0, NL, CO), view("P7", 0, NL), 1.0, view("CT", 8 + t, 9 + t))
-        name("kid", t - 1, 2)
+            name("E16", t, 2)
+        lanes("P4", "WEB", view(rec, 0, NL), "CUS", t, "CUS")
+        if s:
+            names[("CUS" + s, t)] = names[("CUS", t)][:2]
+        mms(view("P7", 0, NL), [(view("IDK"), view(rec, 0, NL)), (view("ID"), view("LI"))])
+        affine(view(rec, CO, CO + NL), view("P7", 0, NL), 1.0, view("CT", 9 + t, 10 + t))
+        name("kid" + s, t, 2)
 
-    cells(view("Y0"), A[0], -9)
-    for w in ("A1", "A2", "LA"):
-        names[(w + "'", -1)] = names[(w, -9)]
+    def second_order():
+        tc(view("EL", 0, 16), every16("CUS"))
+        ts(view("E0L"), every16("CUS"), float(-LAB0), ADD, 0.0625, MUL)
+        tc(view("TS", 0, NL, 1, ("E0L", 0, 16)), view("SR"))
+        name("H0", 0, 3)
+        k = len(nodes)
+        lanes("P6", "W1B", view("TS"), "TAS", -9, "")
+        tc(view("TAU"), every16("TAS"))
+        name("H1", 0, len(nodes) - k)
+        tc(view("TS", 0, NL, 1, ("TAU", 0, 16)), view("COLI"))
+        name("H2", 0)
+        k = len(nodes)
+        lanes("P6", "W1B", view("TS"), "TAS", -9, "")
+        ts(view("SIG"), every16("TAS"), 16.0, MUL, LAB0 + 15.0, ADD)
+        name("H3", 0, len(nodes) - k)
+
+    cells(view("Y0"), A[0], -1, "'")
     node("v", [lambda ip=ip: g.vector.transpose(T.UT[:, ip::8], T.U[:, :, ip, :]) for ip in range(8)], [view("U", ap=0)], [view("UT")], 8 * cy(32))
+    name("TR", -1)
     tc(view("WL"), view("UT"))
+    name("WL", -1)
     for c, (a, b) in enumerate(spans(TCH)):
         copy(view("RT", NK * a, NK * b), view("SR", 0, NL, 1, ("WL", a, b)))
         name("T%d" % c, -1)
-    copy(own("RS0", 0, NL), view("SR"))
-    current("RS0", 0)
+    copy(view("RS0", 0, NL), view("SR"))
+    name("own", -1)
+    current("RS0", -1, "'")
     tc(view("VO"), every16("CUS"))
     tc(view("V", 0, VW, 1, ("VO", 0, 16)), view("Y0"))
     name("VS", 0, 2)
-    tc(view("EL", 0, 16), every16("CUS"))
 
-    def second_order():
-        ts(view("E0L"), view("EL", 0, 16), float(-LAB0), ADD, 0.0625, MUL)
-        tc(view("TS", 0, NL, 1, ("E0L", 0, 16)), view("SR"))
-        name("Q1", 0, 2)
-        lanes("P6", "W1B", [(0, NL, view("TS"))], "TAS")
-        tc(view("TAU"), every16("TAS"))
-        name("Q3", 0, 4)
-
-    y = view("Y0")
+    msk = topo.mask(core, T.cores[(rank + 1) % N])
+    neng = len(topo.engines(core, T.cores[(rank + 1) % N]))
+    y = "Y0"
     for t in range(NR):
         rs, rn = "RS%d" % (t % 2), "RS%d" % ((t + 1) % 2)
         land = "LAND%d" % t
         O2 = view("O2A", 16 * t, 16 * t + 16)
         SP = view("SPA", 16 * t, 16 * t + 16)
         more = t + 1 < NR
-        ynew = view(land, 0, NL)
-        msk = topo.mask(core, T.cores[(rank + 1) % N])
-        neng = len(topo.engines(core, T.cores[(rank + 1) % N]))
-        JL = view("JS", 16, 272, 17)
-        mm(view("P7", 0, NL), view("ID"), view("NM"), True, False)
+        takes = (0, NL) if more else SENDS[t]
 
+        def slot(d, l0, l1):
+            p0, p1 = [p for p in spans(takes) if p[0] <= l0 < p[1]][0]
+            return view(land, N * p0 + d * (p1 - p0) + l0 - p0, N * p0 + d * (p1 - p0) + l1 - p0)
+
+        def choose(l0, l1, pn, s):
+            c0, c1 = l0 // 16, l1 // 16
+            lanes(pn, "WM16", slot(0, l0, l1), "MLS", t, "nmA", l0, l1, s)
+            steps("Z" + s, t, lambda: tc(view("I1", c0, c1), every16("MLS", l0, l1)),
+                  lambda: ts(view("I2", c0, c1), view("I1", c0, c1), NL // (l1 - l0) - 1, SHR, 3 * (l1 - l0), AND),
+                  lambda: tt(view("F1", c0, c1), view("I2", c0, c1), view("ILF", 0, c1 - c0), ADD), lambda: tc(view("ZL", c0, c1), view("F1", c0, c1)))
+
+        def take(l0, l1, pn, s):
+            c0, c1 = l0 // 16, l1 // 16
+            copy(view("ZZ", l0, l1), view(land, N * l0, N * l1, 1, ("ZL", c0, c1)),
+                 wait=[("ar%d_%d" % (t, ip), (N - 1) * neng) for ip, p in enumerate(spans(SENDS[t])) if l0 <= p[0] < l1])
+            name("ZZ" + s, t)
+            lanes(pn, "WM16", view("ZZ", l0, l1), "MZS", t, "nmB", l0, l1, s)
+            steps("W" + s, t, lambda: tc(view("I3", c0, c1), every16("MZS", l0, l1)), lambda: ts(view("I4", c0, c1), view("I3", c0, c1), 4, SHR, 15, AND),
+                  lambda: tt(view("F2", c0, c1), view("I4", c0, c1), view("BSF" if more else "BSE", c0, c1), ADD),
+                  lambda: tc(view("XL", c0, c1), view("F2", c0, c1)))
+        JL = picked(0, 16)
+        mm(view("P7", 0, NL), view("ID"), view("NM"), True, False)
         name("nm", t)
+
         for c, (l0, l1) in enumerate(spans(RCH)):
             copy(cands(rs, l0, l1), view("RT", 0, NCELL, 1, ("LA", l0, l1)))
             name("R%d" % c, t)
@@ -575,8 +574,8 @@ def rank_program(g, core, T, topo):
             name("X%d" % c, t)
         for c, (l0, l1) in enumerate(spans(LCH)):
             n = l1 - l0
-            pa, pb = view("P%d" % (c % 2), 0, n), view("P%d" % (2 + c % 2), 0, n)
-            cur = own(rs, l0, l1)
+            pa, pb, pz = view("P%d" % (c % 2), 0, n), view("P%d" % (2 + c % 2), 0, n), view("P6", 0, n)
+            cur = view(rs, l0, l1)
             mms(pa, [(view("WA"), cur)] + [(slide("KXA", 7, k), cands(rs, l0, l1, k)) for k in range(8)])
             name("a%d" % c, t)
             mms(pb, [(view("WB"), cur)] + [(slide("KXB", 7, k), cands(rs, l0, l1, 8 + k)) for k in range(8)])
@@ -589,7 +588,6 @@ def rank_program(g, core, T, topo):
             name("Sb%d" % c, t)
             tt(view("LM", l0, l1), view("LF", l0, l1), pb, MAX)
             name("LM%d" % c, t)
-            pz = view("P6", 0, n)
             mms(pz, [(view("WZ"), cur), (wa, view("S1", l0, l1)), (wb, view("S2", l0, l1))])
             name("z%d" % c, t)
             tt(view("LF", l0, l1), view("LM", l0, l1), pz, ADD)
@@ -609,31 +607,32 @@ def rank_program(g, core, T, topo):
                 ts(cm, cands("DS", l0, l1), 0.0, GT, 10.5 / 16, SUB)
             name("C%d" % c, t)
         for c, (l0, l1) in enumerate(spans(CCH)):
-            n = l1 - l0
-            pc = view("P%d" % (4 + c % 2), 0, 17 * n // 16)
+            c0, c1 = l0 // 16, l1 // 16
+            pc = view("P%d" % (4 + c % 2), 0, 17 * (c1 - c0))
             rows = [(slide("KB", 15, q), view("CM", 17 * l0, 17 * l1, ap=T.CM[:, l0 + q:l1:16, :])) for q in range(16)]
-            mms(pc, [(view("ID5"), view("ONE", 0, 17 * n // 16))] * (c in CA) + rows[:8], True, False)
+            mms(pc, [(view("ID5"), view("ONE", 0, 17 * (c1 - c0)))] * (c in CA) + rows[:8], True, False)
             name("n%d" % c, t)
             mms(pc, rows[8:], False, True)
             name("m%d" % c, t)
-            scan(view("JS", 17 * l0 // 16, 17 * l1 // 16), pc, view("VAL", 17 * l0 // 16, 17 * l1 // 16), 0.0, MAX, MIN)
+            scan(view("JS", 17 * c0, 17 * c1), pc, view("VAL", 17 * c0, 17 * c1), 0.0, MAX, MIN)
             name("J%d" % c, t)
             for m0, m1 in spans(sorted(set(SENDS[t] + MCH[-2:]))):
                 most = view("MX", NK * m0 + 15, NK * m1, 16)
-                if m1 == NL == l1:
-                    tt(own("DS", m0, m1), most, view(y["n"], m0, m1), SUB)
-                    name("D", t)
+                if m1 == NL:
+                    if l0 < m0 <= l1:
+                        tt(view("DS", m0, m1), most, view(y, m0, m1), SUB)
+                        name("D", t)
                 elif l0 < m1 <= l1:
                     pm = view("P6" if m1 == MCH[-2] else "P%d" % (4 + c % 2), 256, 256 + m1 - m0)
-                    mms(pm, [(view("IDN"), view(y["n"], m0, m1)), (view("ID"), most)])
-                    copy(own("DS", m0, m1), pm)
+                    mms(pm, [(view("IDN"), view(y, m0, m1)), (view("ID"), most)])
+                    copy(view("DS", m0, m1), pm)
                     name("D%d" % m1, t, 2)
 
             if l1 in LEADS:
                 k = LEADS.index(l1) - 1
                 p0 = LEADS[k]
-                c0, c1 = p0 // 16, l1 // 16
-                ts(view("ML", c0, c1), view("JS", 17 * c0 + 16, 17 * c1, 17), float(2 * CO), LT)
+                c0 = p0 // 16
+                ts(view("ML", c0, c1), picked(c0, c1), float(2 * CO), LT)
                 name("ML%d" % k, t)
                 if t > 0:
                     tt(view("CUM", c0, c1), every16("CUS", p0, l1), view("ML", c0, c1), MUL)
@@ -647,109 +646,109 @@ def rank_program(g, core, T, topo):
                             name("Q%d" % (b // 4), t)
                     mm(view("P7", p0, l1), view("WDG"), view("EQ", 256 * c0, 256 * c1, ap=T.EQ[:, c0:c1, 0:16]), False, False)
                     name("Q%d" % (b // 4), t)
+
+            ych = sorted(set(SENDS[t] + YCH))
+            if l1 in ych:
+                p0 = ych[ych.index(l1) - 1]
+                tc(view("JLU", p0 // 16, c1), picked(p0 // 16, c1))
+                act(slot(0, p0, l1), view("DS", 0, 2 * CO + NK * l1, 1, ("JLU", p0 // 16, c1)), ABS)
+                name("Y" if l1 == NL else "Y%d" % l1, t, 2)
             if l1 not in SENDS[t]:
                 continue
-
             ip = SENDS[t].index(l1) - 1
             p0 = SENDS[t][ip]
-            c0, c1 = p0 // 16, l1 // 16
-            jl = view("JS", 17 * c0 + 16, 17 * c1, 17)
-            tc(view("JLU", c0, c1), jl)
-            act(view(land, p0, l1), view("DS", 0, 2 * CO + NK * l1, 1, ("JLU", c0, c1)), ABS)
-            name("Y" if l1 == NL else "Y%d" % l1, t, 2)
             dsts, ids = [], []
             for j in range(1, N):
                 r = (rank + j) % N
                 d = (rank - r) % N
                 a = topo.addr(T.cores[r])
                 ids.append(DstId(rid=a[0], pnc=a[1]))
-                dsts.append(T[land][:, d * NL + p0:d * NL + l1])
+                dsts.append(slot(d, p0, l1)["ap"])
 
-            def send(ids=ids, dsts=dsts, key="%d_%d" % (t, ip), src=T[land][:, p0:l1]):
+            def send(ids=ids, dsts=dsts, key="%d_%d" % (t, ip), src=slot(0, p0, l1)["ap"]):
                 return g.remote_dma_fused([RemoteDMATransfer(dst_ids=ids, dma_engine_mask=msk, remote_sem=T.sem["ar" + key],
                                                              src=src, dsts=dsts)], local_sem=T.sem["lo" + key])
-            node("g", [send], [view(land, p0, l1)], [view(land, d * NL + p0, d * NL + l1) for d in range(1, N)], 0.1, "none",
-                 LAT + (3.0 if t + ip == 0 else 0.0))
+            node("g", [send], [slot(0, p0, l1)], [slot(d, p0, l1) for d in range(1, N)], 0.1, "none", LAT + (3.6 if t + ip == 0 else 0.0))
+            if l1 in takes[1:-1]:
+                choose(p0, l1, "P0", "a")
+                take(p0, l1, "P2", "a")
 
-        wc = sign(view("WC"), ynew, view("TH", t, t + 1), view("NTH", t, t + 1), "BB")
-        mm(view("P7", 0, NL), wc, view("WC"), False, True)
-        name("WC", t, 2)
+        for l0, l1 in spans(takes):
+            wc = sign(view("WC", l0, l1), slot(0, l0, l1), view("TH", t, t + 1), view("NTH", t, t + 1), "BB")
+            mm(view("P7", l0, l1), wc, view("WC", l0, l1), False, l1 == NL)
+            name("WC", t, 2)
         scan(view("LV"), view("DJ"), view("P7", 0, NL), 0.0, MUL, MAX)
         name("LV", t)
         lv = every16("LV")
         if t == 0:
+            lead_weights()
             second_order()
             ts(view("ML6"), JL, float(2 * CO), LT, 65536.0, MUL)
+            name("ML1", t)
             tt(view("LV0"), view("ML6"), lv, ADD)
-            name("LV", t, 2)
+            name("LV", t)
             lv = view("LV0")
-
-        def steps(w, *calls):
-            for k, c in enumerate(calls):
-                c()
-                name("%s%d" % (w, k), t)
-        lanes("P4", "WM16", [(0, NL, ynew)], "MLS")
-        name("MLS", t, 2)
-        steps("Z", lambda: tc(view("I1"), every16("MLS")), lambda: ts(view("I2"), view("I1"), 768, AND),
-              lambda: tt(view("F1"), view("I2"), view("ILF"), ADD), lambda: tc(view("ZL"), view("F1")))
+        choose(takes[-2], NL, "P4", "")
         if more:
             mm(view("P5", 0, 16), view("B"), view("ML"))
             act(view("AD"), view("P5", 0, 16), IDENT, bias=16.0 + MAGIC / 16, scale=-1.0, acc=A[t + 1])
             name("AD", t, 2)
-            cells(ynew, A[t + 1], t)
-        steps("N", lambda: ts(SP, lv, 65538.0, GE, float(CO), MUL), lambda: tt(view("JL2"), JL, SP, ADD), lambda: tc(view("JL2U"), view("JL2")),
-              lambda: copy(own(rn, 0, NL), window(rs, parts[0], "JL2U")))
+            cells(slot(0, 0, NL), A[t + 1], t)
+        steps("N", t, lambda: ts(SP, lv, 65538.0, GE, float(CO), MUL), lambda: tt(view("JL2"), JL, SP, ADD), lambda: tc(view("JL2U"), view("JL2")),
+              lambda: copy(view(rn, 0, NL), view(rs, 0, WW, 1, ("JL2U", 0, 16))))
 
-        copy(view("ZZ"), view(land, 0, N * NL, 1, ("ZL", 0, 16)), wait=[("ar%d_%d" % (t, ip), (N - 1) * neng) for ip in range(len(SENDS[t]) - 1)])
-        name("ZZ", t)
-        lanes("P5", "WM16", [(0, NL, view("ZZ"))], "MZS")
-        name("MZS", t, 2)
-        steps("W", lambda: tc(view("I3"), every16("MZS")), lambda: ts(view("I4"), view("I3"), 4, SHR, 15, AND),
-              lambda: tt(view("F2"), view("I4"), view("BSF"), ADD), lambda: tc(view("XL"), view("F2")))
-        tc(view("RT", 0, NCELL, 1, ("XL", 0, 16)), own(rn, 0, NL))
-        name("RT", t)
-        tc(view("X", 0, NCELL, 1, ("XL", 0, 16)), view("ZZ"))
-        name("X", t)
-        steps("O", lambda: ts(view("O1"), lv, 65538.0, GE, float(2 ** (3 - t)), MUL), lambda: tt(O2, view("O1"), every16("CUS"), ADD),
-              lambda: tt(view("M1"), lv, O2, MIN), lambda: tt(view("M2"), view("M1"), view("TRF"), MAX), lambda: tc(view("VO"), view("M2")),
-              lambda: tc(view("V", 0, VW, 1, ("VO", 0, 16)), ynew))
+        take(takes[-2], NL, "P5", "")
         if more:
-            current(rn, t + 1)
+            tc(view("RT", 0, NCELL, 1, ("XL", 0, 16)), view(rn, 0, NL))
+            name("RT", t)
+            tc(view("X", 0, NCELL, 1, ("XL", 0, 16)), view("ZZ"))
+            name("X", t)
+        steps("O", t, lambda: ts(view("O1"), lv, 65538.0, GE, float(2 ** (3 - t)), MUL), lambda: tt(O2, view("O1"), every16("CUS"), ADD),
+              lambda: tt(view("M1"), lv, O2, MIN), lambda: tt(view("M2"), view("M1"), view("TRF"), MAX), lambda: tc(view("VO"), view("M2")))
+        for l0, l1 in spans(takes):
+            tc(view("V", 0, VW, 1, ("VO", l0 // 16, l1 // 16)), slot(0, l0, l1))
+            name("O5", t)
+        if more:
+            current(rn, t)
         if t == NR - 2:
             act(view("AL", 0, NCELL, 2), view("V", LAB0, DEAD, 2), SIGN, bias=1.0)
             name("AL", t)
-        y = ynew
+        y = land
 
-    dma("y", [(T.yx[:, :], T.X[:, :])], "oyx", [view("X")], [], 5.5)
-    ts(view("EA"), view("O2A"), float(-DEAD), ADD, 1.0 / CO, MUL)
-    tt(view("EB"), view("EA"), view("SPA"), MUL)
-    ts(view("EL", 16, 80), view("EB"), float(DEAD), ADD)
-    tc(view("ELU"), view("EL"))
-    tc(view("ELI"), view("EL"))
-    ts(view("KI"), view("ELI"), 4, SHR)
-    tc(view("KLU"), view("KI"))
+    for c, (l0, l1) in enumerate(spans(ECH)):
+        tc(view("RT", NK * l0, NK * l1, 1, ("XL", l0 // 16, l1 // 16)), view(rn, l0, l1))
+        name("rt%d" % c, t)
+        mms(view("P0", 0, NL), [(slide("KW", 15, q), view("RT", 256 * q, 256 * q + 256)) for q in range(l0 // 16, l1 // 16)], l0 == 0, l1 == NL)
+        tc(view("X", NK * l0, NK * l1, 1, ("XL", l0 // 16, l1 // 16)), view("ZZ", l0, l1))
+        name("x%d" % c, t)
+        dma("y", [(T.yx[:, NK * l0:NK * l1], T.X[:, NK * l0:NK * l1])], "oyx%d" % c, [view("X", NK * l0, NK * l1)], [], 3.0)
+    act(view("GW"), view("P0", 0, NL))
+    name("GW", t)
+    dma("y", [(T.yw[:, :], T.GW[:, :])], "oyw", [view("GW")], [], 2.6)
+    steps("E", t, lambda: ts(view("EA"), view("O2A"), float(-DEAD), ADD, 1.0 / CO, MUL), lambda: tt(view("EB"), view("EA"), view("SPA"), MUL),
+          lambda: ts(view("EL", 16, 80), view("EB"), float(DEAD), ADD), lambda: tc(view("ELU"), view("EL")),
+          lambda: tc(view("ELI"), view("EL")), lambda: ts(view("KI"), view("ELI"), 4, SHR), lambda: tc(view("KLU"), view("KI")))
     act(view("GV"), view("V", 0, VW, 1, ("ELU", 0, 80)))
-    dma("y", [(T.yv[:, :], T.GV[:, :])], "oyv", [view("GV")], [])
-    dw = NK * MAXC
-    for a in range(0, NCELL, dw):
-        b = min(NCELL, a + dw)
+    name("GV", t)
+    dma("y", [(T.yv[:, :], T.GV[:, :])], "oyv", [view("GV")], [], 2.8)
+    for c, a in enumerate(range(0, NCELL, LW)):
+        b = a + LW
         either(lambda: ts(view("AL", a + 1, b, 2), view("V", LAB0 + a + 1, LAB0 + b, 2), 0.0, GE),
                lambda: act(view("AL", a + 1, b, 2), view("V", LAB0 + a + 1, LAB0 + b, 2), SIGN, bias=1.0))
+        name("al%d" % c, t)
         scan(view("LOC", LAB0 + a, LAB0 + b), view("DM", 0, b - a), view("AL", a, b), 0.0, MIN, ADD)
-    act(view("LG"), view("LOC", 0, VW, 1, ("ELU", 0, 80)), COPY, scale=cc(SGN))
-    mms(view("P0", 0, NL), [(slide("KW", 15, q), view("RT", 256 * q, 256 * q + 256)) for q in range(16)])
-    act(view("GW"), view("P0", 0, NL))
-    dma("y", [(T.yw[:, :], T.GW[:, :])], "oyw", [view("GW")], [])
-    sizes = view("LOC", LAB0 + 15, DEAD, 16)
-    ts(view("SZB"), sizes, cc(R1), MUL)
-    act(view("SZA"), view("LOC", LAB0 - 1, DEAD - 16, 16), COPY, scale=cc(R0))
-    tc(view("SZH", 0, NL, 1, ("TAU", 0, 16)), view("SZB"))
-    scan(view("PHB"), view("SZH"), view("SZH"), 0.0, ADD, MAX)
-    scan(view("REA"), view("SZA"), view("NEG"), cc(NR0), ADD, MAX)
+        name("L%d" % c, t)
     k0 = LAB0 // 16
-    tt(view("RR", k0, k0 + NL), view("PHB", 0, NL, 1, ("TAU", 0, 16)), view("REA"), ADD)
-    tt(view("GE"), view("RR", 0, 288, 1, ("KLU", 0, 80)), view("LG"), ADD)
-    dma("y", [(T.ye[:, :], T.GE[0::16, :]), (T.yh[:, :], T.GE[1::16, :])], "oye", [view("GE")], [])
+    by_h = view("LOC", 0, VW, 1, ("SIG", 0, 16))
+    steps("G", t, lambda: either(lambda: ts(view("SZH"), by_h, cc(R1), MUL), lambda: act(view("SZH"), by_h, COPY, scale=cc(R1))),
+          lambda: affine(view("SZA"), view("LOC", LAB0 - 1, DEAD - 16, 16), cc(R0), 0.0),
+          lambda: act(view("LG", NL, NS), view("LOC", 0, VW, 1, ("ELU", 16, 80)), COPY, scale=cc(SGN)),
+          lambda: scan(view("REA"), view("SZA"), view("NEG"), cc(NR0), ADD, MAX),
+          lambda: scan(view("PHB"), view("SZH"), view("SZH"), 0.0, ADD, MAX),
+          lambda: tt(view("RR", k0, k0 + NL), view("PHB", 0, NL, 1, ("TAU", 0, 16)), view("REA"), ADD),
+          lambda: act(view("GE", 0, NL), view("RR", 0, 288, 1, ("KLU", 0, 16)), IDENT, bias=cc(SGN)),
+          lambda: tt(view("GE", NL, NS), view("RR", 0, 288, 1, ("KLU", 16, 80)), view("LG", NL, NS), ADD))
+    dma("y", [(T.ye[:, :], T.GE[0::16, :]), (T.yh[:, :], T.GE[1::16, :])], "oye", [view("GE")], [], 2.2)
 
     flush()
     for t in range(NR):

import numpy as np
from concourse.bass import DstId, RemoteDMATransfer
from concourse.mybir import dt, AluOpType, AxisListType, ActivationFunctionType
import comms_topo

NL, NK, NCELL, NR, NS = 256, 16, 4096, 4, 1280
RCH = (0, 32, 64, 128, 192, 256)
LCH = (0, 64, 128, 192, 256)
XCH = (0, 64, 128, 192, 224, 256)
VCH = (0, 64, 128, 192, 224, 256)
CCH = (0, 64, 128, 192, 256)
MCH = (0, 64, 128, 192, 256)
YCH = (0, 192, 256)
LEADS = (0, 192, 256)
SENDS = ((0, 128, 256), (0, 256), (0, 256), (0, 128, 256))
TCH = (0, 64, 112, 184, 256)
ECH = (0, 64, 128, 192, 256)
CA = (1, 2)
CO = 256
WW = 2 * CO + NCELL
TRASH = 16
LAB0 = 272
DEAD = LAB0 + NCELL
VW = DEAD + 16
VG = 3200
LW = 1024
MAGIC = 12582912.0
CYC, PEC, GAT, SCA, WAKE, SAME, LAT, DU, DX = 0.00083, 0.00083, 1.5, 3.8, 0.12, 0.19, 3.7, 4.1, 8.4
ORDER = {
    "v": "-k0 -TR -SR -WL -A1' -T1 -own -A2' -T0 -LA' -E16 -RT -CUS R1 VS -X Sa0 X0 LM0 LP0 M0 LB0 LM1 V0 LP1 -kb LM2 LB1 C0 LP2 V1 "
         "LB2 M1 V2 LM3 M2 LP3 -kc LB3 J0 J1 V3 Y128 V4 C3 C4 M3 J2 H0 ML0 D MLSa CU0 Y192 Za0 Q0 J3 Y H1 Q1 Q2 ML1 Za1 Za2 CU1 Q3 Za3 H2 "
         "LV MZSa MLS O0 N0 Wa0 O1 N1 Wa1 Z0 O2 H3 E0 Wa2 Z1 O3 N2 Wa3 Z2 E1 O4 x1 Z3 O5 A1 MZS x0 A2 W0 E2 W1 E4 E3 W2 LA al3 W3 "
         "rt0 x3 L1 E5 rt1 L3 L0 L2 rt2 G1 E6 x2 G4 rt3 G3 G5 G7",
    "s": "-k0 -MM' -k1 -k3 -SQ' -k7 -k9 -k2 -FL' -k5 -k6 -k4 -T3 -T2 R0 R2 LF0 Sb0 R3 Sb1 Sa1 LF1 X1 Sa2 LF2 Sb2 R4 X2 C1 Sa3 Sb3 LF3 X3 X4 "
         "C2 D128 -k8 Y128 D192 -kid' Y192 Y WC MM SQ FL AD ZZa ZZ N3 AL al0 al2 kid al1 GV G0 G2 GW G6",
    "t": "-mark' -mark2' -mod' -k3 -k2 -k1 -CUS' a0 b0 b1 z0 a1 a2 b2 z1 z2 n0 b3 a3 m0 n1 z3 m1 nmAa nmBa D192 D128 n2 m2 MLSa n3 m3 "
         "-kid' H1 nmA nm Q0 Q1 Q2 Q3 WC MLS H3 AD MZSa mark mark2 mod nmB MZS CUS E16 kid",
    "g": "-k0 -kd",
    "y": "-k0",
}
MAXC = max(b - a for a, b in zip(MCH, MCH[1:]))


def spans(b):
    return list(zip(b, b[1:]))


BFT, F32, I32, U16 = "bfloat16", "float32", "int32", "uint16"
SCRATCH, PLACE, SEMAPHORES = {}, {}, ["qv", "qs", "qt", "qg"]
for _n, _w, _d in (
        ("X", NCELL, BFT), ("RT", NCELL, BFT), ("V", VW, BFT), ("RS0", WW, BFT), ("RS1", WW, BFT), ("XG", NCELL, BFT),
        ("DS", WW, BFT), ("MX", NCELL, BFT), ("DM", NK * MAXC, BFT), ("LOC", VW, BFT), ("AL", NCELL, BFT),
        ("Y0", NL, BFT), ("TH", 4, BFT), ("EHI", NL, I32), ("UT", NL, I32), ("WL", NL, U16),
        ("SR", NL, BFT), ("LG", NS, F32), ("GE", NS, F32), ("GV", NS, BFT), ("GW", NL, F32)):
    SCRATCH[_n] = ("sbuf", [128, _w], _d)
    PLACE[_n] = (_n, 0, _w, _d)
_at = {BFT: 0, F32: 0, I32: 0, U16: 0}
for _d, _w, _ns in (
        (BFT, NL, "ZZ WC S1 S2 MM DJ NM LI COLI RI TS PMA PMB BB"), (BFT, 144, "ONE"), (BFT, 576, "KK"),
        (BFT, 128, "DMT ID5 B WMK WM16 WEB W1B WDG WBG ID IDK IDM IDN GRP H16 M8B N8B WA WB WZ C1 C2 C3 C4 C5 C6 C7"),
        (BFT, 32, "ML"),
        (F32, NL, "SQ X1 MLS MZS LV CUS TAS LF LM SZA SZH PHB REA NEG"),
        (F32, 288, "RR VAL JS"), (F32, 96, "EL"), (F32, 64, "CC CX O2A SPA EA EB"),
        (F32, 32, "BSF BSE ILF TRF JL2 CUM O1 M1 M2 F1 F2 CT CD NTH AD ML6 LV0"),
        (I32, NL, "A1 A2"), (I32, 96, "ELI KI"), (I32, 32, "PI I1 I2 I3 I4"),
        (U16, NL, "LA LB E16"), (U16, 96, "ELU KLU"), (U16, 32, "JLU JL2U VO ZL XL E0L TAU SIG")):
    for _n in _ns.split():
        PLACE[_n] = ("all_" + _d, _at[_d], {32: 16, 96: 80}.get(_w, _w), _d)
        _at[_d] += _w
for _d in _at:
    SCRATCH["all_" + _d] = ("sbuf", [128, _at[_d]], _d)
SCRATCH["EQ"] = ("sbuf", [128, 16, 256], BFT)
PLACE["EQ"] = ("EQ", 0, 4096, BFT)
SCRATCH["CM"] = ("sbuf", [128, NL, NK + 1], BFT)
PLACE["CM"] = ("CM", 0, NL * (NK + 1), BFT)
SCRATCH["U"] = ("sbuf", [128, 2, 8, 16], I32)
PLACE["U"] = ("U", 0, NL, I32)
for _t in range(NR):
    SCRATCH["LAND%d" % _t] = ("sbuf", [128, 4 * NL], BFT)
    PLACE["LAND%d" % _t] = ("LAND%d" % _t, 0, 4 * NL, BFT)
    for _p in range(len(SENDS[_t]) - 1):
        SEMAPHORES += ["ar%d_%d" % (_t, _p), "lo%d_%d" % (_t, _p)]
for _b in range(8):
    SCRATCH["P%d" % _b] = ("psum", [128, 512], F32)
    PLACE["P%d" % _b] = ("P%d" % _b, 0, 512, F32)
SEMAPHORES += ["dth", "dv", "de", "dw", "dx", "oyv", "oyw", "oye"] + ["oyx%d" % _c for _c in range(len(ECH) - 1)]

ADD, SUB, MUL, MAX, MIN = AluOpType.add, AluOpType.subtract, AluOpType.mult, AluOpType.max, AluOpType.min
GE, GT, LE, LT, EQL, NE = AluOpType.is_ge, AluOpType.is_gt, AluOpType.is_le, AluOpType.is_lt, AluOpType.is_equal, AluOpType.not_equal
SHR, AND = AluOpType.logical_shift_right, AluOpType.bitwise_and
COPY, IDENT = ActivationFunctionType.Copy, ActivationFunctionType.Identity
ABS, SQUARE, SIGN = ActivationFunctionType.Abs, ActivationFunctionType.Square, ActivationFunctionType.Sign


def rank_program(g, core, T, topo):
    rank = T.rank_of(core)
    if rank is None:
        return
    N = len(T.cores)
    Q = {"v": g.vector, "s": g.scalar, "t": g.tensor, "g": g, "y": g.sync}
    nodes, hist, bank, eng, names = [], {}, {}, [], {}

    def view(n, lo=0, hi=None, step=1, ind=None, ap=None, el=None):
        phys, off, w, d = PLACE[n]
        if hi is None:
            hi = w
        if ap is None:
            ap = T[phys][:, off + lo:off + hi:step] if step > 1 else T[phys][:, off + lo:off + hi]
            if ind is not None:
                p2, o2 = PLACE[ind[0]][:2]
                ap = ap.indirect(T[p2][:, o2 + ind[1]:o2 + ind[2]])
        n_el = el or (16 * (ind[2] - ind[1]) if ind is not None else -((lo - hi) // step))
        return {"n": n, "lo": lo, "hi": hi, "ap": ap, "ind": ind, "el": n_el, "b2": d in (BFT, U16), "ps": n[0] == "P" and n[1:].isdigit()}

    def node(q, calls, rd, wr, cost, sem=None, lat=0.0, wait=()):
        i = len(nodes)
        real, banks = set(), {}
        for v, w in [(v, False) for v in rd] + [(v, True) for v in wr]:
            touched = [(v["n"], v["lo"], v["hi"], w)]
            if v["ind"] is not None:
                touched.append((v["ind"][0], v["ind"][1], v["ind"][2], False))
            for (n, lo, hi, ww) in touched:
                if n[0] == "P" and n[1:].isdigit():
                    if n not in banks:
                        banks[n] = bank.get(n)
                        bank[n] = i
                    continue
                h = hist.setdefault(n, [])
                real.update(e[3] for e in h if (ww or e[2]) and e[0] < hi and lo < e[1] and e[3] != i)
                if ww and v["el"] == hi - lo and v["ind"] is None:
                    h = [e for e in h if not (lo <= e[0] and e[1] <= hi)]
                h.append((lo, hi, ww, i))
                hist[n] = h
        nodes.append({"alt": {q: (calls, cost)}, "real": real, "banks": banks, "order": set(b for b in banks.values() if b is not None),
                      "sem": sem, "lat": lat, "wait": wait})
        return i

    def either(on_v, on_s):
        keep = (dict(bank), {n: list(h) for n, h in hist.items()})
        on_s()
        other = nodes.pop()
        bank.clear()
        bank.update(keep[0])
        hist.clear()
        hist.update(keep[1])
        on_v()
        nodes[-1]["alt"].update(other["alt"])
        nodes[-1]["real"] |= other["real"]
        nodes[-1]["wait"] = other["wait"]
        return len(nodes) - 1

    def flush():
        n = len(nodes)
        for q in ORDER:
            row = [i for t in range(NR + 1) for w in ORDER[q].split() for i in names.get((w.strip("-"), t - (w[0] == "-")), [])
                   if q in nodes[i]["alt"]]
            for i in row:
                nodes[i]["alt"] = {q: nodes[i]["alt"][q]}
            for a, b in zip(row, row[1:]):
                nodes[b]["order"].add(a)
        eng.extend(min(x["alt"]) for x in nodes)
        preds = [[(p, False) for p in x["real"]] + [(p, True) for p in x["order"] - x["real"]] for x in nodes]
        succs = [[] for _ in range(n)]
        for i in range(n):
            for p, soft in preds[i]:
                succs[p].append(i)
        left = [len(p) for p in preds]
        seq = [i for i in range(n) if not left[i]]
        start, end = [0.0] * n, [0.0] * n
        for i in seq:
            for p, soft in preds[i]:
                lat, same = nodes[p]["lat"], eng[p] == eng[i]
                start[i] = max(start[i], end[p] + (0.0 if soft and same else lat + (SAME if same and not lat else WAKE)))
            end[i] = start[i] + nodes[i]["alt"][eng[i]][1]
            for j in succs[i]:
                left[j] -= 1
                if not left[j]:
                    seq.append(j)
        assert len(seq) == n, [w for w in names if left[names[w][0]]][:8]
        seq.sort(key=lambda i: (start[i], i))
        for i, x in enumerate(nodes):
            for b, p in x["banks"].items():
                while p is not None and eng[p] == eng[i]:
                    p = nodes[p]["banks"][b]
                if p is not None:
                    x["real"].add(p)
        total, clocks, known, at = {}, {}, {q: {} for q in Q}, {}

        def learn(q, key, cnt):
            k = known[q]
            if k.get(key, 0) < cnt:
                Q[q].wait_ge(T.sem[key], cnt)
                k[key] = cnt
                for kk, nn in clocks[(key, cnt)].items():
                    if k.get(kk, 0) < nn:
                        k[kk] = nn
        for i in seq:
            x, q = nodes[i], eng[i]
            calls = x["alt"][q][0]
            need = {}
            for p in x["real"]:
                if at[p] is not None:
                    need[at[p][0]] = max(need.get(at[p][0], 0), at[p][1])
            for key in sorted(need, key=lambda key: -need[key]):
                learn(q, key, need[key])
            for s, c in x["wait"]:
                if known[q].get(s, 0) < c:
                    Q[q].wait_ge(T.sem[s], c)
                    known[q][s] = c
            key = x["sem"] or "q" + q
            if key == "none":
                calls[0]()
                at[i] = None
                continue
            for k, call in enumerate(calls):
                ins = call()
                if key[0] != "q":
                    ins.then_inc(T.sem[key], 16)
                    total[key] = total.get(key, 0) + 16
                elif k == len(calls) - 1:
                    ins.then_inc(T.sem[key], 1)
                    total[key] = total.get(key, 0) + 1
            at[i] = (key, total[key])
            c = dict(known[q])
            c[key] = total[key]
            clocks[at[i]] = c
        for key in sorted(total):
            learn("g", key, total[key])

    def sc(x):
        return x["ap"] if isinstance(x, dict) else x

    def scr(*xs):
        return [x for x in xs if isinstance(x, dict)]

    def cy(n):
        return 0.015 + CYC * max(64, n)

    def half(*vs):
        return cy(vs[0]["el"] * (0.5 if all(v["b2"] for v in vs) else 1))

    def ts(out, i0, s1, op0, s2=None, op1=None):
        if op1 is None:
            c = 0.05 + CYC * GAT * out["el"] if i0["ind"] else half(out, i0)
            node("v", [lambda: g.vector.tensor_scalar(out["ap"], i0["ap"], sc(s1), None, op0)], [i0] + scr(s1), [out], c)
        else:
            node("v", [lambda: g.vector.tensor_scalar(out["ap"], i0["ap"], sc(s1), sc(s2), op0, op1)], [i0] + scr(s1, s2), [out], half(out, i0))

    def tt(out, a, b, op):
        c = 0.05 + CYC * GAT * out["el"] if a["ind"] else cy(out["el"] * (1 if a["ps"] or b["ps"] else 2))
        node("v", [lambda: g.vector.tensor_tensor(out["ap"], a["ap"], b["ap"], op)], [a, b], [out], c)

    def tc(out, a):
        c = 0.05 + CYC * GAT * out["el"] if a["ind"] else 0.05 + CYC * SCA * out["el"] if out["ind"] else half(out, a)
        node("v", [lambda: g.vector.tensor_copy(out["ap"], a["ap"])], [a], [out], c)

    def ms(out, c):
        node("v", [lambda: g.vector.memset(out["ap"], c)], [], [out], half(out))

    def scan(out, a, b, init, op0, op1):
        node("v", [lambda: g.vector.tensor_tensor_scan(out["ap"], a["ap"], b["ap"], sc(init), op0, op1)], [a, b] + scr(init), [out], half(out, a, b))

    def act(out, a, func=COPY, bias=None, scale=None, wait=(), acc=None):
        kw = {}
        if bias is not None:
            kw["bias"] = sc(bias)
        if scale is not None:
            kw["scale"] = sc(scale)
        if acc is not None:
            kw["accum_out"] = acc["ap"]
        c = 0.065 + CYC * GAT * out["el"] if a["ind"] else cy(a["el"])
        node("s", [lambda: g.scalar.activation(out["ap"], a["ap"], func, **kw)], [a] + scr(bias, scale), [out] + scr(acc), c, wait=wait)

    def mms(out, pairs, start=True, stop=True):
        n = len(pairs)

        def one(k, l, r):
            return lambda: g.tensor.matmul(out["ap"], l["pick"]() if "pick" in l else l["ap"], r["ap"], start and k == 0, stop and k == n - 1)
        node("t", [one(k, l, r) for k, (l, r) in enumerate(pairs)], [x for p in pairs for x in p], [out], n * (0.005 + PEC * max(64, out["el"])))

    def mm(out, l, r, start=True, stop=True):
        mms(out, [(l, r)], start, stop)

    def gio(out, pat, base, cm=0):
        kw = {} if PLACE[out["n"]][3] == I32 else {"allow_small_or_imprecise_dtypes": True}
        node("g", [lambda: g.iota(out["ap"], pat, base, cm, **kw)], [], [out], 0.13 + 2 * CYC * out["el"])

    def dma(q, pairs, sem, rd, wr, us=2.0):
        node(q, [(lambda o=o, i=i: Q[q].dma_start(o, i)) for o, i in pairs], rd, wr, 0.06 * len(pairs), sem, us)

    def copy(out, a, wait=()):
        either(lambda: tc(out, a), lambda: act(out, a, wait=wait))

    def affine(out, a, scale, bias):
        either(lambda: ts(out, a, scale, MUL, bias, ADD), lambda: act(out, a, IDENT, bias=bias, scale=scale))

    def sign(out, a, at, below, w):
        i = either(lambda: ts(out, a, at, GE, 0.5, SUB), lambda: act(out, a, SIGN, bias=below))
        v = view(w)
        v["pick"] = lambda: view(w, 0, 128)["ap"] if eng[i] == "s" else view(w, 128, 256)["ap"]
        return v

    def name(w, t, k=1):
        names.setdefault((w, t), []).extend(range(len(nodes) - k, len(nodes)))

    def steps(w, t, *calls):
        for k, c in enumerate(calls):
            c()
            name("%s%d" % (w, k), t)

    def slide(n, top, k):
        a = 144 * ("KB", "KXA", "KXB", "KW").index(n) + top - k
        return view("KK", a, a + 128)

    def picked(c0, c1):
        return view("JS", 17 * c0 + 16, 17 * c1, 17)

    def every16(n, l0=0, l1=NL):
        return view(n, l0 + 15, l1, 16)

    def lanes(pn, w, src, out, t, first, l0=0, l1=NL, s=""):
        n = l1 - l0
        mm(view(pn, 0, n), view("ID"), view("NM", 0, n), True, False)
        name(first + s, t)
        mm(view(pn, 0, n), view(w), src, False, True)
        scan(view(out, l0, l1), view("DJ", 0, n), view(pn, 0, n), 0.0, MUL, MAX)
        name(out + s, t, 2)

    def cands(n, l0, l1, k=None):
        a = 2 * CO + NK * l0
        return view(n, a, a + NK * (l1 - l0)) if k is None else view(n, a + k, a + NK * (l1 - l0), NK)

    def cc(j):
        return view("CC", j, j + 1)

    def cx(j):
        return view("CX", j, j + 1)

    def spot(n, at, w):
        ts(view("KK", 144 * n + at, 144 * n + 128, 16), view("GRP", 0, 128, 16), cc(PG), EQL, w, MUL)

    def stage(w):
        name(w, -1, len(nodes) - staged[0])
        staged[0] = len(nodes)
    staged = [0]
    (PF, PQ, PG, P8, R0, R1, R2, R3, R4, R5, NP16, WM, WE_, WH_, NWE, NWH, WE2, LOW, WWC, Q16, G2, G21, KAP, B16, BK,
     SGN, NR0, LO, BLO, P88) = range(30)
    A = [view("CC", 40 + t, 41 + t) for t in range(NR)]
    gio(view("PI", 0, 1), [[1, 1]], 0, 1)
    gio(view("EHI"), [[1, NL]], 0)
    dma("s", [(T.Y0[:, :], T.v0[:, :])], "dv", [], [view("Y0")], 2.2)
    dma("s", [(T.TH[:, :], T.th[:, :])], "dth", [], [view("TH")], 3.0)
    dma("y", [(T.U[:, ga], T.w0[ga::2, :]) for ga in range(2)], "dw", [], [view("U", ap=0)], DU)
    dma("y", [(T.EHI[0::16, :], T.e0[:, :]), (T.EHI[1::16, :], T.h0[:, :])], "de", [], [view("EHI")], DU - 0.6)
    dma("y", [(T.X[:, :], T.x0[:, :])], "dx", [], [view("X")], DX)
    gio(view("GRP"), [[1, 8], [0, 16]], 0)
    gio(view("COLI"), [[1, NL]], 0)
    gio(view("H16"), [[1, 16], [0, 8]], 0)
    gio(view("RI"), [[0, 16], [1, 16]], 0)
    gio(view("VAL", 0, 272), [[256, 16], [1, 17]], 2 * CO - 1)
    gio(view("V", 0, VG), [[0, VG]], -1)
    gio(view("DM"), [[0, MAXC], [16384, 16]], 0)
    gio(view("DS", SENDS[0][1], 2 * CO), [[0, 2 * CO - SENDS[0][1]]], 0)
    gio(view("CT", 0, 4), [[1, 4]], 1)
    for t in range(NR):
        gio(view("CD", t, t + 1), [[0, 1]], 2 ** (3 - t))
    ms(view("KK"), 0.0)
    ts(view("PI", 1, 2), view("PI", 0, 1), 15, AND)
    ts(view("PI", 2, 3), view("PI", 0, 1), 4, SHR)
    ts(view("PI", 3, 4), view("PI", 0, 1), 7, AND)
    ms(A[0], MAGIC)
    tc(view("CC", PF, P8 + 1), view("PI", 0, 4))
    ms(view("ONE"), 1.0)
    ts(cc(WM), cc(PQ), 2.0, MUL, 1.0, ADD)
    ts(cc(LO), cc(PQ), 8.0, LT)
    ms(view("ONE", 0, 144, 17), 0.0)
    ms(view("V", DEAD, VW), 0.0)
    ms(view("CM", ap=T.CM[:, :, 0], el=NL), 1.0)
    act(cx(0), cc(PQ), SQUARE, bias=15.5, scale=-1.0)
    act(cc(G2), cc(PG), COPY, scale=2.0)
    act(cc(NP16), cc(PG), COPY, scale=-16.0)
    act(cc(G21), cc(PG), IDENT, bias=1.0, scale=2.0)
    act(cc(B16), cx(0), IDENT, bias=12.0 + 129 * 4096, scale=16.0)
    act(cc(KAP), cx(0), SQUARE, bias=0.75)
    act(cc(P88), cc(P8), IDENT, bias=8.0)
    act(cc(Q16), cc(PQ), COPY, scale=16.0)
    ts(view("CC", R0, R5 + 1), view("GRP", 0, 96, 16), cc(PQ), EQL)
    ts(view("WMK"), view("GRP"), cc(PG), EQL, cc(WM), MUL)
    ts(view("B"), view("GRP"), cc(PG), EQL)
    ts(cx(1), cc(PQ), 1.0, LE, cc(R3), ADD)
    ts(cx(2), cc(PQ), 2.0, LE, cc(R5), ADD)
    for k in range(2):
        ts(view("BB", 128 * k, 128 * k + 128), view("GRP"), cc(PG), EQL, k + 1.0, MUL)
    spot(0, 15, 32768.0)
    act(cc(BK), cc(KAP), IDENT, bias=-0.375, scale=-8.0)
    act(cc(WE_), cc(R0), IDENT, bias=cc(R2), scale=16.0)
    act(cc(NWH), cc(R1), IDENT, bias=cc(R2), scale=-16.0)
    act(cc(BLO), cc(LO), IDENT, bias=-16384.0, scale=32768.0 + LAB0)
    act(cc(NWE), cc(WE_), COPY, scale=-1.0)
    act(cc(WH_), cc(NWH), COPY, scale=-1.0)
    act(cc(WE2), cc(R5), IDENT, bias=cc(WE_), scale=float(LAB0))
    act(cc(LOW), cc(R5), IDENT, bias=cc(WE_), scale=-16384.0)
    ts(view("IDM"), view("COLI", 0, 128), cc(PF), EQL, -4096.0, MUL)
    ts(view("ID"), view("COLI", 0, 128), cc(PF), EQL)
    ts(view("DMT"), view("COLI", 0, 128), cc(NP16), ADD)
    act(view("ILF"), view("COLI", 0, 16), IDENT, bias=cc(PQ), scale=16.0)
    act(view("WEB"), view("B"), COPY, scale=cc(WE2))
    ts(view("M8B"), view("H16"), cc(G2), EQL)
    ts(view("N8B"), view("H16"), cc(G21), EQL)
    for n, w7, w15 in ((1, WE_, WH_), (2, WH_, WE_)):
        spot(n, 7, cc(w7))
        spot(n, 15, cc(w15))
    for k in range(2):
        ts(view("PMA", 128 * k, 128 * k + 128), view("DMT"), cc(P8), EQL, 4096.0 * (k + 1), MUL)
        ts(view("PMB", 128 * k, 128 * k + 128), view("DMT"), cc(P88), EQL, 4096.0 * (k + 1), MUL)
    ts(view("NM"), view("RI"), cc(PQ), NE, -2.0 ** 21, MUL)
    ts(view("DJ"), view("RI"), 0.0, GT)
    for a in range(VG, DEAD, 608):
        ms(view("V", a, min(DEAD, a + 608)), -1.0)
    stage("k0")
    for k, (n, lo, hi) in enumerate((("WA", NWE, NWH), ("WB", NWH, NWE), ("WZ", LOW, WE2))):
        c, d, p = view("C%d" % (2 * k + 1)), view("C%d" % (2 * k + 2)), view("P%d" % (2 + k), 0, 128)
        act(c, view("M8B"), COPY, scale=cc(lo))
        act(d, view("N8B"), COPY, scale=cc(hi))
        mms(p, [(view("ID"), c), (view("ID"), d)])
        stage("k%d" % (1 + k))
        act(view(n), p)
        stage("k4")
    act(view("VAL", 0, 272), view("VAL", 0, 272), IDENT, bias=cc(Q16))
    stage("k5")
    act(view("VAL", 0, 272, 17), view("ILF"))
    stage("k6")
    ts(view("SR"), view("EHI"), cx(1), MUL, cc(R5), ADD)
    stage("SR")
    act(view("IDN"), view("ID"), COPY, scale=-1.0)
    act(view("ID5"), view("ID"), COPY, scale=-5.0 * 32768)
    stage("k7")
    act(view("LI"), view("COLI"), COPY, scale=cc(R3))
    act(view("IDK"), view("ID"), COPY, scale=cx(2))
    act(view("W1B"), view("B"), COPY, scale=cc(R1))
    act(view("WBG"), view("B"), COPY, scale=-2.0 ** 18)
    act(view("WM16"), view("WMK"), COPY, scale=16.0)
    act(view("NTH", 0, 4), view("TH"), IDENT, bias=0.5, scale=-1.0)
    act(view("TRF"), view("ILF"), IDENT, bias=float(TRASH))
    act(view("BSF"), view("COLI", 0, 16), IDENT, bias=cc(Q16), scale=256.0)
    for l0, l1 in spans(ECH):
        act(view("BSE", l0 // 16, l1 // 16), view("COLI", 0, (l1 - l0) // 16), IDENT, bias=cc(Q16), scale=256.0)
    act(cc(SGN), cc(R1), IDENT, bias=cc(R0), scale=-1.0)
    act(cc(NR0), cc(R0), COPY, scale=-1.0)
    stage("k8")
    act(cc(WWC), cc(R4), IDENT, bias=cc(R3), scale=256.0)
    stage("k9")
    spot(3, 15, cc(WWC))
    ts(view("CT", 4, 8), view("CT", 0, 4), cc(R4), MUL)
    ts(view("CD", 4, 8), view("CD", 0, 4), cc(R2), MUL)
    stage("kb")
    tt(view("CT", 8, 12), view("CT", 4, 8), view("CD", 4, 8), ADD)
    stage("kc")
    gio(view("RR"), [[0, 288]], -1)
    gio(view("NEG"), [[0, NL]], -5)
    gio(view("LOC", 0, LAB0), [[0, LAB0]], 0)
    gio(view("LOC", DEAD, VW), [[0, 16]], 0)
    stage("kd")

    def lead_weights():
        for o, a, op, fill in (("C7", "WBG", GT, 0.0), ("WDG", "C7", NE, 65536.0)):
            node("g", [lambda o=o, a=a, op=op, fill=fill: g.affine_select(view(o)["ap"], view(a)["ap"], [[1, 128]], op, fill, 0, -1)],
                 [view(a)], [view(o)], 0.17 + 2 * CYC * 128)

    def cells(y, a, t, s=""):
        p = view("P1", 0, NL)
        mm(view("P0", 0, NL), view("WMK"), y)
        name("mark" + s, t)
        mm(p, view("WMK"), y, True, False)
        name("mark2" + s, t)
        affine(view("MM"), view("P0", 0, NL), 1.0 / 4096, 128.5 + 1.0 / 8192)
        name("MM" + s, t)
        mm(p, view("IDM"), view("MM"), False, True)
        name("mod" + s, t)
        act(view("SQ"), p, SQUARE, bias=cc(B16))
        name("SQ" + s, t)
        affine(view("X1"), view("SQ"), 1.0 / 32, cc(BK))
        name("FL" + s, t)
        ts(view("A1"), view("X1"), a, ADD)
        name("A1" + s, t)
        ts(view("A2"), view("A1"), 4095, AND)
        name("A2" + s, t)
        tc(view("LA"), view("A2"))
        name("LA" + s, t)

    def current(rec, t, s=""):
        if t >= 0:
            mm(view("P5", 0, NL), view("WEB"), view(rec, 0, NL))
            tc(view("E16"), view("P5", 0, NL))
            name("E16", t, 2)
        lanes("P4", "WEB", view(rec, 0, NL), "CUS", t, "CUS")
        if s:
            names[("CUS" + s, t)] = names[("CUS", t)][:2]
        mms(view("P7", 0, NL), [(view("IDK"), view(rec, 0, NL)), (view("ID"), view("LI"))])
        affine(view(rec, CO, CO + NL), view("P7", 0, NL), 1.0, view("CT", 9 + t, 10 + t))
        name("kid" + s, t, 2)

    def second_order():
        tc(view("EL", 0, 16), every16("CUS"))
        ts(view("E0L"), every16("CUS"), float(-LAB0), ADD, 0.0625, MUL)
        tc(view("TS", 0, NL, 1, ("E0L", 0, 16)), view("SR"))
        name("H0", 0, 3)
        k = len(nodes)
        lanes("P6", "W1B", view("TS"), "TAS", -9, "")
        tc(view("TAU"), every16("TAS"))
        name("H1", 0, len(nodes) - k)
        tc(view("TS", 0, NL, 1, ("TAU", 0, 16)), view("COLI"))
        name("H2", 0)
        k = len(nodes)
        lanes("P6", "W1B", view("TS"), "TAS", -9, "")
        ts(view("SIG"), every16("TAS"), 16.0, MUL, LAB0 + 15.0, ADD)
        name("H3", 0, len(nodes) - k)

    cells(view("Y0"), A[0], -1, "'")
    node("v", [lambda ip=ip: g.vector.transpose(T.UT[:, ip::8], T.U[:, :, ip, :]) for ip in range(8)], [view("U", ap=0)], [view("UT")], 8 * cy(32))
    name("TR", -1)
    tc(view("WL"), view("UT"))
    name("WL", -1)
    for c, (a, b) in enumerate(spans(TCH)):
        copy(view("RT", NK * a, NK * b), view("SR", 0, NL, 1, ("WL", a, b)))
        name("T%d" % c, -1)
    copy(view("RS0", 0, NL), view("SR"))
    name("own", -1)
    current("RS0", -1, "'")
    tc(view("VO"), every16("CUS"))
    tc(view("V", 0, VW, 1, ("VO", 0, 16)), view("Y0"))
    name("VS", 0, 2)

    msk = topo.mask(core, T.cores[(rank + 1) % N])
    neng = len(topo.engines(core, T.cores[(rank + 1) % N]))
    y = "Y0"
    for t in range(NR):
        rs, rn = "RS%d" % (t % 2), "RS%d" % ((t + 1) % 2)
        land = "LAND%d" % t
        O2 = view("O2A", 16 * t, 16 * t + 16)
        SP = view("SPA", 16 * t, 16 * t + 16)
        more = t + 1 < NR
        takes = (0, NL) if more else SENDS[t]

        def slot(d, l0, l1):
            p0, p1 = [p for p in spans(takes) if p[0] <= l0 < p[1]][0]
            return view(land, N * p0 + d * (p1 - p0) + l0 - p0, N * p0 + d * (p1 - p0) + l1 - p0)

        def choose(l0, l1, pn, s):
            c0, c1 = l0 // 16, l1 // 16
            lanes(pn, "WM16", slot(0, l0, l1), "MLS", t, "nmA", l0, l1, s)
            steps("Z" + s, t, lambda: tc(view("I1", c0, c1), every16("MLS", l0, l1)),
                  lambda: ts(view("I2", c0, c1), view("I1", c0, c1), NL // (l1 - l0) - 1, SHR, 3 * (l1 - l0), AND),
                  lambda: tt(view("F1", c0, c1), view("I2", c0, c1), view("ILF", 0, c1 - c0), ADD), lambda: tc(view("ZL", c0, c1), view("F1", c0, c1)))

        def take(l0, l1, pn, s):
            c0, c1 = l0 // 16, l1 // 16
            copy(view("ZZ", l0, l1), view(land, N * l0, N * l1, 1, ("ZL", c0, c1)),
                 wait=[("ar%d_%d" % (t, ip), (N - 1) * neng) for ip, p in enumerate(spans(SENDS[t])) if l0 <= p[0] < l1])
            name("ZZ" + s, t)
            lanes(pn, "WM16", view("ZZ", l0, l1), "MZS", t, "nmB", l0, l1, s)
            steps("W" + s, t, lambda: tc(view("I3", c0, c1), every16("MZS", l0, l1)), lambda: ts(view("I4", c0, c1), view("I3", c0, c1), 4, SHR, 15, AND),
                  lambda: tt(view("F2", c0, c1), view("I4", c0, c1), view("BSF" if more else "BSE", c0, c1), ADD),
                  lambda: tc(view("XL", c0, c1), view("F2", c0, c1)))
        JL = picked(0, 16)
        mm(view("P7", 0, NL), view("ID"), view("NM"), True, False)
        name("nm", t)

        for c, (l0, l1) in enumerate(spans(RCH)):
            copy(cands(rs, l0, l1), view("RT", 0, NCELL, 1, ("LA", l0, l1)))
            name("R%d" % c, t)
        for c, (l0, l1) in enumerate(spans(XCH)):
            copy(view("XG", NK * l0, NK * l1), view("X", 0, NCELL, 1, ("LA", l0, l1)))
            name("X%d" % c, t)
        for c, (l0, l1) in enumerate(spans(LCH)):
            n = l1 - l0
            pa, pb, pz = view("P%d" % (c % 2), 0, n), view("P%d" % (2 + c % 2), 0, n), view("P6", 0, n)
            cur = view(rs, l0, l1)
            mms(pa, [(view("WA"), cur)] + [(slide("KXA", 7, k), cands(rs, l0, l1, k)) for k in range(8)])
            name("a%d" % c, t)
            mms(pb, [(view("WB"), cur)] + [(slide("KXB", 7, k), cands(rs, l0, l1, 8 + k)) for k in range(8)])
            name("b%d" % c, t)
            wa = sign(view("S1", l0, l1), pa, 0.0, 0.5, "PMA")
            name("Sa%d" % c, t)
            affine(view("LF", l0, l1), pa, cc(LO), cc(BLO))
            name("LF%d" % c, t)
            wb = sign(view("S2", l0, l1), pb, 0.0, 0.5, "PMB")
            name("Sb%d" % c, t)
            tt(view("LM", l0, l1), view("LF", l0, l1), pb, MAX)
            name("LM%d" % c, t)
            mms(pz, [(view("WZ"), cur), (wa, view("S1", l0, l1)), (wb, view("S2", l0, l1))])
            name("z%d" % c, t)
            tt(view("LF", l0, l1), view("LM", l0, l1), pz, ADD)
            name("LP%d" % c, t)
            ts(view("LB", l0, l1), view("LF", l0, l1), float(DEAD), MIN, 0.0, MAX)
            name("LB%d" % c, t)
        for c, (l0, l1) in enumerate(spans(MCH)):
            scan(view("MX", NK * l0, NK * l1), view("DM", 0, NK * (l1 - l0)), view("XG", NK * l0, NK * l1), 0.0, MIN, MAX)
            name("M%d" % c, t)
        for c, (l0, l1) in enumerate(spans(VCH)):
            tt(cands("DS", l0, l1), view("V", 0, VW, 1, ("LB", l0, l1)), view("XG", NK * l0, NK * l1), SUB)
            name("V%d" % c, t)
            cm = view("CM", 17 * l0, 17 * l1, ap=T.CM[:, l0:l1, 1:17], el=NK * (l1 - l0))
            if [k for k in CA if CCH[k] <= l0 < CCH[k + 1]]:
                act(cm, cands("DS", l0, l1), SIGN, bias=-0.5)
            else:
                ts(cm, cands("DS", l0, l1), 0.0, GT, 10.5 / 16, SUB)
            name("C%d" % c, t)
        for c, (l0, l1) in enumerate(spans(CCH)):
            c0, c1 = l0 // 16, l1 // 16
            pc = view("P%d" % (4 + c % 2), 0, 17 * (c1 - c0))
            rows = [(slide("KB", 15, q), view("CM", 17 * l0, 17 * l1, ap=T.CM[:, l0 + q:l1:16, :])) for q in range(16)]
            mms(pc, [(view("ID5"), view("ONE", 0, 17 * (c1 - c0)))] * (c in CA) + rows[:8], True, False)
            name("n%d" % c, t)
            mms(pc, rows[8:], False, True)
            name("m%d" % c, t)
            scan(view("JS", 17 * c0, 17 * c1), pc, view("VAL", 17 * c0, 17 * c1), 0.0, MAX, MIN)
            name("J%d" % c, t)
            for m0, m1 in spans(sorted(set(SENDS[t] + MCH[-2:]))):
                most = view("MX", NK * m0 + 15, NK * m1, 16)
                if m1 == NL:
                    if l0 < m0 <= l1:
                        tt(view("DS", m0, m1), most, view(y, m0, m1), SUB)
                        name("D", t)
                elif l0 < m1 <= l1:
                    pm = view("P6" if m1 == MCH[-2] else "P%d" % (4 + c % 2), 256, 256 + m1 - m0)
                    mms(pm, [(view("IDN"), view(y, m0, m1)), (view("ID"), most)])
                    copy(view("DS", m0, m1), pm)
                    name("D%d" % m1, t, 2)

            if l1 in LEADS:
                k = LEADS.index(l1) - 1
                p0 = LEADS[k]
                c0 = p0 // 16
                ts(view("ML", c0, c1), picked(c0, c1), float(2 * CO), LT)
                name("ML%d" % k, t)
                if t > 0:
                    tt(view("CUM", c0, c1), every16("CUS", p0, l1), view("ML", c0, c1), MUL)
                    name("CU%d" % k, t)
                    for b in range(c0, c1):
                        w = NL - 16 * b
                        ts(view("EQ", 256 * b, 256 * b + w, ap=T.EQ[:, b, 0:w]), view("E16", 16 * b, NL), view("CUM", b, b + 1), EQL)
                        name("Q%d" % (b // 4), t)
                        if b < 15:
                            mm(view("P7", 16 * b + 16, NL), view("WBG"), view("EQ", 256 * b, 256 * b + w, ap=T.EQ[:, b, 16:w]), False, False)
                            name("Q%d" % (b // 4), t)
                    mm(view("P7", p0, l1), view("WDG"), view("EQ", 256 * c0, 256 * c1, ap=T.EQ[:, c0:c1, 0:16]), False, False)
                    name("Q%d" % (b // 4), t)

            ych = sorted(set(SENDS[t] + YCH))
            if l1 in ych:
                p0 = ych[ych.index(l1) - 1]
                tc(view("JLU", p0 // 16, c1), picked(p0 // 16, c1))
                act(slot(0, p0, l1), view("DS", 0, 2 * CO + NK * l1, 1, ("JLU", p0 // 16, c1)), ABS)
                name("Y" if l1 == NL else "Y%d" % l1, t, 2)
            if l1 not in SENDS[t]:
                continue
            ip = SENDS[t].index(l1) - 1
            p0 = SENDS[t][ip]
            dsts, ids = [], []
            for j in range(1, N):
                r = (rank + j) % N
                d = (rank - r) % N
                a = topo.addr(T.cores[r])
                ids.append(DstId(rid=a[0], pnc=a[1]))
                dsts.append(slot(d, p0, l1)["ap"])

            def send(ids=ids, dsts=dsts, key="%d_%d" % (t, ip), src=slot(0, p0, l1)["ap"]):
                return g.remote_dma_fused([RemoteDMATransfer(dst_ids=ids, dma_engine_mask=msk, remote_sem=T.sem["ar" + key],
                                                             src=src, dsts=dsts)], local_sem=T.sem["lo" + key])
            node("g", [send], [slot(0, p0, l1)], [slot(d, p0, l1) for d in range(1, N)], 0.1, "none", LAT + (3.6 if t + ip == 0 else 0.0))
            if l1 in takes[1:-1]:
                choose(p0, l1, "P0", "a")
                take(p0, l1, "P2", "a")

        for l0, l1 in spans(takes):
            wc = sign(view("WC", l0, l1), slot(0, l0, l1), view("TH", t, t + 1), view("NTH", t, t + 1), "BB")
            mm(view("P7", l0, l1), wc, view("WC", l0, l1), False, l1 == NL)
            name("WC", t, 2)
        scan(view("LV"), view("DJ"), view("P7", 0, NL), 0.0, MUL, MAX)
        name("LV", t)
        lv = every16("LV")
        if t == 0:
            lead_weights()
            second_order()
            ts(view("ML6"), JL, float(2 * CO), LT, 65536.0, MUL)
            name("ML1", t)
            tt(view("LV0"), view("ML6"), lv, ADD)
            name("LV", t)
            lv = view("LV0")
        choose(takes[-2], NL, "P4", "")
        if more:
            mm(view("P5", 0, 16), view("B"), view("ML"))
            act(view("AD"), view("P5", 0, 16), IDENT, bias=16.0 + MAGIC / 16, scale=-1.0, acc=A[t + 1])
            name("AD", t, 2)
            cells(slot(0, 0, NL), A[t + 1], t)
        steps("N", t, lambda: ts(SP, lv, 65538.0, GE, float(CO), MUL), lambda: tt(view("JL2"), JL, SP, ADD), lambda: tc(view("JL2U"), view("JL2")),
              lambda: copy(view(rn, 0, NL), view(rs, 0, WW, 1, ("JL2U", 0, 16))))

        take(takes[-2], NL, "P5", "")
        if more:
            tc(view("RT", 0, NCELL, 1, ("XL", 0, 16)), view(rn, 0, NL))
            name("RT", t)
            tc(view("X", 0, NCELL, 1, ("XL", 0, 16)), view("ZZ"))
            name("X", t)
        steps("O", t, lambda: ts(view("O1"), lv, 65538.0, GE, float(2 ** (3 - t)), MUL), lambda: tt(O2, view("O1"), every16("CUS"), ADD),
              lambda: tt(view("M1"), lv, O2, MIN), lambda: tt(view("M2"), view("M1"), view("TRF"), MAX), lambda: tc(view("VO"), view("M2")))
        for l0, l1 in spans(takes):
            tc(view("V", 0, VW, 1, ("VO", l0 // 16, l1 // 16)), slot(0, l0, l1))
            name("O5", t)
        if more:
            current(rn, t)
        if t == NR - 2:
            act(view("AL", 0, NCELL, 2), view("V", LAB0, DEAD, 2), SIGN, bias=1.0)
            name("AL", t)
        y = land

    for c, (l0, l1) in enumerate(spans(ECH)):
        tc(view("RT", NK * l0, NK * l1, 1, ("XL", l0 // 16, l1 // 16)), view(rn, l0, l1))
        name("rt%d" % c, t)
        mms(view("P0", 0, NL), [(slide("KW", 15, q), view("RT", 256 * q, 256 * q + 256)) for q in range(l0 // 16, l1 // 16)], l0 == 0, l1 == NL)
        tc(view("X", NK * l0, NK * l1, 1, ("XL", l0 // 16, l1 // 16)), view("ZZ", l0, l1))
        name("x%d" % c, t)
        dma("y", [(T.yx[:, NK * l0:NK * l1], T.X[:, NK * l0:NK * l1])], "oyx%d" % c, [view("X", NK * l0, NK * l1)], [], 3.0)
    act(view("GW"), view("P0", 0, NL))
    name("GW", t)
    dma("y", [(T.yw[:, :], T.GW[:, :])], "oyw", [view("GW")], [], 2.6)
    steps("E", t, lambda: ts(view("EA"), view("O2A"), float(-DEAD), ADD, 1.0 / CO, MUL), lambda: tt(view("EB"), view("EA"), view("SPA"), MUL),
          lambda: ts(view("EL", 16, 80), view("EB"), float(DEAD), ADD), lambda: tc(view("ELU"), view("EL")),
          lambda: tc(view("ELI"), view("EL")), lambda: ts(view("KI"), view("ELI"), 4, SHR), lambda: tc(view("KLU"), view("KI")))
    act(view("GV"), view("V", 0, VW, 1, ("ELU", 0, 80)))
    name("GV", t)
    dma("y", [(T.yv[:, :], T.GV[:, :])], "oyv", [view("GV")], [], 2.8)
    for c, a in enumerate(range(0, NCELL, LW)):
        b = a + LW
        either(lambda: ts(view("AL", a + 1, b, 2), view("V", LAB0 + a + 1, LAB0 + b, 2), 0.0, GE),
               lambda: act(view("AL", a + 1, b, 2), view("V", LAB0 + a + 1, LAB0 + b, 2), SIGN, bias=1.0))
        name("al%d" % c, t)
        scan(view("LOC", LAB0 + a, LAB0 + b), view("DM", 0, b - a), view("AL", a, b), 0.0, MIN, ADD)
        name("L%d" % c, t)
    k0 = LAB0 // 16
    by_h = view("LOC", 0, VW, 1, ("SIG", 0, 16))
    steps("G", t, lambda: either(lambda: ts(view("SZH"), by_h, cc(R1), MUL), lambda: act(view("SZH"), by_h, COPY, scale=cc(R1))),
          lambda: affine(view("SZA"), view("LOC", LAB0 - 1, DEAD - 16, 16), cc(R0), 0.0),
          lambda: act(view("LG", NL, NS), view("LOC", 0, VW, 1, ("ELU", 16, 80)), COPY, scale=cc(SGN)),
          lambda: scan(view("REA"), view("SZA"), view("NEG"), cc(NR0), ADD, MAX),
          lambda: scan(view("PHB"), view("SZH"), view("SZH"), 0.0, ADD, MAX),
          lambda: tt(view("RR", k0, k0 + NL), view("PHB", 0, NL, 1, ("TAU", 0, 16)), view("REA"), ADD),
          lambda: act(view("GE", 0, NL), view("RR", 0, 288, 1, ("KLU", 0, 16)), IDENT, bias=cc(SGN)),
          lambda: tt(view("GE", NL, NS), view("RR", 0, 288, 1, ("KLU", 16, 80)), view("LG", NL, NS), ADD))
    dma("y", [(T.ye[:, :], T.GE[0::16, :]), (T.yh[:, :], T.GE[1::16, :])], "oye", [view("GE")], [], 2.2)

    flush()
    for t in range(NR):
        for ip in range(len(SENDS[t]) - 1):
            g.wait_ge(T.sem["lo%d_%d" % (t, ip)], neng)
